import numpy as np
import ml_dtypes


def mxq(x, axis, fmt="e4m3"):
    dtype, down = {"e4m3": (ml_dtypes.float8_e4m3fn, 7), "e5m2": (ml_dtypes.float8_e5m2, 14)}[fmt]
    v = np.moveaxis(np.asarray(x, np.float32).astype(ml_dtypes.bfloat16).astype(np.float64), axis, -1)
    blocks = v.reshape(v.shape[:-1] + (-1, 32))
    amax = np.abs(blocks).max(-1, keepdims=True)
    byte = np.maximum(np.where(amax > 0, np.frexp(amax)[1] - 1 + 127, 0) - down, 1)
    scale = np.exp2(byte - 127.0)
    codes = (blocks / scale).astype(np.float32).astype(dtype).astype(np.float64)
    return np.moveaxis((codes * scale).reshape(v.shape), -1, axis)


WIDE = False


def mx_kscale(k):
    if not WIDE:
        return np.ones(k)
    levels = np.array([10, -10, 5, -5, 0])
    if k % 512:
        return np.exp2(np.random.permutation(np.resize(levels, k // 32))).repeat(32)
    a = np.empty((k // 512, 16))
    for p in range(k // 512):
        a[p, :8] = np.random.permutation(np.resize(levels, 8))
        for g in range(8):
            far = levels[np.abs(levels - a[p, g]) >= 10]
            a[p, g + 8] = far[np.random.randint(len(far))]
    return np.exp2(a.ravel()).repeat(32)


def f64(x):
    return np.asarray(x).astype(np.float64)


def striped(idx):
    return np.tile(idx.reshape(-1, 16).T, (8, 1)).astype(np.uint16)


def unstriped(offs):
    return offs[:16].T.reshape(-1).astype(np.int64)


def gelu(v):
    return 0.5 * v * (1.0 + np.tanh(np.sqrt(2.0 / np.pi) * (v + 0.044715 * v**3)))


K, T, E, C, H, N = 2048, 512, 2, 256, 512, 512


def by_expert(wq, xq):
    return np.concatenate([wq[e].T @ xq[:, e * C:(e + 1) * C] for e in range(E)], axis=1)


def setup_inputs():
    n = np.random.standard_normal
    s = mx_kscale(K)[:, None]
    u = mx_kscale(H)
    return {
        "xT": (n((K, T)) * s).astype(np.float32),
        "w1": (n((E, K, H)) / np.sqrt(K) / s[None]).astype(np.float32),
        "w3": (n((E, K, H)) / np.sqrt(K) / s[None] * u[None, None, :]).astype(np.float32),
        "w2": (n((E, H, N)) / np.sqrt(H) / u[None, :, None]).astype(np.float32),
        "gate": np.tile(np.random.uniform(0.2, 1.0, E * C), (N, 1)).astype(np.float32),
        "offs": striped(np.random.permutation(T)[:E * C]),
    }


def reference(xT, w1, w3, w2, gate, offs):
    idx = unstriped(offs)
    xq = mxq(f64(xT)[:, idx], 0, "e4m3")
    h = gelu(by_expert(mxq(f64(w1), 1, "e4m3"), xq))
    h = h * by_expert(mxq(f64(w3), 1, "e4m3"), xq)
    y = by_expert(mxq(f64(w2), 1, "e4m3"), mxq(h, 0, "e4m3"))
    out = np.zeros((N, T))
    out[:, idx] = f64(gate) * y
    return out

@@ -1,0 +1,248 @@
+from contextlib import ExitStack
+
+import concourse.mybir as mybir
+
+K, T, E, C, H, N = 2048, 512, 2, 256, 512, 512
+FLOPS = 2 * E * C * (2 * K * H + H * N)
+
+F32 = mybir.dt.float32
+BF16 = mybir.dt.bfloat16
+U32 = mybir.dt.uint32
+U16 = mybir.dt.uint16
+U8 = mybir.dt.uint8
+FP8X4 = mybir.dt.float8_e4m3fn_x4
+MULT = mybir.AluOpType.mult
+GELU = mybir.ActivationFunctionType.Gelu_apprx_tanh
+
+P = 128
+PACK = 4
+K_PASS = P * PACK
+PASSES = K // K_PASS
+WIDTH = 512
+BLOCKS = WIDTH // P
+BANK = 512
+LIST_COLS = C // 16
+HALF = WIDTH // 2
+
+GROUP = 16
+VECTOR_GROUPS = {
+    ("x", 0): (12, 12, 12, 12),
+    ("w1", 0): (16, 16, 16, 16),
+    ("w3", 0): (16, 16, 16, 16),
+    ("w2", 0): (0,),
+    ("w1", 1): (16, 0, 16, 0),
+    ("w3", 1): (0, 16, 16, 20),
+    ("w2", 1): (0,),
+}
+
+
+def tile_routed_moe_kernel(tc, xT, w1, w3, w2, gate, offs, out):
+    nc = tc.nc
+    up_weights = {"w1": w1, "w3": w3}
+
+    stream = [("x", 0, s) for s in range(PASSES)]
+    for e in range(E):
+        stream += [("w1", e, s) for s in range(PASSES)]
+        stream += [("w3", e, s) for s in range(PASSES)]
+        stream += [("w2", e, 0)]
+    last = PASSES - 1
+
+    with ExitStack() as ctx:
+        keep = ctx.enter_context(tc.tile_pool(name="keep", bufs=1))
+        raw_pool = ctx.enter_context(tc.tile_pool(name="raw", bufs=10))
+        rounded_pool = ctx.enter_context(tc.tile_pool(name="rounded", bufs=8))
+        hidden_pool = ctx.enter_context(tc.tile_pool(name="hidden", bufs=1))
+        y_pool = ctx.enter_context(tc.tile_pool(name="y", bufs=BLOCKS))
+        psum = ctx.enter_context(tc.psum_pool(name="psum", bufs=1))
+
+        offsets = keep.tile([P, E * LIST_COLS], U16, name="offsets")
+        nc.sync.dma_start(offsets[:], offs)
+
+        warm = keep.tile([P, 1], F32, name="warm")
+        nc.gpsimd.memset(warm[:], 0.0)
+        nc.scalar.activation(warm[:], warm[:], GELU)
+
+        x_scales = keep.tile([P, T], U8, name="x_scales", align_bytes=64)
+        nc.gpsimd.memset(x_scales[:], 0)
+
+        windows = [keep.tile([P, T], F32, name=f"window{n}") for n in range(BLOCKS)]
+
+        raws, rounded, codes = {}, {}, {}
+        gates, slot_words, slot_scales = {}, {}, {}
+        sums, gelus, hidden_codes, y_slots = {}, {}, {}, {}
+
+        def expert_list(e):
+            return offsets[:, e * LIST_COLS : (e + 1) * LIST_COLS]
+
+        def load(entry):
+            kind, e, s = entry
+            raw = raw_pool.tile([P, PACK, WIDTH], F32, name="raw")
+            raws[entry] = raw
+            if kind == "w2":
+                rows = w2[e].rearrange("(q t r) n -> r q t n", t=4, r=4)
+                for r in range(4):
+                    nc.sync.dma_start(raw[r::4], rows[r])
+                gt = keep.tile([P, BLOCKS, C], F32, name=f"gate{e}")
+                nc.sync.dma_start(gt[:], gate[:, e * C : (e + 1) * C].rearrange("(n p) c -> p n c", p=P))
+                gates[e] = gt
+                return
+            source = xT if kind == "x" else up_weights[kind][e]
+            nc.sync.dma_start(raw[:], source[s * K_PASS : (s + 1) * K_PASS, :].rearrange("(p j) c -> p j c", j=PACK))
+
+        def interleave(copy, dst, src, c0, c1):
+            copy(
+                dst[:].rearrange("p (c i j) -> p c j i", i=4, j=PACK)[:, c0 // 4 : c1 // 4],
+                src[:].rearrange("p j (c i) -> p c j i", i=4)[:, c0 // 4 : c1 // 4],
+            )
+
+        def interleave_permuted(copy, dst, src, q0, q1):
+            copy(
+                dst[:].rearrange("p (t q r j) -> p t q j r", t=4, r=4, j=PACK)[:, :, q0:q1],
+                src[:].rearrange("p j (q t r) -> p t q j r", t=4, r=4)[:, :, q0:q1],
+            )
+
+        def round_to_bf16(entry):
+            kind, e, s = entry
+            raw = raws[entry]
+            dst = rounded_pool.tile([P, PACK * WIDTH], BF16, name="dst", align_bytes=64)
+            rounded[entry] = dst
+            on_vector = VECTOR_GROUPS[kind, e][s]
+            if kind in up_weights:
+                if on_vector > 0:
+                    interleave_permuted(nc.vector.tensor_copy, dst, raw, 0, on_vector)
+                interleave_permuted(nc.scalar.copy, dst, raw, on_vector, WIDTH // GROUP)
+            else:
+                cuts = (0, HALF, WIDTH) if entry == stream[-1] else (on_vector * GROUP, WIDTH)
+                if on_vector > 0:
+                    interleave(nc.vector.tensor_copy, dst, raw, 0, on_vector * GROUP)
+                for c0, c1 in zip(cuts[:-1], cuts[1:]):
+                    interleave(nc.scalar.copy, dst, raw, c0, c1)
+
+        def quantize(entry):
+            kind, e, s = entry
+            src = rounded[entry]
+            if kind == "w2":
+                words = hidden_pool.tile([P, WIDTH], U32, name="w2_words", tag="h", align_bytes=64)
+                scales = hidden_pool.tile([P, WIDTH], U8, name="w2_scales", tag="h_rounded", align_bytes=64)
+            else:
+                words = keep.tile([P, WIDTH], U32, name=f"{kind}_words{e}_{s}", align_bytes=64)
+            if kind == "x":
+                scales = x_scales
+                nc.vector.quantize_mx(words[:].bitcast(FP8X4), x_scales[4 * s : P, :], src[:])
+            else:
+                if kind != "w2":
+                    scales = keep.tile([P, WIDTH], U8, name=f"{kind}_scales{e}_{s}", align_bytes=64)
+                cuts = (0, HALF, WIDTH) if entry in stream[-2:] else (0, WIDTH)
+                for c0, c1 in zip(cuts[:-1], cuts[1:]):
+                    nc.vector.quantize_mx(
+                        words[:, c0:c1].bitcast(FP8X4), scales[:, c0:c1], src[:, PACK * c0 : PACK * c1]
+                    )
+            codes[entry] = (words, scales)
+
+        def gather(e):
+            bytes_of_slots = keep.tile([P, C], U8, name=f"slot_scales{e}", align_bytes=64)
+            nc.vector.tensor_copy(bytes_of_slots[:], x_scales[:].indirect(expert_list(e)))
+            slot_scales[e] = bytes_of_slots
+            for s in range(PASSES):
+                words_of_slots = keep.tile([P, C], U32, name=f"slot_words{e}_{s}", align_bytes=64)
+                nc.vector.tensor_copy(words_of_slots[:], codes["x", 0, s][0][:].indirect(expert_list(e)))
+                slot_words[e, s] = words_of_slots
+
+        def multiply_up(entry):
+            kind, e, s = entry
+            if s == 0:
+                sums[kind, e] = [
+                    psum.tile([P, BANK], F32, name=f"{kind}_bank{t}", tag=f"{kind}_bank{t}") for t in range(BLOCKS)
+                ]
+            words, scales = codes[entry]
+            for t in range(BLOCKS):
+                cols = slice(t * P, (t + 1) * P)
+                nc.tensor.matmul_mx(
+                    sums[kind, e][t][:, 0:C],
+                    lhsT=words[:, cols].bitcast(FP8X4),
+                    lhsT_scale=scales[:, cols],
+                    rhs=slot_words[e, s][:].bitcast(FP8X4),
+                    rhs_scale=slot_scales[e][4 * s : P, :],
+                    start=(s == 0),
+                    stop=(s == last),
+                )
+
+        def gelu(e):
+            gelus[e] = raws["w3", e, last][:, :, HALF:WIDTH]
+            for t in range(BLOCKS):
+                nc.scalar.activation(gelus[e][:, t, :], sums["w1", e][t][:, 0:C], GELU)
+
+        def hidden(e):
+            h = hidden_pool.tile([P, PACK, C], F32, name="h", tag="h", align_bytes=64)
+            for t in range(BLOCKS):
+                nc.vector.tensor_tensor(h[:, t, :], sums["w3", e][t][:, 0:C], gelus[e][:, t, :], MULT)
+            h_rounded = hidden_pool.tile([P, PACK * C], BF16, name="h_rounded", tag="h_rounded", align_bytes=64)
+            interleave(nc.vector.tensor_copy, h_rounded, h, 0, C)
+            h_words = hidden_pool.tile([P, C], U32, name="h_words", align_bytes=64)
+            h_scales = hidden_pool.tile([P, C], U8, name="h_scales", align_bytes=64)
+            nc.vector.quantize_mx(h_words[:].bitcast(FP8X4), h_scales[:], h_rounded[:])
+            hidden_codes[e] = (h_words, h_scales)
+
+        def multiply_down(e, n, bank):
+            words, scales = codes["w2", e, 0]
+            h_words, h_scales = hidden_codes[e]
+            cols = slice(n * P, (n + 1) * P)
+            nc.tensor.matmul_mx(
+                bank,
+                lhsT=words[:, cols].bitcast(FP8X4),
+                lhsT_scale=scales[:, cols],
+                rhs=h_words[:].bitcast(FP8X4),
+                rhs_scale=h_scales[:],
+                start=True,
+                stop=True,
+            )
+
+        def down_in_pairs(e, n):
+            tag = f"w3_bank{2 + n // 2}"
+            y = psum.tile([P, BANK], F32, name=tag, tag=tag)
+            for b in range(2):
+                multiply_down(e, n + b, y[:, b * C : (b + 1) * C])
+            y_sbuf = raws["w1", e + 1, 0][:, n : n + 2, HALF:WIDTH]
+            nc.scalar.copy(y_sbuf, y[:].rearrange("p (b c) -> p b c", b=2))
+            for b in range(2):
+                y_slots[e, n + b] = y_sbuf[:, b, :]
+
+        def down(e, n):
+            tag = f"w1_bank{n}"
+            y = psum.tile([P, BANK], F32, name=tag, tag=tag)
+            multiply_down(e, n, y[:, 0:C])
+            y_sbuf = y_pool.tile([P, C], F32, name="y_sbuf")
+            nc.scalar.copy(y_sbuf[:], y[:, 0:C])
+            y_slots[e, n] = y_sbuf[:]
+
+        def scatter(e, n):
+            nc.vector.tensor_tensor(windows[n][:].indirect(expert_list(e)), y_slots[e, n], gates[e][:, n, :], MULT)
+
+        load(stream[0])
+        round_to_bf16(stream[0])
+        for i, entry in enumerate(stream):
+            if i + 1 < len(stream):
+                load(stream[i + 1])
+                round_to_bf16(stream[i + 1])
+            kind, e, s = entry
+            if kind == "w2":
+                hidden(e)
+            quantize(entry)
+            if entry == ("x", 0, last):
+                gather(0)
+            if kind in up_weights:
+                multiply_up(entry)
+            if entry == ("w1", 0, last):
+                gather(1)
+            if kind == "w3" and s == last:
+                gelu(e)
+            if entry == ("w1", 1, 0):
+                for n in range(0, BLOCKS, 2):
+                    down_in_pairs(0, n)
+                    scatter(0, n)
+                    scatter(0, n + 1)
+
+        for n in range(BLOCKS):
+            down(1, n)
+            scatter(1, n)
+            nc.sync.dma_start(out[n * P : (n + 1) * P, :], windows[n][:])

@@ -58,10 +58,6 @@ def tile_routed_moe_kernel(tc, xT, w1, w3, w2, gate, offs, out):
         offsets = keep.tile([P, E * LIST_COLS], U16, name="offsets")
         nc.sync.dma_start(offsets[:], offs)
 
-        warm = keep.tile([P, 1], F32, name="warm")
-        nc.gpsimd.memset(warm[:], 0.0)
-        nc.scalar.activation(warm[:], warm[:], GELU)
-
         x_scales = keep.tile([P, T], U8, name="x_scales", align_bytes=64)
         nc.gpsimd.memset(x_scales[:], 0)
 

@@ -24,63 +24,78 @@ BANK = 512
 LIST_COLS = C // 16
 HALF = WIDTH // 2
 
+SLOTS = E * C
 GROUP = 16
+GROUPS = WIDTH // GROUP
+HALF_C = C // 2
+WINDOW = T + T // 2
+
 VECTOR_GROUPS = {
-    ("x", 0): (12, 12, 12, 12),
-    ("w1", 0): (16, 16, 16, 16),
-    ("w3", 0): (16, 16, 16, 16),
-    ("w2", 0): (0,),
-    ("w1", 1): (16, 0, 16, 0),
-    ("w3", 1): (0, 16, 16, 20),
+    ("x", 0): (0, 0, 0, 0,),
+    ("w1", 0): (0, 32, 0, 32,),
+    ("w3", 0): (0, 32, 16, 20,),
+    ("w2", 0): (12,),
+    ("w1", 1): (0, 0, 0, 32,),
+    ("w3", 1): (0, 32, 16, 20,),
     ("w2", 1): (0,),
 }
+STREAM = [("x", 0, s) for s in range(PASSES)] + [("w1", 0, s) for s in range(PASSES)] + [("w3", 0, s) for s in range(PASSES)] + [("w2", 0, 0)] + [("w1", 1, s) for s in range(PASSES)] + [("w3", 1, s) for s in range(PASSES)] + [("w2", 1, 0)]
+GATE_BEFORE = [("w1", 1, 0), None]
+RAW_BUFS = 12
+ROUNDED_BUFS = 8
+GELU_HOST = [("w3", 0, 0), ("w3", 1, 0)]
+W2V = (0, 0)
+SPLIT0 = (True, True)
+LAST_BY_T = False
+W2_LOADS = (1, 1)
 
 
 def tile_routed_moe_kernel(tc, xT, w1, w3, w2, gate, offs, out):
     nc = tc.nc
     up_weights = {"w1": w1, "w3": w3}
 
-    stream = [("x", 0, s) for s in range(PASSES)]
-    for e in range(E):
-        stream += [("w1", e, s) for s in range(PASSES)]
-        stream += [("w3", e, s) for s in range(PASSES)]
-        stream += [("w2", e, 0)]
+    stream = STREAM
     last = PASSES - 1
+    last_up = ("w3", E - 1, last)
+    last_down = ("w2", E - 1, 0)
 
     with ExitStack() as ctx:
         keep = ctx.enter_context(tc.tile_pool(name="keep", bufs=1))
-        raw_pool = ctx.enter_context(tc.tile_pool(name="raw", bufs=10))
-        rounded_pool = ctx.enter_context(tc.tile_pool(name="rounded", bufs=8))
-        hidden_pool = ctx.enter_context(tc.tile_pool(name="hidden", bufs=1))
-        y_pool = ctx.enter_context(tc.tile_pool(name="y", bufs=BLOCKS))
+        raw_pool = ctx.enter_context(tc.tile_pool(name="raw", bufs=RAW_BUFS))
+        rounded_pool = ctx.enter_context(tc.tile_pool(name="rounded", bufs=ROUNDED_BUFS))
         psum = ctx.enter_context(tc.psum_pool(name="psum", bufs=1))
 
         offsets = keep.tile([P, E * LIST_COLS], U16, name="offsets")
         nc.sync.dma_start(offsets[:], offs)
 
-        x_scales = keep.tile([P, T], U8, name="x_scales", align_bytes=64)
-        nc.gpsimd.memset(x_scales[:], 0)
+        x_scales = keep.tile([P, WINDOW], U8, name="x_scales", align_bytes=64)
+        nc.gpsimd.memset(x_scales[:, 0:T], 0)
 
         windows = [keep.tile([P, T], F32, name=f"window{n}") for n in range(BLOCKS)]
 
         raws, rounded, codes = {}, {}, {}
         gates, slot_words, slot_scales = {}, {}, {}
-        sums, gelus, hidden_codes, y_slots = {}, {}, {}, {}
+        sums, gelus, hidden_rounded, hidden_codes = {}, {}, {}, {}
 
-        def expert_list(e):
-            return offsets[:, e * LIST_COLS : (e + 1) * LIST_COLS]
+        def load_gate(e):
+            gt = keep.tile([P, BLOCKS, C], F32, name=f"gate{e}")
+            nc.sync.dma_start(gt[:], gate[:, e * C : (e + 1) * C].rearrange("(n p) c -> p n c", p=P))
+            gates[e] = gt
 
         def load(entry):
             kind, e, s = entry
+            if entry == GATE_BEFORE[0] or entry == GATE_BEFORE[1]:
+                load_gate(GATE_BEFORE.index(entry))
             raw = raw_pool.tile([P, PACK, WIDTH], F32, name="raw")
             raws[entry] = raw
             if kind == "w2":
                 rows = w2[e].rearrange("(q t r) n -> r q t n", t=4, r=4)
-                for r in range(4):
-                    nc.sync.dma_start(raw[r::4], rows[r])
-                gt = keep.tile([P, BLOCKS, C], F32, name=f"gate{e}")
-                nc.sync.dma_start(gt[:], gate[:, e * C : (e + 1) * C].rearrange("(n p) c -> p n c", p=P))
-                gates[e] = gt
+                for c0 in range(0, WIDTH, WIDTH // W2_LOADS[e]):
+                    cols = slice(c0, c0 + WIDTH // W2_LOADS[e])
+                    for r in range(4):
+                        nc.sync.dma_start(raw[r::4, :, cols], rows[r][:, :, cols])
+                if entry == last_down:
+                    load_gate(e)
                 return
             source = xT if kind == "x" else up_weights[kind][e]
             nc.sync.dma_start(raw[:], source[s * K_PASS : (s + 1) * K_PASS, :].rearrange("(p j) c -> p j c", j=PACK))
@@ -91,10 +106,10 @@ def tile_routed_moe_kernel(tc, xT, w1, w3, w2, gate, offs, out):
                 src[:].rearrange("p j (c i) -> p c j i", i=4)[:, c0 // 4 : c1 // 4],
             )
 
-        def interleave_permuted(copy, dst, src, q0, q1):
+        def interleave_permuted(copy, dst, src, ts, qs):
             copy(
-                dst[:].rearrange("p (t q r j) -> p t q j r", t=4, r=4, j=PACK)[:, :, q0:q1],
-                src[:].rearrange("p j (q t r) -> p t q j r", t=4, r=4)[:, :, q0:q1],
+                dst[:].rearrange("p (t q r j) -> p t q j r", t=4, r=4, j=PACK)[:, ts, qs],
+                src[:].rearrange("p j (q t r) -> p t q j r", t=4, r=4)[:, ts, qs],
             )
 
         def round_to_bf16(entry):
@@ -103,83 +118,99 @@ def tile_routed_moe_kernel(tc, xT, w1, w3, w2, gate, offs, out):
             dst = rounded_pool.tile([P, PACK * WIDTH], BF16, name="dst", align_bytes=64)
             rounded[entry] = dst
             on_vector = VECTOR_GROUPS[kind, e][s]
-            if kind in up_weights:
+            if kind == "w3" and s == last and LAST_BY_T:
+                interleave_permuted(nc.vector.tensor_copy, dst, raw, slice(0, 2), slice(0, GROUPS))
+                interleave_permuted(nc.scalar.copy, dst, raw, slice(2, 4), slice(0, GROUPS))
+            elif kind in up_weights:
                 if on_vector > 0:
-                    interleave_permuted(nc.vector.tensor_copy, dst, raw, 0, on_vector)
-                interleave_permuted(nc.scalar.copy, dst, raw, on_vector, WIDTH // GROUP)
+                    interleave_permuted(nc.vector.tensor_copy, dst, raw, slice(0, 4), slice(0, on_vector))
+                if on_vector < GROUPS:
+                    interleave_permuted(nc.scalar.copy, dst, raw, slice(0, 4), slice(on_vector, GROUPS))
+            elif kind == "w2":
+                for n in range(BLOCKS):
+                    interleave(nc.scalar.copy if n >= W2V[e] else nc.vector.tensor_copy, dst, raw, n * P, (n + 1) * P)
             else:
-                cuts = (0, HALF, WIDTH) if entry == stream[-1] else (on_vector * GROUP, WIDTH)
                 if on_vector > 0:
                     interleave(nc.vector.tensor_copy, dst, raw, 0, on_vector * GROUP)
-                for c0, c1 in zip(cuts[:-1], cuts[1:]):
-                    interleave(nc.scalar.copy, dst, raw, c0, c1)
+                if on_vector < GROUPS:
+                    interleave(nc.scalar.copy, dst, raw, on_vector * GROUP, WIDTH)
 
         def quantize(entry):
             kind, e, s = entry
             src = rounded[entry]
-            if kind == "w2":
-                words = hidden_pool.tile([P, WIDTH], U32, name="w2_words", tag="h", align_bytes=64)
-                scales = hidden_pool.tile([P, WIDTH], U8, name="w2_scales", tag="h_rounded", align_bytes=64)
-            else:
-                words = keep.tile([P, WIDTH], U32, name=f"{kind}_words{e}_{s}", align_bytes=64)
             if kind == "x":
-                scales = x_scales
-                nc.vector.quantize_mx(words[:].bitcast(FP8X4), x_scales[4 * s : P, :], src[:])
-            else:
-                if kind != "w2":
-                    scales = keep.tile([P, WIDTH], U8, name=f"{kind}_scales{e}_{s}", align_bytes=64)
-                cuts = (0, HALF, WIDTH) if entry in stream[-2:] else (0, WIDTH)
-                for c0, c1 in zip(cuts[:-1], cuts[1:]):
-                    nc.vector.quantize_mx(
-                        words[:, c0:c1].bitcast(FP8X4), scales[:, c0:c1], src[:, PACK * c0 : PACK * c1]
-                    )
+                words = keep.tile([P, WINDOW], U32, name=f"x_words{s}", align_bytes=64)
+                nc.vector.quantize_mx(words[:, 0:T].bitcast(FP8X4), x_scales[4 * s : P, 0:T], src[:])
+                codes[entry] = (words, x_scales)
+                return
+            words = keep.tile([P, WIDTH], U32, name=f"{kind}_words{e}_{s}", align_bytes=64)
+            scales = keep.tile([P, WIDTH], U8, name=f"{kind}_scales{e}_{s}", align_bytes=64)
+            pieces = 2 if (kind, s) == ("w3", last) else BLOCKS if kind == "w2" else 1
+            for i in range(pieces):
+                c0, c1 = i * WIDTH // pieces, (i + 1) * WIDTH // pieces
+                nc.vector.quantize_mx(words[:, c0:c1].bitcast(FP8X4), scales[:, c0:c1], src[:, PACK * c0 : PACK * c1])
             codes[entry] = (words, scales)
 
-        def gather(e):
-            bytes_of_slots = keep.tile([P, C], U8, name=f"slot_scales{e}", align_bytes=64)
-            nc.vector.tensor_copy(bytes_of_slots[:], x_scales[:].indirect(expert_list(e)))
-            slot_scales[e] = bytes_of_slots
-            for s in range(PASSES):
-                words_of_slots = keep.tile([P, C], U32, name=f"slot_words{e}_{s}", align_bytes=64)
-                nc.vector.tensor_copy(words_of_slots[:], codes["x", 0, s][0][:].indirect(expert_list(e)))
-                slot_words[e, s] = words_of_slots
+        def gather_words(s):
+            words_of_slots = keep.tile([P, SLOTS], U32, name=f"slot_words{s}", align_bytes=64)
+            nc.vector.tensor_copy(words_of_slots[:], codes["x", 0, s][0][:].indirect(offsets[:]))
+            slot_words[s] = words_of_slots
+
+        def gather_scales():
+            bytes_of_slots = keep.tile([P, SLOTS], U8, name="slot_scales", align_bytes=64)
+            nc.vector.tensor_copy(bytes_of_slots[:], x_scales[:].indirect(offsets[:]))
+            slot_scales[0] = bytes_of_slots
 
         def multiply_up(entry):
             kind, e, s = entry
             if s == 0:
                 sums[kind, e] = [
-                    psum.tile([P, BANK], F32, name=f"{kind}_bank{t}", tag=f"{kind}_bank{t}") for t in range(BLOCKS)
+                    psum.tile([P, BANK], F32, name=f"{kind}_{e}_bank{u}", tag=f"{kind}_{e}_bank{u}") for u in range(2)
                 ]
             words, scales = codes[entry]
-            for t in range(BLOCKS):
-                cols = slice(t * P, (t + 1) * P)
-                nc.tensor.matmul_mx(
-                    sums[kind, e][t][:, 0:C],
-                    lhsT=words[:, cols].bitcast(FP8X4),
-                    lhsT_scale=scales[:, cols],
-                    rhs=slot_words[e, s][:].bitcast(FP8X4),
-                    rhs_scale=slot_scales[e][4 * s : P, :],
-                    start=(s == 0),
-                    stop=(s == last),
+            if True:
+                for u in range(2):
+                    slots = slice(e * C + u * HALF_C, e * C + (u + 1) * HALF_C)
+                    for t in range(BLOCKS):
+                        cols = slice(t * P, (t + 1) * P)
+                        nc.tensor.matmul_mx(
+                            sums[kind, e][u][:, t * HALF_C : (t + 1) * HALF_C],
+                            lhsT=words[:, cols].bitcast(FP8X4),
+                            lhsT_scale=scales[:, cols],
+                            rhs=slot_words[s][:, slots].bitcast(FP8X4),
+                            rhs_scale=slot_scales[0][4 * s : P, slots],
+                            start=(s == 0 and t == 0),
+                            stop=(s == last and t == BLOCKS - 1),
+                        )
+
+        def by_slot(bank):
+            return bank[:].rearrange("p (t c) -> p c t", t=PACK)
+
+        def gelu(e, host):
+            gelus[e] = raws[host][:, 0:2, :]
+            for u in range(2):
+                nc.scalar.activation(
+                    gelus[e][:, u, :].rearrange("p (c t) -> p c t", t=PACK), by_slot(sums["w1", e][u]), GELU
                 )
 
-        def gelu(e):
-            gelus[e] = raws["w3", e, last][:, :, HALF:WIDTH]
-            for t in range(BLOCKS):
-                nc.scalar.activation(gelus[e][:, t, :], sums["w1", e][t][:, 0:C], GELU)
-
         def hidden(e):
-            h = hidden_pool.tile([P, PACK, C], F32, name="h", tag="h", align_bytes=64)
-            for t in range(BLOCKS):
-                nc.vector.tensor_tensor(h[:, t, :], sums["w3", e][t][:, 0:C], gelus[e][:, t, :], MULT)
-            h_rounded = hidden_pool.tile([P, PACK * C], BF16, name="h_rounded", tag="h_rounded", align_bytes=64)
-            interleave(nc.vector.tensor_copy, h_rounded, h, 0, C)
-            h_words = hidden_pool.tile([P, C], U32, name="h_words", align_bytes=64)
-            h_scales = hidden_pool.tile([P, C], U8, name="h_scales", align_bytes=64)
-            nc.vector.quantize_mx(h_words[:].bitcast(FP8X4), h_scales[:], h_rounded[:])
+            h = keep.tile([P, PACK * C], BF16, name=f"h{e}", align_bytes=64)
+            for u in range(2):
+                nc.vector.tensor_tensor(
+                    h[:, u * BANK : (u + 1) * BANK].rearrange("p (c t) -> p c t", t=PACK),
+                    by_slot(sums["w3", e][u]),
+                    gelus[e][:, u, :].rearrange("p (c t) -> p c t", t=PACK),
+                    MULT,
+                )
+            h_words = keep.tile([P, C], U32, name=f"h_words{e}", align_bytes=64)
+            h_scales = keep.tile([P, C], U8, name=f"h_scales{e}", align_bytes=64)
+            pieces = 2
+            for i in range(pieces):
+                c0, c1 = i * C // pieces, (i + 1) * C // pieces
+                nc.vector.quantize_mx(h_words[:, c0:c1].bitcast(FP8X4), h_scales[:, c0:c1], h[:, PACK * c0 : PACK * c1])
             hidden_codes[e] = (h_words, h_scales)
 
-        def multiply_down(e, n, bank):
+        def multiply_down(e, n, c0, c1, bank):
             words, scales = codes["w2", e, 0]
             h_words, h_scales = hidden_codes[e]
             cols = slice(n * P, (n + 1) * P)
@@ -187,58 +218,57 @@ def tile_routed_moe_kernel(tc, xT, w1, w3, w2, gate, offs, out):
                 bank,
                 lhsT=words[:, cols].bitcast(FP8X4),
                 lhsT_scale=scales[:, cols],
-                rhs=h_words[:].bitcast(FP8X4),
-                rhs_scale=h_scales[:],
+                rhs=h_words[:, c0:c1].bitcast(FP8X4),
+                rhs_scale=h_scales[:, c0:c1],
                 start=True,
                 stop=True,
             )
 
-        def down_in_pairs(e, n):
-            tag = f"w3_bank{2 + n // 2}"
-            y = psum.tile([P, BANK], F32, name=tag, tag=tag)
-            for b in range(2):
-                multiply_down(e, n + b, y[:, b * C : (b + 1) * C])
-            y_sbuf = raws["w1", e + 1, 0][:, n : n + 2, HALF:WIDTH]
-            nc.scalar.copy(y_sbuf, y[:].rearrange("p (b c) -> p b c", b=2))
-            for b in range(2):
-                y_slots[e, n + b] = y_sbuf[:, b, :]
+        def scatter(e, n, c0, c1, y_sbuf):
+            entries = offsets[:, (e * C + c0) // 16 : (e * C + c1) // 16]
+            nc.vector.tensor_tensor(windows[n][:].indirect(entries), y_sbuf, gates[e][:, n, c0:c1], MULT)
 
-        def down(e, n):
-            tag = f"w1_bank{n}"
+        def down(e, n, c0, c1, tag):
             y = psum.tile([P, BANK], F32, name=tag, tag=tag)
-            multiply_down(e, n, y[:, 0:C])
-            y_sbuf = y_pool.tile([P, C], F32, name="y_sbuf")
-            nc.scalar.copy(y_sbuf[:], y[:, 0:C])
-            y_slots[e, n] = y_sbuf[:]
+            multiply_down(e, n, c0, c1, y[:, 0 : c1 - c0])
+            y_sbuf = keep.tile([P, c1 - c0], F32, name=f"y{e}_{n}_{c0}")
+            nc.scalar.copy(y_sbuf[:], y[:, 0 : c1 - c0])
+            scatter(e, n, c0, c1, y_sbuf[:])
 
-        def scatter(e, n):
-            nc.vector.tensor_tensor(windows[n][:].indirect(expert_list(e)), y_slots[e, n], gates[e][:, n, :], MULT)
+        def way_back(e, banks):
+            if SPLIT0[e]:
+                down(e, 0, 0, HALF_C, banks[0])
+                down(e, 0, HALF_C, C, banks[1])
+            else:
+                down(e, 0, 0, C, banks[0])
+            for n in range(BLOCKS):
+                if n > 0:
+                    down(e, n, 0, C, banks[n + 1])
+                if e == E - 1:
+                    nc.sync.dma_start(out[n * P : (n + 1) * P, :], windows[n][:])
 
         load(stream[0])
         round_to_bf16(stream[0])
         for i, entry in enumerate(stream):
+            kind, e, s = entry
             if i + 1 < len(stream):
                 load(stream[i + 1])
-                round_to_bf16(stream[i + 1])
-            kind, e, s = entry
+                if kind != "w2":
+                    round_to_bf16(stream[i + 1])
             if kind == "w2":
                 hidden(e)
             quantize(entry)
+            if kind == "x" and s > 0:
+                gather_words(s - 1)
             if entry == ("x", 0, last):
-                gather(0)
+                gather_scales()
+                gather_words(last)
             if kind in up_weights:
                 multiply_up(entry)
-            if entry == ("w1", 0, last):
-                gather(1)
-            if kind == "w3" and s == last:
-                gelu(e)
-            if entry == ("w1", 1, 0):
-                for n in range(0, BLOCKS, 2):
-                    down_in_pairs(0, n)
-                    scatter(0, n)
-                    scatter(0, n + 1)
-
-        for n in range(BLOCKS):
-            down(1, n)
-            scatter(1, n)
-            nc.sync.dma_start(out[n * P : (n + 1) * P, :], windows[n][:])
+            if entry in GELU_HOST:
+                gelu(GELU_HOST.index(entry), entry)
+            if kind == "w2":
+                o = 1 - e
+                way_back(e, [f"w1_{e}_bank0", f"w1_{e}_bank1", f"w3_{o}_bank0", f"w3_{o}_bank1", f"w1_{o}_bank0"])
+                if i + 1 < len(stream):
+                    round_to_bf16(stream[i + 1])

@@ -31,9 +31,9 @@ HALF_C = C // 2
 WINDOW = T + T // 2
 
 VECTOR_GROUPS = {
-    ("x", 0): (0, 0, 0, 0,),
+    ("x", 0): (8, 8, 8, 8,),
     ("w1", 0): (0, 32, 0, 32,),
-    ("w3", 0): (0, 32, 16, 20,),
+    ("w3", 0): (16, 32, 16, 20,),
     ("w2", 0): (12,),
     ("w1", 1): (0, 0, 0, 32,),
     ("w3", 1): (0, 32, 16, 20,),
@@ -48,6 +48,8 @@ W2V = (0, 0)
 SPLIT0 = (True, True)
 LAST_BY_T = False
 W2_LOADS = (1, 1)
+Y_HOST = {(0, 2): ("w1", 1, 0), (0, 3): ("w1", 1, 1)}
+RUN = 2
 
 
 def tile_routed_moe_kernel(tc, xT, w1, w3, w2, gate, offs, out):
@@ -89,11 +91,11 @@ def tile_routed_moe_kernel(tc, xT, w1, w3, w2, gate, offs, out):
             raw = raw_pool.tile([P, PACK, WIDTH], F32, name="raw")
             raws[entry] = raw
             if kind == "w2":
-                rows = w2[e].rearrange("(q t r) n -> r q t n", t=4, r=4)
+                rows = w2[e].rearrange("(q t r) n -> r q t n", t=4, r=RUN)
                 for c0 in range(0, WIDTH, WIDTH // W2_LOADS[e]):
                     cols = slice(c0, c0 + WIDTH // W2_LOADS[e])
-                    for r in range(4):
-                        nc.sync.dma_start(raw[r::4, :, cols], rows[r][:, :, cols])
+                    for r in range(RUN):
+                        nc.sync.dma_start(raw[r::RUN, :, cols], rows[r][:, :, cols])
                 if entry == last_down:
                     load_gate(e)
                 return
@@ -102,14 +104,15 @@ def tile_routed_moe_kernel(tc, xT, w1, w3, w2, gate, offs, out):
 
         def interleave(copy, dst, src, c0, c1):
             copy(
-                dst[:].rearrange("p (c i j) -> p c j i", i=4, j=PACK)[:, c0 // 4 : c1 // 4],
-                src[:].rearrange("p j (c i) -> p c j i", i=4)[:, c0 // 4 : c1 // 4],
+                dst[:].rearrange("p (c i j) -> p c j i", i=RUN, j=PACK)[:, c0 // RUN : c1 // RUN],
+                src[:].rearrange("p j (c i) -> p c j i", i=RUN)[:, c0 // RUN : c1 // RUN],
             )
 
         def interleave_permuted(copy, dst, src, ts, qs):
+            qs = slice(qs.start * 4 // RUN, qs.stop * 4 // RUN)
             copy(
-                dst[:].rearrange("p (t q r j) -> p t q j r", t=4, r=4, j=PACK)[:, ts, qs],
-                src[:].rearrange("p j (q t r) -> p t q j r", t=4, r=4)[:, ts, qs],
+                dst[:].rearrange("p (t q r j) -> p t q j r", t=4, r=RUN, j=PACK)[:, ts, qs],
+                src[:].rearrange("p j (q t r) -> p t q j r", t=4, r=RUN)[:, ts, qs],
             )
 
         def round_to_bf16(entry):
@@ -127,8 +130,7 @@ def tile_routed_moe_kernel(tc, xT, w1, w3, w2, gate, offs, out):
                 if on_vector < GROUPS:
                     interleave_permuted(nc.scalar.copy, dst, raw, slice(0, 4), slice(on_vector, GROUPS))
             elif kind == "w2":
-                for n in range(BLOCKS):
-                    interleave(nc.scalar.copy if n >= W2V[e] else nc.vector.tensor_copy, dst, raw, n * P, (n + 1) * P)
+                pass
             else:
                 if on_vector > 0:
                     interleave(nc.vector.tensor_copy, dst, raw, 0, on_vector * GROUP)
@@ -145,7 +147,7 @@ def tile_routed_moe_kernel(tc, xT, w1, w3, w2, gate, offs, out):
                 return
             words = keep.tile([P, WIDTH], U32, name=f"{kind}_words{e}_{s}", align_bytes=64)
             scales = keep.tile([P, WIDTH], U8, name=f"{kind}_scales{e}_{s}", align_bytes=64)
-            pieces = 2 if (kind, s) == ("w3", last) else BLOCKS if kind == "w2" else 1
+            pieces = 2 if (kind, s) == ("w3", last) else 0 if kind == "w2" else 1
             for i in range(pieces):
                 c0, c1 = i * WIDTH // pieces, (i + 1) * WIDTH // pieces
                 nc.vector.quantize_mx(words[:, c0:c1].bitcast(FP8X4), scales[:, c0:c1], src[:, PACK * c0 : PACK * c1])
@@ -231,21 +233,30 @@ def tile_routed_moe_kernel(tc, xT, w1, w3, w2, gate, offs, out):
         def down(e, n, c0, c1, tag):
             y = psum.tile([P, BANK], F32, name=tag, tag=tag)
             multiply_down(e, n, c0, c1, y[:, 0 : c1 - c0])
-            y_sbuf = keep.tile([P, c1 - c0], F32, name=f"y{e}_{n}_{c0}")
-            nc.scalar.copy(y_sbuf[:], y[:, 0 : c1 - c0])
-            scatter(e, n, c0, c1, y_sbuf[:])
+            if (e, n) in Y_HOST:
+                y_sbuf = raws[Y_HOST[e, n]][:, 2 + n % 2, c0:c1]
+            else:
+                y_sbuf = keep.tile([P, c1 - c0], F32, name=f"y{e}_{n}_{c0}")[:]
+            nc.scalar.copy(y_sbuf, y[:, 0 : c1 - c0])
+            scatter(e, n, c0, c1, y_sbuf)
 
-        def way_back(e, banks):
-            if SPLIT0[e]:
+        def w2_block(e, n):
+            entry = ("w2", e, 0)
+            words, scales = codes[entry]
+            cols = slice(n * P, (n + 1) * P)
+            interleave(nc.scalar.copy if n >= W2V[e] else nc.vector.tensor_copy, rounded[entry], raws[entry], n * P, (n + 1) * P)
+            nc.vector.quantize_mx(words[:, cols].bitcast(FP8X4), scales[:, cols], rounded[entry][:, n * BANK : (n + 1) * BANK])
+
+        def way_back(e, n):
+            o = 1 - e
+            banks = [f"w1_{e}_bank0", f"w1_{e}_bank1", f"w3_{o}_bank0", f"w3_{o}_bank1", f"w3_{e}_bank0"]
+            if n == 0 and SPLIT0[e]:
                 down(e, 0, 0, HALF_C, banks[0])
                 down(e, 0, HALF_C, C, banks[1])
             else:
-                down(e, 0, 0, C, banks[0])
-            for n in range(BLOCKS):
-                if n > 0:
-                    down(e, n, 0, C, banks[n + 1])
-                if e == E - 1:
-                    nc.sync.dma_start(out[n * P : (n + 1) * P, :], windows[n][:])
+                down(e, n, 0, C, banks[n + 1])
+            if e == E - 1:
+                nc.sync.dma_start(out[n * P : (n + 1) * P, :], windows[n][:])
 
         load(stream[0])
         round_to_bf16(stream[0])
@@ -268,7 +279,13 @@ def tile_routed_moe_kernel(tc, xT, w1, w3, w2, gate, offs, out):
             if entry in GELU_HOST:
                 gelu(GELU_HOST.index(entry), entry)
             if kind == "w2":
-                o = 1 - e
-                way_back(e, [f"w1_{e}_bank0", f"w1_{e}_bank1", f"w3_{o}_bank0", f"w3_{o}_bank1", f"w1_{o}_bank0"])
+                for n in range(BLOCKS):
+                    w2_block(e, n)
+                for n in range(BLOCKS):
+                    if (e, n) not in Y_HOST or Y_HOST[e, n] == entry:
+                        way_back(e, n)
                 if i + 1 < len(stream):
                     round_to_bf16(stream[i + 1])
+            for (e2, n), host in Y_HOST.items():
+                if host == entry and kind != "w2":
+                    way_back(e2, n)

@@ -33,23 +33,30 @@ WINDOW = T + T // 2
 VECTOR_GROUPS = {
     ("x", 0): (8, 8, 8, 8,),
     ("w1", 0): (0, 32, 0, 32,),
-    ("w3", 0): (16, 32, 16, 20,),
+    ("w3", 0): (16, 32, 32, 16,),
     ("w2", 0): (12,),
     ("w1", 1): (0, 0, 0, 32,),
-    ("w3", 1): (0, 32, 16, 20,),
+    ("w3", 1): (0, 32, 16, 16,),
     ("w2", 1): (0,),
 }
 STREAM = [("x", 0, s) for s in range(PASSES)] + [("w1", 0, s) for s in range(PASSES)] + [("w3", 0, s) for s in range(PASSES)] + [("w2", 0, 0)] + [("w1", 1, s) for s in range(PASSES)] + [("w3", 1, s) for s in range(PASSES)] + [("w2", 1, 0)]
 GATE_BEFORE = [("w1", 1, 0), None]
-RAW_BUFS = 12
-ROUNDED_BUFS = 8
+RAW_BUFS = 9
+ROUNDED_BUFS = 7
 GELU_HOST = [("w3", 0, 0), ("w3", 1, 0)]
 W2V = (0, 0)
 SPLIT0 = (True, True)
-LAST_BY_T = False
-W2_LOADS = (1, 1)
+LAST_BY_T = True
+W2_LOADS = (1, 2)
 Y_HOST = {(0, 2): ("w1", 1, 0), (0, 3): ("w1", 1, 1)}
 RUN = 2
+GATE_LOADS = (1, 2)
+W2_PIECES = (4, 4)
+HIDDEN_AT = [("w2", 0, 0), ("w2", 1, 0)]
+WAY_AT = [("w2", 0, 0), ("w2", 1, 0)]
+PRUN = 2
+OFFS_LATE = True
+PAIRED = [("x", 0, 2), ("w1", 0, 0), ("w1", 0, 2)]
 
 
 def tile_routed_moe_kernel(tc, xT, w1, w3, w2, gate, offs, out):
@@ -64,11 +71,12 @@ def tile_routed_moe_kernel(tc, xT, w1, w3, w2, gate, offs, out):
     with ExitStack() as ctx:
         keep = ctx.enter_context(tc.tile_pool(name="keep", bufs=1))
         raw_pool = ctx.enter_context(tc.tile_pool(name="raw", bufs=RAW_BUFS))
+        pair_pool = ctx.enter_context(tc.tile_pool(name="pair", bufs=max(1, len(PAIRED))))
+        code_pool = ctx.enter_context(tc.tile_pool(name="codes", bufs=8))
         rounded_pool = ctx.enter_context(tc.tile_pool(name="rounded", bufs=ROUNDED_BUFS))
         psum = ctx.enter_context(tc.psum_pool(name="psum", bufs=1))
 
         offsets = keep.tile([P, E * LIST_COLS], U16, name="offsets")
-        nc.sync.dma_start(offsets[:], offs)
 
         x_scales = keep.tile([P, WINDOW], U8, name="x_scales", align_bytes=64)
         nc.gpsimd.memset(x_scales[:, 0:T], 0)
@@ -76,26 +84,42 @@ def tile_routed_moe_kernel(tc, xT, w1, w3, w2, gate, offs, out):
         windows = [keep.tile([P, T], F32, name=f"window{n}") for n in range(BLOCKS)]
 
         raws, rounded, codes = {}, {}, {}
+        w2_parts = {}
         gates, slot_words, slot_scales = {}, {}, {}
         sums, gelus, hidden_rounded, hidden_codes = {}, {}, {}, {}
 
         def load_gate(e):
             gt = keep.tile([P, BLOCKS, C], F32, name=f"gate{e}")
-            nc.sync.dma_start(gt[:], gate[:, e * C : (e + 1) * C].rearrange("(n p) c -> p n c", p=P))
+            rows = gate[:, e * C : (e + 1) * C].rearrange("(n p) c -> p n c", p=P)
+            for n0 in range(0, BLOCKS, BLOCKS // GATE_LOADS[e]):
+                n1 = n0 + BLOCKS // GATE_LOADS[e]
+                nc.sync.dma_start(gt[:, n0:n1], rows[:, n0:n1])
             gates[e] = gt
 
         def load(entry):
             kind, e, s = entry
             if entry == GATE_BEFORE[0] or entry == GATE_BEFORE[1]:
                 load_gate(GATE_BEFORE.index(entry))
+            if entry in raws:
+                return
+            if entry in PAIRED:
+                pair = pair_pool.tile([P, 2, PACK, WIDTH], F32, name="pair")
+                source = xT if kind == "x" else up_weights[kind][e]
+                rows = source[s * K_PASS : (s + 2) * K_PASS, :].rearrange("(g p j) c -> p g (j c)", g=2, j=PACK)
+                nc.sync.dma_start(pair[:].rearrange("p g j c -> p g (j c)"), rows)
+                raws[entry] = pair[:, 0]
+                raws[kind, e, s + 1] = pair[:, 1]
+                return
             raw = raw_pool.tile([P, PACK, WIDTH], F32, name="raw")
             raws[entry] = raw
             if kind == "w2":
                 rows = w2[e].rearrange("(q t r) n -> r q t n", t=4, r=RUN)
-                for c0 in range(0, WIDTH, WIDTH // W2_LOADS[e]):
-                    cols = slice(c0, c0 + WIDTH // W2_LOADS[e])
+                parts = raw[:].rearrange("p j c -> p (j c)").rearrange("p (g j c) -> p g j c", g=W2_LOADS[e], j=PACK)
+                w2_parts[e] = parts
+                for g in range(W2_LOADS[e]):
+                    cols = slice(g * WIDTH // W2_LOADS[e], (g + 1) * WIDTH // W2_LOADS[e])
                     for r in range(RUN):
-                        nc.sync.dma_start(raw[r::RUN, :, cols], rows[r][:, :, cols])
+                        nc.sync.dma_start(parts[r::RUN, g], rows[r][:, :, cols])
                 if entry == last_down:
                     load_gate(e)
                 return
@@ -145,8 +169,8 @@ def tile_routed_moe_kernel(tc, xT, w1, w3, w2, gate, offs, out):
                 nc.vector.quantize_mx(words[:, 0:T].bitcast(FP8X4), x_scales[4 * s : P, 0:T], src[:])
                 codes[entry] = (words, x_scales)
                 return
-            words = keep.tile([P, WIDTH], U32, name=f"{kind}_words{e}_{s}", align_bytes=64)
-            scales = keep.tile([P, WIDTH], U8, name=f"{kind}_scales{e}_{s}", align_bytes=64)
+            words = code_pool.tile([P, WIDTH], U32, name=f"{kind}_words{e}_{s}", tag="words", align_bytes=64)
+            scales = code_pool.tile([P, WIDTH], U8, name=f"{kind}_scales{e}_{s}", tag="scales", align_bytes=64)
             pieces = 2 if (kind, s) == ("w3", last) else 0 if kind == "w2" else 1
             for i in range(pieces):
                 c0, c1 = i * WIDTH // pieces, (i + 1) * WIDTH // pieces
@@ -186,27 +210,30 @@ def tile_routed_moe_kernel(tc, xT, w1, w3, w2, gate, offs, out):
                         )
 
         def by_slot(bank):
-            return bank[:].rearrange("p (t c) -> p c t", t=PACK)
+            return bank[:].rearrange("p (t c i) -> p c t i", t=PACK, i=PRUN)
+
+        def interleaved(rows):
+            return rows.rearrange("p (c i t) -> p c t i", t=PACK, i=PRUN)
 
         def gelu(e, host):
             gelus[e] = raws[host][:, 0:2, :]
             for u in range(2):
                 nc.scalar.activation(
-                    gelus[e][:, u, :].rearrange("p (c t) -> p c t", t=PACK), by_slot(sums["w1", e][u]), GELU
+                    interleaved(gelus[e][:, u, :]), by_slot(sums["w1", e][u]), GELU
                 )
 
         def hidden(e):
             h = keep.tile([P, PACK * C], BF16, name=f"h{e}", align_bytes=64)
             for u in range(2):
                 nc.vector.tensor_tensor(
-                    h[:, u * BANK : (u + 1) * BANK].rearrange("p (c t) -> p c t", t=PACK),
+                    interleaved(h[:, u * BANK : (u + 1) * BANK]),
                     by_slot(sums["w3", e][u]),
-                    gelus[e][:, u, :].rearrange("p (c t) -> p c t", t=PACK),
+                    interleaved(gelus[e][:, u, :]),
                     MULT,
                 )
             h_words = keep.tile([P, C], U32, name=f"h_words{e}", align_bytes=64)
             h_scales = keep.tile([P, C], U8, name=f"h_scales{e}", align_bytes=64)
-            pieces = 2
+            pieces = 2 if SPLIT0[e] else 1
             for i in range(pieces):
                 c0, c1 = i * C // pieces, (i + 1) * C // pieces
                 nc.vector.quantize_mx(h_words[:, c0:c1].bitcast(FP8X4), h_scales[:, c0:c1], h[:, PACK * c0 : PACK * c1])
@@ -233,19 +260,25 @@ def tile_routed_moe_kernel(tc, xT, w1, w3, w2, gate, offs, out):
         def down(e, n, c0, c1, tag):
             y = psum.tile([P, BANK], F32, name=tag, tag=tag)
             multiply_down(e, n, c0, c1, y[:, 0 : c1 - c0])
-            if (e, n) in Y_HOST:
+            if (e, n) in Y_HOST and Y_HOST[e, n][0] == "w2":
+                last_part = w2_parts[e][:, W2_LOADS[e] - 1, c0 // HALF_C + 2 * n]
+                y_sbuf = last_part[:, WIDTH // W2_LOADS[e] - (c1 - c0) :]
+            elif (e, n) in Y_HOST:
                 y_sbuf = raws[Y_HOST[e, n]][:, 2 + n % 2, c0:c1]
             else:
                 y_sbuf = keep.tile([P, c1 - c0], F32, name=f"y{e}_{n}_{c0}")[:]
             nc.scalar.copy(y_sbuf, y[:, 0 : c1 - c0])
             scatter(e, n, c0, c1, y_sbuf)
 
-        def w2_block(e, n):
+        def w2_block(e, n, width):
             entry = ("w2", e, 0)
             words, scales = codes[entry]
-            cols = slice(n * P, (n + 1) * P)
-            interleave(nc.scalar.copy if n >= W2V[e] else nc.vector.tensor_copy, rounded[entry], raws[entry], n * P, (n + 1) * P)
-            nc.vector.quantize_mx(words[:, cols].bitcast(FP8X4), scales[:, cols], rounded[entry][:, n * BANK : (n + 1) * BANK])
+            cols = slice(n * width, (n + 1) * width)
+            g, c0 = divmod(n * width, WIDTH // W2_LOADS[e])
+            part = rounded[entry][:, n * width * PACK : (n + 1) * width * PACK]
+            copy = nc.scalar.copy if n >= W2V[e] else nc.vector.tensor_copy
+            interleave(copy, part, w2_parts[e][:, g, :, c0 : c0 + width], 0, width)
+            nc.vector.quantize_mx(words[:, cols].bitcast(FP8X4), scales[:, cols], part)
 
         def way_back(e, n):
             o = 1 - e
@@ -258,7 +291,11 @@ def tile_routed_moe_kernel(tc, xT, w1, w3, w2, gate, offs, out):
             if e == E - 1:
                 nc.sync.dma_start(out[n * P : (n + 1) * P, :], windows[n][:])
 
+        if not OFFS_LATE:
+            nc.sync.dma_start(offsets[:], offs)
         load(stream[0])
+        if OFFS_LATE:
+            nc.sync.dma_start(offsets[:], offs)
         round_to_bf16(stream[0])
         for i, entry in enumerate(stream):
             kind, e, s = entry
@@ -266,8 +303,8 @@ def tile_routed_moe_kernel(tc, xT, w1, w3, w2, gate, offs, out):
                 load(stream[i + 1])
                 if kind != "w2":
                     round_to_bf16(stream[i + 1])
-            if kind == "w2":
-                hidden(e)
+            if entry == HIDDEN_AT[0] or entry == HIDDEN_AT[1]:
+                hidden(HIDDEN_AT.index(entry))
             quantize(entry)
             if kind == "x" and s > 0:
                 gather_words(s - 1)
@@ -279,11 +316,14 @@ def tile_routed_moe_kernel(tc, xT, w1, w3, w2, gate, offs, out):
             if entry in GELU_HOST:
                 gelu(GELU_HOST.index(entry), entry)
             if kind == "w2":
+                for n in range(W2_PIECES[e]):
+                    w2_block(e, n, WIDTH // W2_PIECES[e])
+            if entry in WAY_AT:
+                e2 = WAY_AT.index(entry)
                 for n in range(BLOCKS):
-                    w2_block(e, n)
-                for n in range(BLOCKS):
-                    if (e, n) not in Y_HOST or Y_HOST[e, n] == entry:
-                        way_back(e, n)
+                    if (e2, n) not in Y_HOST or Y_HOST[e2, n][0] == "w2":
+                        way_back(e2, n)
+            if kind == "w2":
                 if i + 1 < len(stream):
                     round_to_bf16(stream[i + 1])
             for (e2, n), host in Y_HOST.items():

@@ -33,17 +33,17 @@ WINDOW = T + T // 2
 VECTOR_GROUPS = {
     ("x", 0): (8, 8, 8, 8,),
     ("w1", 0): (0, 32, 0, 32,),
-    ("w3", 0): (16, 32, 32, 16,),
+    ("w3", 0): (16, 16, 32, 16,),
     ("w2", 0): (12,),
     ("w1", 1): (0, 0, 0, 32,),
-    ("w3", 1): (0, 32, 16, 16,),
+    ("w3", 1): (0, 16, 16, 16,),
     ("w2", 1): (0,),
 }
 STREAM = [("x", 0, s) for s in range(PASSES)] + [("w1", 0, s) for s in range(PASSES)] + [("w3", 0, s) for s in range(PASSES)] + [("w2", 0, 0)] + [("w1", 1, s) for s in range(PASSES)] + [("w3", 1, s) for s in range(PASSES)] + [("w2", 1, 0)]
 GATE_BEFORE = [("w1", 1, 0), None]
 RAW_BUFS = 9
 ROUNDED_BUFS = 7
-GELU_HOST = [("w3", 0, 0), ("w3", 1, 0)]
+GELU_HOST = [("w3", 0, 1), ("w3", 1, 2)]
 W2V = (0, 0)
 SPLIT0 = (True, True)
 LAST_BY_T = True
@@ -57,6 +57,10 @@ WAY_AT = [("w2", 0, 0), ("w2", 1, 0)]
 PRUN = 2
 OFFS_LATE = True
 PAIRED = [("x", 0, 2), ("w1", 0, 0), ("w1", 0, 2)]
+QPAIR = []
+LAST_V3 = (True, True)
+W2_CUTS = ((0, 512), (0, 256, 512))
+EARLY = (False, False)
 
 
 def tile_routed_moe_kernel(tc, xT, w1, w3, w2, gate, offs, out):
@@ -84,7 +88,7 @@ def tile_routed_moe_kernel(tc, xT, w1, w3, w2, gate, offs, out):
         windows = [keep.tile([P, T], F32, name=f"window{n}") for n in range(BLOCKS)]
 
         raws, rounded, codes = {}, {}, {}
-        w2_parts = {}
+        w2_parts, joined = {}, {}
         gates, slot_words, slot_scales = {}, {}, {}
         sums, gelus, hidden_rounded, hidden_codes = {}, {}, {}, {}
 
@@ -114,12 +118,13 @@ def tile_routed_moe_kernel(tc, xT, w1, w3, w2, gate, offs, out):
             raws[entry] = raw
             if kind == "w2":
                 rows = w2[e].rearrange("(q t r) n -> r q t n", t=4, r=RUN)
-                parts = raw[:].rearrange("p j c -> p (j c)").rearrange("p (g j c) -> p g j c", g=W2_LOADS[e], j=PACK)
-                w2_parts[e] = parts
-                for g in range(W2_LOADS[e]):
-                    cols = slice(g * WIDTH // W2_LOADS[e], (g + 1) * WIDTH // W2_LOADS[e])
+                flat = raw[:].rearrange("p j c -> p (j c)")
+                for c0, c1 in zip(W2_CUTS[e][:-1], W2_CUTS[e][1:]):
+                    part = flat[:, PACK * c0 : PACK * c1].rearrange("p (j c) -> p j c", j=PACK)
+                    for n in range(c0 // P, c1 // P):
+                        w2_parts[e, n] = part[:, :, n * P - c0 : (n + 1) * P - c0]
                     for r in range(RUN):
-                        nc.sync.dma_start(parts[r::RUN, g], rows[r][:, :, cols])
+                        nc.sync.dma_start(part[r::RUN], rows[r][:, :, c0:c1])
                 if entry == last_down:
                     load_gate(e)
                 return
@@ -142,12 +147,22 @@ def tile_routed_moe_kernel(tc, xT, w1, w3, w2, gate, offs, out):
         def round_to_bf16(entry):
             kind, e, s = entry
             raw = raws[entry]
-            dst = rounded_pool.tile([P, PACK * WIDTH], BF16, name="dst", align_bytes=64)
-            rounded[entry] = dst
+            if entry in QPAIR:
+                both = keep.tile([P, 2 * PACK * WIDTH], BF16, name=f"both_{kind}{e}_{s}", align_bytes=64)
+                joined[entry] = both
+                rounded[entry] = both[:, 0 : PACK * WIDTH]
+                rounded[kind, e, s + 1] = both[:, PACK * WIDTH :]
+            elif entry not in rounded:
+                rounded[entry] = rounded_pool.tile([P, PACK * WIDTH], BF16, name="dst", align_bytes=64)
+            dst = rounded[entry]
             on_vector = VECTOR_GROUPS[kind, e][s]
             if kind == "w3" and s == last and LAST_BY_T:
                 interleave_permuted(nc.vector.tensor_copy, dst, raw, slice(0, 2), slice(0, GROUPS))
-                interleave_permuted(nc.scalar.copy, dst, raw, slice(2, 4), slice(0, GROUPS))
+                if LAST_V3[e]:
+                    interleave_permuted(nc.vector.tensor_copy, dst, raw, slice(3, 4), slice(0, GROUPS))
+                    interleave_permuted(nc.scalar.copy, dst, raw, slice(2, 3), slice(0, GROUPS))
+                else:
+                    interleave_permuted(nc.scalar.copy, dst, raw, slice(2, 4), slice(0, GROUPS))
             elif kind in up_weights:
                 if on_vector > 0:
                     interleave_permuted(nc.vector.tensor_copy, dst, raw, slice(0, 4), slice(0, on_vector))
@@ -169,11 +184,22 @@ def tile_routed_moe_kernel(tc, xT, w1, w3, w2, gate, offs, out):
                 nc.vector.quantize_mx(words[:, 0:T].bitcast(FP8X4), x_scales[4 * s : P, 0:T], src[:])
                 codes[entry] = (words, x_scales)
                 return
+            if entry in QPAIR:
+                return
+            if (kind, e, s - 1) in QPAIR:
+                words = keep.tile([P, 2 * WIDTH], U32, name=f"{kind}_words{e}_{s}", align_bytes=64)
+                scales = keep.tile([P, 2 * WIDTH], U8, name=f"{kind}_scales{e}_{s}", align_bytes=64)
+                nc.vector.quantize_mx(words[:].bitcast(FP8X4), scales[:], joined[kind, e, s - 1][:])
+                codes[kind, e, s - 1] = (words[:, 0:WIDTH], scales[:, 0:WIDTH])
+                codes[entry] = (words[:, WIDTH:], scales[:, WIDTH:])
+                return
             words = code_pool.tile([P, WIDTH], U32, name=f"{kind}_words{e}_{s}", tag="words", align_bytes=64)
             scales = code_pool.tile([P, WIDTH], U8, name=f"{kind}_scales{e}_{s}", tag="scales", align_bytes=64)
             pieces = 2 if (kind, s) == ("w3", last) else 0 if kind == "w2" else 1
-            for i in range(pieces):
-                c0, c1 = i * WIDTH // pieces, (i + 1) * WIDTH // pieces
+            cuts = [i * WIDTH // pieces for i in range(pieces + 1)] if pieces else []
+            if pieces == 2 and LAST_V3[e]:
+                cuts = [0, 2 * P, 3 * P, 4 * P]
+            for c0, c1 in zip(cuts[:-1], cuts[1:]):
                 nc.vector.quantize_mx(words[:, c0:c1].bitcast(FP8X4), scales[:, c0:c1], src[:, PACK * c0 : PACK * c1])
             codes[entry] = (words, scales)
 
@@ -223,20 +249,22 @@ def tile_routed_moe_kernel(tc, xT, w1, w3, w2, gate, offs, out):
                 )
 
         def hidden(e):
-            h = keep.tile([P, PACK * C], BF16, name=f"h{e}", align_bytes=64)
+            h = [
+                keep.tile([P, BANK], BF16, name=f"h{e}_{u}", tag=f"first{e}" if u == 0 else f"second{e}", align_bytes=64)
+                for u in range(2)
+            ]
             for u in range(2):
                 nc.vector.tensor_tensor(
-                    interleaved(h[:, u * BANK : (u + 1) * BANK]),
+                    interleaved(h[u][:]),
                     by_slot(sums["w3", e][u]),
                     interleaved(gelus[e][:, u, :]),
                     MULT,
                 )
             h_words = keep.tile([P, C], U32, name=f"h_words{e}", align_bytes=64)
             h_scales = keep.tile([P, C], U8, name=f"h_scales{e}", align_bytes=64)
-            pieces = 2 if SPLIT0[e] else 1
-            for i in range(pieces):
-                c0, c1 = i * C // pieces, (i + 1) * C // pieces
-                nc.vector.quantize_mx(h_words[:, c0:c1].bitcast(FP8X4), h_scales[:, c0:c1], h[:, PACK * c0 : PACK * c1])
+            for u in range(2):
+                cols = slice(u * HALF_C, (u + 1) * HALF_C)
+                nc.vector.quantize_mx(h_words[:, cols].bitcast(FP8X4), h_scales[:, cols], h[u][:])
             hidden_codes[e] = (h_words, h_scales)
 
         def multiply_down(e, n, c0, c1, bank):
@@ -260,24 +288,23 @@ def tile_routed_moe_kernel(tc, xT, w1, w3, w2, gate, offs, out):
         def down(e, n, c0, c1, tag):
             y = psum.tile([P, BANK], F32, name=tag, tag=tag)
             multiply_down(e, n, c0, c1, y[:, 0 : c1 - c0])
-            if (e, n) in Y_HOST and Y_HOST[e, n][0] == "w2":
-                last_part = w2_parts[e][:, W2_LOADS[e] - 1, c0 // HALF_C + 2 * n]
-                y_sbuf = last_part[:, WIDTH // W2_LOADS[e] - (c1 - c0) :]
-            elif (e, n) in Y_HOST:
+            if (e, n) in Y_HOST:
                 y_sbuf = raws[Y_HOST[e, n]][:, 2 + n % 2, c0:c1]
             else:
                 y_sbuf = keep.tile([P, c1 - c0], F32, name=f"y{e}_{n}_{c0}")[:]
             nc.scalar.copy(y_sbuf, y[:, 0 : c1 - c0])
             scatter(e, n, c0, c1, y_sbuf)
 
-        def w2_block(e, n, width):
+        def w2_block(e, n):
             entry = ("w2", e, 0)
             words, scales = codes[entry]
-            cols = slice(n * width, (n + 1) * width)
-            g, c0 = divmod(n * width, WIDTH // W2_LOADS[e])
-            part = rounded[entry][:, n * width * PACK : (n + 1) * width * PACK]
+            cols = slice(n * P, (n + 1) * P)
+            if n == 0 and EARLY[e]:
+                part = keep.tile([P, BANK], BF16, name=f"w2_first{e}", tag=f"first{e}", align_bytes=64)[:]
+            else:
+                part = rounded[entry][:, n * BANK : (n + 1) * BANK]
             copy = nc.scalar.copy if n >= W2V[e] else nc.vector.tensor_copy
-            interleave(copy, part, w2_parts[e][:, g, :, c0 : c0 + width], 0, width)
+            interleave(copy, part, w2_parts[e, n], 0, P)
             nc.vector.quantize_mx(words[:, cols].bitcast(FP8X4), scales[:, cols], part)
 
         def way_back(e, n):
@@ -303,21 +330,25 @@ def tile_routed_moe_kernel(tc, xT, w1, w3, w2, gate, offs, out):
                 load(stream[i + 1])
                 if kind != "w2":
                     round_to_bf16(stream[i + 1])
+            quantize(entry)
+            if kind == "w2" and EARLY[e]:
+                w2_block(e, 0)
             if entry == HIDDEN_AT[0] or entry == HIDDEN_AT[1]:
                 hidden(HIDDEN_AT.index(entry))
-            quantize(entry)
             if kind == "x" and s > 0:
                 gather_words(s - 1)
             if entry == ("x", 0, last):
                 gather_scales()
                 gather_words(last)
-            if kind in up_weights:
+            if (kind, e, s - 1) in QPAIR:
+                multiply_up((kind, e, s - 1))
+            if kind in up_weights and entry not in QPAIR:
                 multiply_up(entry)
             if entry in GELU_HOST:
                 gelu(GELU_HOST.index(entry), entry)
             if kind == "w2":
-                for n in range(W2_PIECES[e]):
-                    w2_block(e, n, WIDTH // W2_PIECES[e])
+                for n in range(1 if EARLY[e] else 0, BLOCKS):
+                    w2_block(e, n)
             if entry in WAY_AT:
                 e2 = WAY_AT.index(entry)
                 for n in range(BLOCKS):

@@ -32,11 +32,11 @@ WINDOW = T + T // 2
 
 VECTOR_GROUPS = {
     ("x", 0): (8, 8, 8, 8,),
-    ("w1", 0): (0, 32, 0, 32,),
-    ("w3", 0): (16, 16, 32, 16,),
+    ("w1", 0): (0, 16, 0, 32,),
+    ("w3", 0): (12, 12, 32, 16,),
     ("w2", 0): (12,),
     ("w1", 1): (0, 0, 0, 32,),
-    ("w3", 1): (0, 16, 16, 16,),
+    ("w3", 1): (0, 12, 16, 16,),
     ("w2", 1): (0,),
 }
 STREAM = [("x", 0, s) for s in range(PASSES)] + [("w1", 0, s) for s in range(PASSES)] + [("w3", 0, s) for s in range(PASSES)] + [("w2", 0, 0)] + [("w1", 1, s) for s in range(PASSES)] + [("w3", 1, s) for s in range(PASSES)] + [("w2", 1, 0)]
@@ -61,6 +61,12 @@ QPAIR = []
 LAST_V3 = (True, True)
 W2_CUTS = ((0, 512), (0, 256, 512))
 EARLY = (False, False)
+W1_WIDE = False
+WARM = False
+W2_ROUND = ((0, 128, 256, 384, 512), (0, 128, 256, 384, 512))
+Y_IN_W2 = (False, False)
+PAIR_BUFS = 3
+OWN_PART = True
 
 
 def tile_routed_moe_kernel(tc, xT, w1, w3, w2, gate, offs, out):
@@ -75,12 +81,17 @@ def tile_routed_moe_kernel(tc, xT, w1, w3, w2, gate, offs, out):
     with ExitStack() as ctx:
         keep = ctx.enter_context(tc.tile_pool(name="keep", bufs=1))
         raw_pool = ctx.enter_context(tc.tile_pool(name="raw", bufs=RAW_BUFS))
-        pair_pool = ctx.enter_context(tc.tile_pool(name="pair", bufs=max(1, len(PAIRED))))
+        pair_pool = ctx.enter_context(tc.tile_pool(name="pair", bufs=PAIR_BUFS))
         code_pool = ctx.enter_context(tc.tile_pool(name="codes", bufs=8))
         rounded_pool = ctx.enter_context(tc.tile_pool(name="rounded", bufs=ROUNDED_BUFS))
         psum = ctx.enter_context(tc.psum_pool(name="psum", bufs=1))
 
         offsets = keep.tile([P, E * LIST_COLS], U16, name="offsets")
+
+        if WARM:
+            warm = keep.tile([P, 1], F32, name="warm")
+            nc.gpsimd.memset(warm[:], 0.0)
+            nc.scalar.activation(warm[:], warm[:], GELU)
 
         x_scales = keep.tile([P, WINDOW], U8, name="x_scales", align_bytes=64)
         nc.gpsimd.memset(x_scales[:, 0:T], 0)
@@ -121,8 +132,7 @@ def tile_routed_moe_kernel(tc, xT, w1, w3, w2, gate, offs, out):
                 flat = raw[:].rearrange("p j c -> p (j c)")
                 for c0, c1 in zip(W2_CUTS[e][:-1], W2_CUTS[e][1:]):
                     part = flat[:, PACK * c0 : PACK * c1].rearrange("p (j c) -> p j c", j=PACK)
-                    for n in range(c0 // P, c1 // P):
-                        w2_parts[e, n] = part[:, :, n * P - c0 : (n + 1) * P - c0]
+                    w2_parts[e, c0] = part
                     for r in range(RUN):
                         nc.sync.dma_start(part[r::RUN], rows[r][:, :, c0:c1])
                 if entry == last_down:
@@ -220,7 +230,20 @@ def tile_routed_moe_kernel(tc, xT, w1, w3, w2, gate, offs, out):
                     psum.tile([P, BANK], F32, name=f"{kind}_{e}_bank{u}", tag=f"{kind}_{e}_bank{u}") for u in range(2)
                 ]
             words, scales = codes[entry]
-            if True:
+            if kind == "w1" and W1_WIDE:
+                slots = slice(e * C, (e + 1) * C)
+                for t in range(BLOCKS):
+                    cols = slice(t * P, (t + 1) * P)
+                    nc.tensor.matmul_mx(
+                        sums[kind, e][t // 2][:, (t % 2) * C : (t % 2 + 1) * C],
+                        lhsT=words[:, cols].bitcast(FP8X4),
+                        lhsT_scale=scales[:, cols],
+                        rhs=slot_words[s][:, slots].bitcast(FP8X4),
+                        rhs_scale=slot_scales[0][4 * s : P, slots],
+                        start=(s == 0 and t % 2 == 0),
+                        stop=(s == last and t % 2 == 1),
+                    )
+            else:
                 for u in range(2):
                     slots = slice(e * C + u * HALF_C, e * C + (u + 1) * HALF_C)
                     for t in range(BLOCKS):
@@ -238,31 +261,52 @@ def tile_routed_moe_kernel(tc, xT, w1, w3, w2, gate, offs, out):
         def by_slot(bank):
             return bank[:].rearrange("p (t c i) -> p c t i", t=PACK, i=PRUN)
 
+        def by_slot2(bank):
+            return bank[:].rearrange("p (t a c i) -> p a c t i", t=PACK, a=2, i=PRUN)
+
         def interleaved(rows):
             return rows.rearrange("p (c i t) -> p c t i", t=PACK, i=PRUN)
 
         def gelu(e, host):
             gelus[e] = raws[host][:, 0:2, :]
+            if W1_WIDE or OWN_PART:
+                gelus[e] = raws[host][:, :, C:]
             for u in range(2):
-                nc.scalar.activation(
-                    interleaved(gelus[e][:, u, :]), by_slot(sums["w1", e][u]), GELU
-                )
+                if W1_WIDE:
+                    nc.scalar.activation(gelus[e][:, 2 * u : 2 * u + 2, :], sums["w1", e][u][:].rearrange("p (t c) -> p t c", t=2), GELU)
+                elif OWN_PART:
+                    nc.scalar.activation(gelu_of_half(e, u), by_slot2(sums["w1", e][u]), GELU)
+                else:
+                    nc.scalar.activation(interleaved(gelus[e][:, u, :]), by_slot(sums["w1", e][u]), GELU)
+
+        def gelu_of_half(e, u):
+            if W1_WIDE:
+                by_block = gelus[e][:, :, u * HALF_C : (u + 1) * HALF_C]
+                return by_block.rearrange("p t (c i) -> p c t i", i=PRUN)
+            if OWN_PART:
+                return gelus[e][:, 2 * u : 2 * u + 2, :].rearrange("p a (c t i) -> p a c t i", t=PACK, i=PRUN)
+            return interleaved(gelus[e][:, u, :])
 
         def hidden(e):
             h = [
                 keep.tile([P, BANK], BF16, name=f"h{e}_{u}", tag=f"first{e}" if u == 0 else f"second{e}", align_bytes=64)
-                for u in range(2)
+                for u in range(2 if SPLIT0[e] else 0)
             ]
+            if not SPLIT0[e]:
+                whole = keep.tile([P, 2 * BANK], BF16, name=f"h{e}", align_bytes=64)
+                h = [whole[:, 0:BANK], whole[:, BANK:]]
             for u in range(2):
                 nc.vector.tensor_tensor(
-                    interleaved(h[u][:]),
-                    by_slot(sums["w3", e][u]),
-                    interleaved(gelus[e][:, u, :]),
+                    h[u][:].rearrange("p (a c i t) -> p a c t i", a=2, t=PACK, i=PRUN) if OWN_PART else interleaved(h[u][:]),
+                    by_slot2(sums["w3", e][u]) if OWN_PART else by_slot(sums["w3", e][u]),
+                    gelu_of_half(e, u),
                     MULT,
                 )
             h_words = keep.tile([P, C], U32, name=f"h_words{e}", align_bytes=64)
             h_scales = keep.tile([P, C], U8, name=f"h_scales{e}", align_bytes=64)
-            for u in range(2):
+            if not SPLIT0[e]:
+                nc.vector.quantize_mx(h_words[:].bitcast(FP8X4), h_scales[:], whole[:])
+            for u in range(2 if SPLIT0[e] else 0):
                 cols = slice(u * HALF_C, (u + 1) * HALF_C)
                 nc.vector.quantize_mx(h_words[:, cols].bitcast(FP8X4), h_scales[:, cols], h[u][:])
             hidden_codes[e] = (h_words, h_scales)
@@ -288,23 +332,25 @@ def tile_routed_moe_kernel(tc, xT, w1, w3, w2, gate, offs, out):
         def down(e, n, c0, c1, tag):
             y = psum.tile([P, BANK], F32, name=tag, tag=tag)
             multiply_down(e, n, c0, c1, y[:, 0 : c1 - c0])
-            if (e, n) in Y_HOST:
-                y_sbuf = raws[Y_HOST[e, n]][:, 2 + n % 2, c0:c1]
+            if Y_IN_W2[e] and n < 2:
+                y_sbuf = w2_parts[e, W2_CUTS[e][-2]][:, 2 * n + c0 // HALF_C, 0 : c1 - c0]
+            elif (e, n) in Y_HOST:
+                y_sbuf = raws[Y_HOST[e, n]][:, n, C + c0 : C + c1]
             else:
                 y_sbuf = keep.tile([P, c1 - c0], F32, name=f"y{e}_{n}_{c0}")[:]
             nc.scalar.copy(y_sbuf, y[:, 0 : c1 - c0])
             scatter(e, n, c0, c1, y_sbuf)
 
-        def w2_block(e, n):
+        def w2_block(e, c0, c1):
             entry = ("w2", e, 0)
             words, scales = codes[entry]
-            cols = slice(n * P, (n + 1) * P)
-            if n == 0 and EARLY[e]:
+            cols = slice(c0, c1)
+            if c0 == 0 and EARLY[e]:
                 part = keep.tile([P, BANK], BF16, name=f"w2_first{e}", tag=f"first{e}", align_bytes=64)[:]
             else:
-                part = rounded[entry][:, n * BANK : (n + 1) * BANK]
-            copy = nc.scalar.copy if n >= W2V[e] else nc.vector.tensor_copy
-            interleave(copy, part, w2_parts[e, n], 0, P)
+                part = rounded[entry][:, c0 * PACK : c1 * PACK]
+            start = max(c for c in W2_CUTS[e] if c <= c0)
+            interleave(nc.scalar.copy, part, w2_parts[e, start][:, :, c0 - start : c1 - start], 0, c1 - c0)
             nc.vector.quantize_mx(words[:, cols].bitcast(FP8X4), scales[:, cols], part)
 
         def way_back(e, n):
@@ -332,7 +378,7 @@ def tile_routed_moe_kernel(tc, xT, w1, w3, w2, gate, offs, out):
                     round_to_bf16(stream[i + 1])
             quantize(entry)
             if kind == "w2" and EARLY[e]:
-                w2_block(e, 0)
+                w2_block(e, 0, P)
             if entry == HIDDEN_AT[0] or entry == HIDDEN_AT[1]:
                 hidden(HIDDEN_AT.index(entry))
             if kind == "x" and s > 0:
@@ -347,8 +393,9 @@ def tile_routed_moe_kernel(tc, xT, w1, w3, w2, gate, offs, out):
             if entry in GELU_HOST:
                 gelu(GELU_HOST.index(entry), entry)
             if kind == "w2":
-                for n in range(1 if EARLY[e] else 0, BLOCKS):
-                    w2_block(e, n)
+                for c0, c1 in zip(W2_ROUND[e][:-1], W2_ROUND[e][1:]):
+                    if c0 > 0 or not EARLY[e]:
+                        w2_block(e, c0, c1)
             if entry in WAY_AT:
                 e2 = WAY_AT.index(entry)
                 for n in range(BLOCKS):

@@ -61,12 +61,16 @@ QPAIR = []
 LAST_V3 = (True, True)
 W2_CUTS = ((0, 512), (0, 256, 512))
 EARLY = (False, False)
-W1_WIDE = False
+W1_WIDE = True
 WARM = False
 W2_ROUND = ((0, 128, 256, 384, 512), (0, 128, 256, 384, 512))
 Y_IN_W2 = (False, False)
 PAIR_BUFS = 3
 OWN_PART = True
+WINDOW_HOST = {}
+T_SPLIT = []
+W3_WIDE = True
+WIDE_ORDER = [(0, 0), (0, 1), (1, 0), (1, 1)]
 
 
 def tile_routed_moe_kernel(tc, xT, w1, w3, w2, gate, offs, out):
@@ -96,10 +100,10 @@ def tile_routed_moe_kernel(tc, xT, w1, w3, w2, gate, offs, out):
         x_scales = keep.tile([P, WINDOW], U8, name="x_scales", align_bytes=64)
         nc.gpsimd.memset(x_scales[:, 0:T], 0)
 
-        windows = [keep.tile([P, T], F32, name=f"window{n}") for n in range(BLOCKS)]
+        windows = {n: keep.tile([P, T], F32, name=f"window{n}") for n in range(BLOCKS) if n not in WINDOW_HOST.values()}
 
         raws, rounded, codes = {}, {}, {}
-        w2_parts, joined = {}, {}
+        w2_parts, joined, held = {}, {}, {}
         gates, slot_words, slot_scales = {}, {}, {}
         sums, gelus, hidden_rounded, hidden_codes = {}, {}, {}, {}
 
@@ -162,6 +166,8 @@ def tile_routed_moe_kernel(tc, xT, w1, w3, w2, gate, offs, out):
                 joined[entry] = both
                 rounded[entry] = both[:, 0 : PACK * WIDTH]
                 rounded[kind, e, s + 1] = both[:, PACK * WIDTH :]
+            elif entry in WINDOW_HOST:
+                rounded[entry] = keep.tile([P, PACK * WIDTH], BF16, name="dst", tag=f"window{WINDOW_HOST[entry]}", align_bytes=64)
             elif entry not in rounded:
                 rounded[entry] = rounded_pool.tile([P, PACK * WIDTH], BF16, name="dst", align_bytes=64)
             dst = rounded[entry]
@@ -173,6 +179,10 @@ def tile_routed_moe_kernel(tc, xT, w1, w3, w2, gate, offs, out):
                     interleave_permuted(nc.scalar.copy, dst, raw, slice(2, 3), slice(0, GROUPS))
                 else:
                     interleave_permuted(nc.scalar.copy, dst, raw, slice(2, 4), slice(0, GROUPS))
+            elif entry in T_SPLIT:
+                interleave_permuted(nc.vector.tensor_copy, dst, raw, slice(0, 2), slice(0, GROUPS))
+                second = nc.vector.tensor_copy if on_vector == GROUPS else nc.scalar.copy
+                interleave_permuted(second, dst, raw, slice(2, 4), slice(0, GROUPS))
             elif kind in up_weights:
                 if on_vector > 0:
                     interleave_permuted(nc.vector.tensor_copy, dst, raw, slice(0, 4), slice(0, on_vector))
@@ -209,7 +219,12 @@ def tile_routed_moe_kernel(tc, xT, w1, w3, w2, gate, offs, out):
             cuts = [i * WIDTH // pieces for i in range(pieces + 1)] if pieces else []
             if pieces == 2 and LAST_V3[e]:
                 cuts = [0, 2 * P, 3 * P, 4 * P]
-            for c0, c1 in zip(cuts[:-1], cuts[1:]):
+            spans = list(zip(cuts[:-1], cuts[1:]))
+            if entry in T_SPLIT:
+                spans = [(0, HALF), (HALF, WIDTH)]
+                if VECTOR_GROUPS[kind, e][s] < GROUPS:
+                    spans = spans[::-1]
+            for c0, c1 in spans:
                 nc.vector.quantize_mx(words[:, c0:c1].bitcast(FP8X4), scales[:, c0:c1], src[:, PACK * c0 : PACK * c1])
             codes[entry] = (words, scales)
 
@@ -230,7 +245,7 @@ def tile_routed_moe_kernel(tc, xT, w1, w3, w2, gate, offs, out):
                     psum.tile([P, BANK], F32, name=f"{kind}_{e}_bank{u}", tag=f"{kind}_{e}_bank{u}") for u in range(2)
                 ]
             words, scales = codes[entry]
-            if kind == "w1" and W1_WIDE:
+            if (kind == "w1" and W1_WIDE) or W3_WIDE:
                 slots = slice(e * C, (e + 1) * C)
                 for t in range(BLOCKS):
                     cols = slice(t * P, (t + 1) * P)
@@ -273,16 +288,17 @@ def tile_routed_moe_kernel(tc, xT, w1, w3, w2, gate, offs, out):
                 gelus[e] = raws[host][:, :, C:]
             for u in range(2):
                 if W1_WIDE:
-                    nc.scalar.activation(gelus[e][:, 2 * u : 2 * u + 2, :], sums["w1", e][u][:].rearrange("p (t c) -> p t c", t=2), GELU)
+                    nc.scalar.activation(
+                        gelus[e].rearrange("p a (c t i) -> p a c t i", t=PACK, i=PRUN)[:, :, :, 2 * u : 2 * u + 2, :],
+                        sums["w1", e][u][:].rearrange("p (t a c i) -> p a c t i", t=2, a=PACK, i=PRUN),
+                        GELU,
+                    )
                 elif OWN_PART:
                     nc.scalar.activation(gelu_of_half(e, u), by_slot2(sums["w1", e][u]), GELU)
                 else:
                     nc.scalar.activation(interleaved(gelus[e][:, u, :]), by_slot(sums["w1", e][u]), GELU)
 
         def gelu_of_half(e, u):
-            if W1_WIDE:
-                by_block = gelus[e][:, :, u * HALF_C : (u + 1) * HALF_C]
-                return by_block.rearrange("p t (c i) -> p c t i", i=PRUN)
             if OWN_PART:
                 return gelus[e][:, 2 * u : 2 * u + 2, :].rearrange("p a (c t i) -> p a c t i", t=PACK, i=PRUN)
             return interleaved(gelus[e][:, u, :])
@@ -295,7 +311,15 @@ def tile_routed_moe_kernel(tc, xT, w1, w3, w2, gate, offs, out):
             if not SPLIT0[e]:
                 whole = keep.tile([P, 2 * BANK], BF16, name=f"h{e}", align_bytes=64)
                 h = [whole[:, 0:BANK], whole[:, BANK:]]
-            for u in range(2):
+            for b, u in WIDE_ORDER if W3_WIDE else []:
+                ts = slice(2 * b, 2 * b + 2)
+                nc.vector.tensor_tensor(
+                    h[u][:].rearrange("p (a c i t) -> p a c t i", a=2, t=PACK, i=PRUN)[:, :, :, ts, :],
+                    sums["w3", e][b][:].rearrange("p (t a c i) -> p a c t i", t=2, a=PACK, i=PRUN)[:, 2 * u : 2 * u + 2],
+                    gelu_of_half(e, u)[:, :, :, ts, :],
+                    MULT,
+                )
+            for u in range(0 if W3_WIDE else 2):
                 nc.vector.tensor_tensor(
                     h[u][:].rearrange("p (a c i t) -> p a c t i", a=2, t=PACK, i=PRUN) if OWN_PART else interleaved(h[u][:]),
                     by_slot2(sums["w3", e][u]) if OWN_PART else by_slot(sums["w3", e][u]),
@@ -326,6 +350,12 @@ def tile_routed_moe_kernel(tc, xT, w1, w3, w2, gate, offs, out):
             )
 
         def scatter(e, n, c0, c1, y_sbuf):
+            if e == 0 and n in WINDOW_HOST.values():
+                held[n] = y_sbuf
+                return
+            scatter_now(e, n, c0, c1, y_sbuf)
+
+        def scatter_now(e, n, c0, c1, y_sbuf):
             entries = offsets[:, (e * C + c0) // 16 : (e * C + c1) // 16]
             nc.vector.tensor_tensor(windows[n][:].indirect(entries), y_sbuf, gates[e][:, n, c0:c1], MULT)
 
@@ -407,3 +437,7 @@ def tile_routed_moe_kernel(tc, xT, w1, w3, w2, gate, offs, out):
             for (e2, n), host in Y_HOST.items():
                 if host == entry and kind != "w2":
                     way_back(e2, n)
+            if entry in WINDOW_HOST:
+                n = WINDOW_HOST[entry]
+                windows[n] = keep.tile([P, T], F32, name=f"window{n}", tag=f"window{n}", align_bytes=64)
+                scatter_now(0, n, 0, C, held[n])

@@ -18,329 +18,231 @@ P = 128
 PACK = 4
 K_PASS = P * PACK
 PASSES = K // K_PASS
+LAST = PASSES - 1
 WIDTH = 512
 BLOCKS = WIDTH // P
 BANK = 512
-LIST_COLS = C // 16
-HALF = WIDTH // 2
-
 SLOTS = E * C
-GROUP = 16
-GROUPS = WIDTH // GROUP
 HALF_C = C // 2
+QUARTERS = 4
+LIST_ROWS = 16
+PAIR = 2
 WINDOW = T + T // 2
 
-VECTOR_GROUPS = {
-    ("x", 0): (8, 8, 8, 8,),
-    ("w1", 0): (0, 16, 0, 32,),
-    ("w3", 0): (12, 12, 32, 16,),
-    ("w2", 0): (12,),
-    ("w1", 1): (0, 0, 0, 32,),
-    ("w3", 1): (0, 12, 16, 16,),
-    ("w2", 1): (0,),
-}
-STREAM = [("x", 0, s) for s in range(PASSES)] + [("w1", 0, s) for s in range(PASSES)] + [("w3", 0, s) for s in range(PASSES)] + [("w2", 0, 0)] + [("w1", 1, s) for s in range(PASSES)] + [("w3", 1, s) for s in range(PASSES)] + [("w2", 1, 0)]
-GATE_BEFORE = [("w1", 1, 0), None]
-RAW_BUFS = 9
-ROUNDED_BUFS = 7
-GELU_HOST = [("w3", 0, 1), ("w3", 1, 2)]
-W2V = (0, 0)
-SPLIT0 = (True, True)
-LAST_BY_T = True
-W2_LOADS = (1, 2)
-Y_HOST = {(0, 2): ("w1", 1, 0), (0, 3): ("w1", 1, 1)}
-RUN = 2
-GATE_LOADS = (1, 2)
-W2_PIECES = (4, 4)
-HIDDEN_AT = [("w2", 0, 0), ("w2", 1, 0)]
-WAY_AT = [("w2", 0, 0), ("w2", 1, 0)]
-PRUN = 2
-OFFS_LATE = True
-PAIRED = [("x", 0, 2), ("w1", 0, 0), ("w1", 0, 2)]
-QPAIR = []
-LAST_V3 = (True, True)
-W2_CUTS = ((0, 512), (0, 256, 512))
-EARLY = (False, False)
-W1_WIDE = True
-WARM = False
-W2_ROUND = ((0, 128, 256, 384, 512), (0, 128, 256, 384, 512))
-Y_IN_W2 = (False, False)
-PAIR_BUFS = 3
-OWN_PART = True
-WINDOW_HOST = {}
-T_SPLIT = []
-W3_WIDE = True
-WIDE_ORDER = [(0, 0), (0, 1), (1, 0), (1, 1)]
+STREAM = [("x", 0, s) for s in range(PASSES)] + [
+    (kind, e, s) for e in range(E) for kind, passes in (("w1", PASSES), ("w3", PASSES), ("w2", 1)) for s in range(passes)
+]
+
+LOADED_WITH_NEXT = [("x", 0, 2), ("w1", 0, 0), ("w1", 0, 2)]
+GELU_BEHIND = (1, 2)
+SHARED = 3 * WIDTH // 8
+
+
+def columns_on_vector(kind, e, s):
+    if kind == "x":
+        return WIDTH // 4
+    if kind == "w1" and s == LAST:
+        return WIDTH
+    if kind == "w1" and e == 0:
+        return WIDTH // 2 if s == 1 else 0
+    if kind == "w1" or (e, s) == (1, 0):
+        return 0
+    if s == GELU_BEHIND[e] + 1:
+        return WIDTH
+    if s == LAST - 1:
+        return WIDTH // 2
+    return SHARED
 
 
 def tile_routed_moe_kernel(tc, xT, w1, w3, w2, gate, offs, out):
     nc = tc.nc
-    up_weights = {"w1": w1, "w3": w3}
-
-    stream = STREAM
-    last = PASSES - 1
-    last_up = ("w3", E - 1, last)
-    last_down = ("w2", E - 1, 0)
+    along_k = {("x", 0): xT, ("w1", 0): w1[0], ("w1", 1): w1[1], ("w3", 0): w3[0], ("w3", 1): w3[1]}
 
     with ExitStack() as ctx:
         keep = ctx.enter_context(tc.tile_pool(name="keep", bufs=1))
-        raw_pool = ctx.enter_context(tc.tile_pool(name="raw", bufs=RAW_BUFS))
-        pair_pool = ctx.enter_context(tc.tile_pool(name="pair", bufs=PAIR_BUFS))
-        code_pool = ctx.enter_context(tc.tile_pool(name="codes", bufs=8))
-        rounded_pool = ctx.enter_context(tc.tile_pool(name="rounded", bufs=ROUNDED_BUFS))
+        raw_pool = ctx.enter_context(tc.tile_pool(name="raw", bufs=9))
+        pair_pool = ctx.enter_context(tc.tile_pool(name="pair", bufs=len(LOADED_WITH_NEXT)))
+        code_pool = ctx.enter_context(tc.tile_pool(name="codes", bufs=2 * PASSES))
+        rounded_pool = ctx.enter_context(tc.tile_pool(name="rounded", bufs=7))
         psum = ctx.enter_context(tc.psum_pool(name="psum", bufs=1))
 
-        offsets = keep.tile([P, E * LIST_COLS], U16, name="offsets")
-
-        if WARM:
-            warm = keep.tile([P, 1], F32, name="warm")
-            nc.gpsimd.memset(warm[:], 0.0)
-            nc.scalar.activation(warm[:], warm[:], GELU)
+        offsets = keep.tile([P, SLOTS // LIST_ROWS], U16, name="offsets")
 
         x_scales = keep.tile([P, WINDOW], U8, name="x_scales", align_bytes=64)
         nc.gpsimd.memset(x_scales[:, 0:T], 0)
 
-        windows = {n: keep.tile([P, T], F32, name=f"window{n}") for n in range(BLOCKS) if n not in WINDOW_HOST.values()}
+        windows = [keep.tile([P, T], F32, name=f"window{n}") for n in range(BLOCKS)]
 
         raws, rounded, codes = {}, {}, {}
-        w2_parts, joined, held = {}, {}, {}
-        gates, slot_words, slot_scales = {}, {}, {}
-        sums, gelus, hidden_rounded, hidden_codes = {}, {}, {}, {}
+        w2_raw, gates, sums, hidden_codes, slot_words, slot_scales = {}, {}, {}, {}, {}, []
 
-        def load_gate(e):
-            gt = keep.tile([P, BLOCKS, C], F32, name=f"gate{e}")
+        def load_gate(e, pieces):
+            tile = keep.tile([P, BLOCKS, C], F32, name=f"gate{e}")
             rows = gate[:, e * C : (e + 1) * C].rearrange("(n p) c -> p n c", p=P)
-            for n0 in range(0, BLOCKS, BLOCKS // GATE_LOADS[e]):
-                n1 = n0 + BLOCKS // GATE_LOADS[e]
-                nc.sync.dma_start(gt[:, n0:n1], rows[:, n0:n1])
-            gates[e] = gt
+            for n0 in range(0, BLOCKS, BLOCKS // pieces):
+                nc.sync.dma_start(tile[:, n0 : n0 + BLOCKS // pieces], rows[:, n0 : n0 + BLOCKS // pieces])
+            gates[e] = tile
+
+        def load_w2(e, raw, pieces):
+            rows = w2[e].rearrange("(m t r) n -> r m t n", t=PACK, r=PAIR)
+            flat = raw[:].rearrange("p t c -> p (t c)")
+            width = WIDTH // pieces
+            for c0 in range(0, WIDTH, width):
+                part = flat[:, PACK * c0 : PACK * (c0 + width)].rearrange("p (t c) -> p t c", t=PACK)
+                for n in range(c0 // P, (c0 + width) // P):
+                    w2_raw[e, n] = part[:, :, n * P - c0 : (n + 1) * P - c0]
+                for r in range(PAIR):
+                    nc.sync.dma_start(part[r::PAIR], rows[r][:, :, c0 : c0 + width])
 
         def load(entry):
             kind, e, s = entry
-            if entry == GATE_BEFORE[0] or entry == GATE_BEFORE[1]:
-                load_gate(GATE_BEFORE.index(entry))
+            if entry == ("w1", 1, 0):
+                load_gate(0, 1)
             if entry in raws:
                 return
-            if entry in PAIRED:
+            if entry in LOADED_WITH_NEXT:
                 pair = pair_pool.tile([P, 2, PACK, WIDTH], F32, name="pair")
-                source = xT if kind == "x" else up_weights[kind][e]
-                rows = source[s * K_PASS : (s + 2) * K_PASS, :].rearrange("(g p j) c -> p g (j c)", g=2, j=PACK)
-                nc.sync.dma_start(pair[:].rearrange("p g j c -> p g (j c)"), rows)
-                raws[entry] = pair[:, 0]
-                raws[kind, e, s + 1] = pair[:, 1]
+                rows = along_k[kind, e][s * K_PASS : (s + 2) * K_PASS, :]
+                nc.sync.dma_start(
+                    pair[:].rearrange("p g j c -> p g (j c)"), rows.rearrange("(g p j) c -> p g (j c)", g=2, j=PACK)
+                )
+                raws[entry], raws[kind, e, s + 1] = pair[:, 0], pair[:, 1]
                 return
             raw = raw_pool.tile([P, PACK, WIDTH], F32, name="raw")
             raws[entry] = raw
             if kind == "w2":
-                rows = w2[e].rearrange("(q t r) n -> r q t n", t=4, r=RUN)
-                flat = raw[:].rearrange("p j c -> p (j c)")
-                for c0, c1 in zip(W2_CUTS[e][:-1], W2_CUTS[e][1:]):
-                    part = flat[:, PACK * c0 : PACK * c1].rearrange("p (j c) -> p j c", j=PACK)
-                    w2_parts[e, c0] = part
-                    for r in range(RUN):
-                        nc.sync.dma_start(part[r::RUN], rows[r][:, :, c0:c1])
-                if entry == last_down:
-                    load_gate(e)
-                return
-            source = xT if kind == "x" else up_weights[kind][e]
-            nc.sync.dma_start(raw[:], source[s * K_PASS : (s + 1) * K_PASS, :].rearrange("(p j) c -> p j c", j=PACK))
+                load_w2(e, raw, 2 if e == E - 1 else 1)
+                if e == E - 1:
+                    load_gate(e, 2)
+            else:
+                rows = along_k[kind, e][s * K_PASS : (s + 1) * K_PASS, :]
+                nc.sync.dma_start(raw[:], rows.rearrange("(p j) c -> p j c", j=PACK))
 
         def interleave(copy, dst, src, c0, c1):
             copy(
-                dst[:].rearrange("p (c i j) -> p c j i", i=RUN, j=PACK)[:, c0 // RUN : c1 // RUN],
-                src[:].rearrange("p j (c i) -> p c j i", i=RUN)[:, c0 // RUN : c1 // RUN],
+                dst[:].rearrange("p (c i j) -> p c j i", i=PAIR, j=PACK)[:, c0 // PAIR : c1 // PAIR],
+                src[:].rearrange("p j (c i) -> p c j i", i=PAIR)[:, c0 // PAIR : c1 // PAIR],
             )
 
-        def interleave_permuted(copy, dst, src, ts, qs):
-            qs = slice(qs.start * 4 // RUN, qs.stop * 4 // RUN)
+        def interleave_permuted(copy, dst, src, blocks, c0, c1):
+            ms = slice(c0 // (PACK * PAIR), c1 // (PACK * PAIR))
             copy(
-                dst[:].rearrange("p (t q r j) -> p t q j r", t=4, r=RUN, j=PACK)[:, ts, qs],
-                src[:].rearrange("p j (q t r) -> p t q j r", t=4, r=RUN)[:, ts, qs],
+                dst[:].rearrange("p (t m r j) -> p t m j r", t=BLOCKS, r=PAIR, j=PACK)[:, blocks, ms],
+                src[:].rearrange("p j (m t r) -> p t m j r", t=BLOCKS, r=PAIR)[:, blocks, ms],
             )
 
         def round_to_bf16(entry):
             kind, e, s = entry
             raw = raws[entry]
-            if entry in QPAIR:
-                both = keep.tile([P, 2 * PACK * WIDTH], BF16, name=f"both_{kind}{e}_{s}", align_bytes=64)
-                joined[entry] = both
-                rounded[entry] = both[:, 0 : PACK * WIDTH]
-                rounded[kind, e, s + 1] = both[:, PACK * WIDTH :]
-            elif entry in WINDOW_HOST:
-                rounded[entry] = keep.tile([P, PACK * WIDTH], BF16, name="dst", tag=f"window{WINDOW_HOST[entry]}", align_bytes=64)
-            elif entry not in rounded:
-                rounded[entry] = rounded_pool.tile([P, PACK * WIDTH], BF16, name="dst", align_bytes=64)
-            dst = rounded[entry]
-            on_vector = VECTOR_GROUPS[kind, e][s]
-            if kind == "w3" and s == last and LAST_BY_T:
-                interleave_permuted(nc.vector.tensor_copy, dst, raw, slice(0, 2), slice(0, GROUPS))
-                if LAST_V3[e]:
-                    interleave_permuted(nc.vector.tensor_copy, dst, raw, slice(3, 4), slice(0, GROUPS))
-                    interleave_permuted(nc.scalar.copy, dst, raw, slice(2, 3), slice(0, GROUPS))
-                else:
-                    interleave_permuted(nc.scalar.copy, dst, raw, slice(2, 4), slice(0, GROUPS))
-            elif entry in T_SPLIT:
-                interleave_permuted(nc.vector.tensor_copy, dst, raw, slice(0, 2), slice(0, GROUPS))
-                second = nc.vector.tensor_copy if on_vector == GROUPS else nc.scalar.copy
-                interleave_permuted(second, dst, raw, slice(2, 4), slice(0, GROUPS))
-            elif kind in up_weights:
-                if on_vector > 0:
-                    interleave_permuted(nc.vector.tensor_copy, dst, raw, slice(0, 4), slice(0, on_vector))
-                if on_vector < GROUPS:
-                    interleave_permuted(nc.scalar.copy, dst, raw, slice(0, 4), slice(on_vector, GROUPS))
-            elif kind == "w2":
-                pass
-            else:
-                if on_vector > 0:
-                    interleave(nc.vector.tensor_copy, dst, raw, 0, on_vector * GROUP)
-                if on_vector < GROUPS:
-                    interleave(nc.scalar.copy, dst, raw, on_vector * GROUP, WIDTH)
+            dst = rounded_pool.tile([P, PACK * WIDTH], BF16, name="dst", align_bytes=64)
+            rounded[entry] = dst
+            if kind == "w2":
+                return
+            if (kind, s) == ("w3", LAST):
+                interleave_permuted(nc.vector.tensor_copy, dst, raw, slice(0, 2), 0, WIDTH)
+                interleave_permuted(nc.vector.tensor_copy, dst, raw, slice(3, 4), 0, WIDTH)
+                interleave_permuted(nc.scalar.copy, dst, raw, slice(2, 3), 0, WIDTH)
+                return
+            cut = columns_on_vector(kind, e, s)
+            for copy, c0, c1 in ((nc.vector.tensor_copy, 0, cut), (nc.scalar.copy, cut, WIDTH)):
+                if c1 > c0 and kind == "x":
+                    interleave(copy, dst, raw, c0, c1)
+                elif c1 > c0:
+                    interleave_permuted(copy, dst, raw, slice(0, BLOCKS), c0, c1)
+
+        def quantize_columns(words, scales, src, c0, c1):
+            nc.vector.quantize_mx(words[:, c0:c1].bitcast(FP8X4), scales[:, c0:c1], src[:, PACK * c0 : PACK * c1])
 
         def quantize(entry):
             kind, e, s = entry
-            src = rounded[entry]
             if kind == "x":
                 words = keep.tile([P, WINDOW], U32, name=f"x_words{s}", align_bytes=64)
-                nc.vector.quantize_mx(words[:, 0:T].bitcast(FP8X4), x_scales[4 * s : P, 0:T], src[:])
+                quantize_columns(words, x_scales[4 * s : P], rounded[entry], 0, T)
                 codes[entry] = (words, x_scales)
                 return
-            if entry in QPAIR:
-                return
-            if (kind, e, s - 1) in QPAIR:
-                words = keep.tile([P, 2 * WIDTH], U32, name=f"{kind}_words{e}_{s}", align_bytes=64)
-                scales = keep.tile([P, 2 * WIDTH], U8, name=f"{kind}_scales{e}_{s}", align_bytes=64)
-                nc.vector.quantize_mx(words[:].bitcast(FP8X4), scales[:], joined[kind, e, s - 1][:])
-                codes[kind, e, s - 1] = (words[:, 0:WIDTH], scales[:, 0:WIDTH])
-                codes[entry] = (words[:, WIDTH:], scales[:, WIDTH:])
-                return
-            words = code_pool.tile([P, WIDTH], U32, name=f"{kind}_words{e}_{s}", tag="words", align_bytes=64)
-            scales = code_pool.tile([P, WIDTH], U8, name=f"{kind}_scales{e}_{s}", tag="scales", align_bytes=64)
-            pieces = 2 if (kind, s) == ("w3", last) else 0 if kind == "w2" else 1
-            cuts = [i * WIDTH // pieces for i in range(pieces + 1)] if pieces else []
-            if pieces == 2 and LAST_V3[e]:
-                cuts = [0, 2 * P, 3 * P, 4 * P]
-            spans = list(zip(cuts[:-1], cuts[1:]))
-            if entry in T_SPLIT:
-                spans = [(0, HALF), (HALF, WIDTH)]
-                if VECTOR_GROUPS[kind, e][s] < GROUPS:
-                    spans = spans[::-1]
-            for c0, c1 in spans:
-                nc.vector.quantize_mx(words[:, c0:c1].bitcast(FP8X4), scales[:, c0:c1], src[:, PACK * c0 : PACK * c1])
+            words = code_pool.tile([P, WIDTH], U32, name="words", align_bytes=64)
+            scales = code_pool.tile([P, WIDTH], U8, name="scales", align_bytes=64)
             codes[entry] = (words, scales)
+            if kind == "w2":
+                return
+            cuts = (0, 2 * P, 3 * P, WIDTH) if (kind, s) == ("w3", LAST) else (0, WIDTH)
+            for c0, c1 in zip(cuts[:-1], cuts[1:]):
+                quantize_columns(words, scales, rounded[entry], c0, c1)
+
+        def w2_block(e, n):
+            entry = ("w2", e, 0)
+            interleave(nc.scalar.copy, rounded[entry][:, n * PACK * P : (n + 1) * PACK * P], w2_raw[e, n], 0, P)
+            quantize_columns(*codes[entry], rounded[entry], n * P, (n + 1) * P)
 
         def gather_words(s):
-            words_of_slots = keep.tile([P, SLOTS], U32, name=f"slot_words{s}", align_bytes=64)
-            nc.vector.tensor_copy(words_of_slots[:], codes["x", 0, s][0][:].indirect(offsets[:]))
-            slot_words[s] = words_of_slots
+            slot_words[s] = keep.tile([P, SLOTS], U32, name=f"slot_words{s}", align_bytes=64)
+            nc.vector.tensor_copy(slot_words[s][:], codes["x", 0, s][0][:].indirect(offsets[:]))
 
         def gather_scales():
-            bytes_of_slots = keep.tile([P, SLOTS], U8, name="slot_scales", align_bytes=64)
-            nc.vector.tensor_copy(bytes_of_slots[:], x_scales[:].indirect(offsets[:]))
-            slot_scales[0] = bytes_of_slots
+            slot_scales.append(keep.tile([P, SLOTS], U8, name="slot_scales", align_bytes=64))
+            nc.vector.tensor_copy(slot_scales[0][:], x_scales[:].indirect(offsets[:]))
+
+        def bank(tag):
+            return psum.tile([P, BANK], F32, name=tag, tag=tag)
 
         def multiply_up(entry):
             kind, e, s = entry
             if s == 0:
-                sums[kind, e] = [
-                    psum.tile([P, BANK], F32, name=f"{kind}_{e}_bank{u}", tag=f"{kind}_{e}_bank{u}") for u in range(2)
-                ]
+                sums[kind, e] = [bank(f"{kind}_{e}_bank{b}") for b in range(2)]
             words, scales = codes[entry]
-            if (kind == "w1" and W1_WIDE) or W3_WIDE:
-                slots = slice(e * C, (e + 1) * C)
-                for t in range(BLOCKS):
-                    cols = slice(t * P, (t + 1) * P)
-                    nc.tensor.matmul_mx(
-                        sums[kind, e][t // 2][:, (t % 2) * C : (t % 2 + 1) * C],
-                        lhsT=words[:, cols].bitcast(FP8X4),
-                        lhsT_scale=scales[:, cols],
-                        rhs=slot_words[s][:, slots].bitcast(FP8X4),
-                        rhs_scale=slot_scales[0][4 * s : P, slots],
-                        start=(s == 0 and t % 2 == 0),
-                        stop=(s == last and t % 2 == 1),
-                    )
-            else:
-                for u in range(2):
-                    slots = slice(e * C + u * HALF_C, e * C + (u + 1) * HALF_C)
-                    for t in range(BLOCKS):
-                        cols = slice(t * P, (t + 1) * P)
-                        nc.tensor.matmul_mx(
-                            sums[kind, e][u][:, t * HALF_C : (t + 1) * HALF_C],
-                            lhsT=words[:, cols].bitcast(FP8X4),
-                            lhsT_scale=scales[:, cols],
-                            rhs=slot_words[s][:, slots].bitcast(FP8X4),
-                            rhs_scale=slot_scales[0][4 * s : P, slots],
-                            start=(s == 0 and t == 0),
-                            stop=(s == last and t == BLOCKS - 1),
-                        )
+            slots = slice(e * C, (e + 1) * C)
+            for t in range(BLOCKS):
+                cols = slice(t * P, (t + 1) * P)
+                nc.tensor.matmul_mx(
+                    sums[kind, e][t // 2][:, (t % 2) * C : (t % 2 + 1) * C],
+                    lhsT=words[:, cols].bitcast(FP8X4),
+                    lhsT_scale=scales[:, cols],
+                    rhs=slot_words[s][:, slots].bitcast(FP8X4),
+                    rhs_scale=slot_scales[0][4 * s : P, slots],
+                    start=(s == 0 and t % 2 == 0),
+                    stop=(s == LAST and t % 2 == 1),
+                )
 
-        def by_slot(bank):
-            return bank[:].rearrange("p (t c i) -> p c t i", t=PACK, i=PRUN)
+        def of_bank(sums_of_bank):
+            return sums_of_bank[:].rearrange("p (t a c i) -> p a c t i", t=2, a=QUARTERS, i=PAIR)
 
-        def by_slot2(bank):
-            return bank[:].rearrange("p (t a c i) -> p a c t i", t=PACK, a=2, i=PRUN)
+        def of_gelus(e, b):
+            rows = raws["w3", e, GELU_BEHIND[e]][:, :, C:]
+            return rows.rearrange("p a (c t i) -> p a c t i", t=BLOCKS, i=PAIR)[:, :, :, 2 * b : 2 * b + 2, :]
 
-        def interleaved(rows):
-            return rows.rearrange("p (c i t) -> p c t i", t=PACK, i=PRUN)
-
-        def gelu(e, host):
-            gelus[e] = raws[host][:, 0:2, :]
-            if W1_WIDE or OWN_PART:
-                gelus[e] = raws[host][:, :, C:]
-            for u in range(2):
-                if W1_WIDE:
-                    nc.scalar.activation(
-                        gelus[e].rearrange("p a (c t i) -> p a c t i", t=PACK, i=PRUN)[:, :, :, 2 * u : 2 * u + 2, :],
-                        sums["w1", e][u][:].rearrange("p (t a c i) -> p a c t i", t=2, a=PACK, i=PRUN),
-                        GELU,
-                    )
-                elif OWN_PART:
-                    nc.scalar.activation(gelu_of_half(e, u), by_slot2(sums["w1", e][u]), GELU)
-                else:
-                    nc.scalar.activation(interleaved(gelus[e][:, u, :]), by_slot(sums["w1", e][u]), GELU)
-
-        def gelu_of_half(e, u):
-            if OWN_PART:
-                return gelus[e][:, 2 * u : 2 * u + 2, :].rearrange("p a (c t i) -> p a c t i", t=PACK, i=PRUN)
-            return interleaved(gelus[e][:, u, :])
+        def gelu(e):
+            for b in range(2):
+                nc.scalar.activation(of_gelus(e, b), of_bank(sums["w1", e][b]), GELU)
 
         def hidden(e):
-            h = [
-                keep.tile([P, BANK], BF16, name=f"h{e}_{u}", tag=f"first{e}" if u == 0 else f"second{e}", align_bytes=64)
-                for u in range(2 if SPLIT0[e] else 0)
-            ]
-            if not SPLIT0[e]:
-                whole = keep.tile([P, 2 * BANK], BF16, name=f"h{e}", align_bytes=64)
-                h = [whole[:, 0:BANK], whole[:, BANK:]]
-            for b, u in WIDE_ORDER if W3_WIDE else []:
-                ts = slice(2 * b, 2 * b + 2)
+            h = [keep.tile([P, PACK * HALF_C], BF16, name=f"h{e}_{u}", align_bytes=64) for u in range(2)]
+            halves = keep.tile([P, 2, 2 * C], BF16, name=f"halves{e}", align_bytes=64)
+            for b, a0, a1 in ((0, 0, QUARTERS), (1, 0, QUARTERS // 2), (1, QUARTERS // 2, QUARTERS)):
                 nc.vector.tensor_tensor(
-                    h[u][:].rearrange("p (a c i t) -> p a c t i", a=2, t=PACK, i=PRUN)[:, :, :, ts, :],
-                    sums["w3", e][b][:].rearrange("p (t a c i) -> p a c t i", t=2, a=PACK, i=PRUN)[:, 2 * u : 2 * u + 2],
-                    gelu_of_half(e, u)[:, :, :, ts, :],
+                    halves[:, b, :].rearrange("p (a c i t) -> p a c t i", a=QUARTERS, t=2, i=PAIR)[:, a0:a1],
+                    of_bank(sums["w3", e][b])[:, a0:a1],
+                    of_gelus(e, b)[:, a0:a1],
                     MULT,
                 )
-            for u in range(0 if W3_WIDE else 2):
-                nc.vector.tensor_tensor(
-                    h[u][:].rearrange("p (a c i t) -> p a c t i", a=2, t=PACK, i=PRUN) if OWN_PART else interleaved(h[u][:]),
-                    by_slot2(sums["w3", e][u]) if OWN_PART else by_slot(sums["w3", e][u]),
-                    gelu_of_half(e, u),
-                    MULT,
+            for u in range(2):
+                nc.vector.tensor_copy(
+                    h[u][:].bitcast(U32).rearrange("p (c b) -> p c b", b=2),
+                    halves[:].bitcast(U32).rearrange("p b c -> p c b")[:, u * HALF_C : (u + 1) * HALF_C],
                 )
             h_words = keep.tile([P, C], U32, name=f"h_words{e}", align_bytes=64)
             h_scales = keep.tile([P, C], U8, name=f"h_scales{e}", align_bytes=64)
-            if not SPLIT0[e]:
-                nc.vector.quantize_mx(h_words[:].bitcast(FP8X4), h_scales[:], whole[:])
-            for u in range(2 if SPLIT0[e] else 0):
+            for u in range(2):
                 cols = slice(u * HALF_C, (u + 1) * HALF_C)
                 nc.vector.quantize_mx(h_words[:, cols].bitcast(FP8X4), h_scales[:, cols], h[u][:])
             hidden_codes[e] = (h_words, h_scales)
 
-        def multiply_down(e, n, c0, c1, bank):
+        def down(e, n, c0, c1, tag, y_sbuf):
+            y = bank(tag)
             words, scales = codes["w2", e, 0]
             h_words, h_scales = hidden_codes[e]
             cols = slice(n * P, (n + 1) * P)
             nc.tensor.matmul_mx(
-                bank,
+                y[:, 0 : c1 - c0],
                 lhsT=words[:, cols].bitcast(FP8X4),
                 lhsT_scale=scales[:, cols],
                 rhs=h_words[:, c0:c1].bitcast(FP8X4),
@@ -348,96 +250,51 @@ def tile_routed_moe_kernel(tc, xT, w1, w3, w2, gate, offs, out):
                 start=True,
                 stop=True,
             )
-
-        def scatter(e, n, c0, c1, y_sbuf):
-            if e == 0 and n in WINDOW_HOST.values():
-                held[n] = y_sbuf
-                return
-            scatter_now(e, n, c0, c1, y_sbuf)
-
-        def scatter_now(e, n, c0, c1, y_sbuf):
-            entries = offsets[:, (e * C + c0) // 16 : (e * C + c1) // 16]
+            nc.scalar.copy(y_sbuf, y[:, 0 : c1 - c0])
+            entries = offsets[:, (e * C + c0) // LIST_ROWS : (e * C + c1) // LIST_ROWS]
             nc.vector.tensor_tensor(windows[n][:].indirect(entries), y_sbuf, gates[e][:, n, c0:c1], MULT)
 
-        def down(e, n, c0, c1, tag):
-            y = psum.tile([P, BANK], F32, name=tag, tag=tag)
-            multiply_down(e, n, c0, c1, y[:, 0 : c1 - c0])
-            if Y_IN_W2[e] and n < 2:
-                y_sbuf = w2_parts[e, W2_CUTS[e][-2]][:, 2 * n + c0 // HALF_C, 0 : c1 - c0]
-            elif (e, n) in Y_HOST:
-                y_sbuf = raws[Y_HOST[e, n]][:, n, C + c0 : C + c1]
+        def way_back(e, n, host=None):
+            tags = [f"w1_{e}_bank0", f"w1_{e}_bank1", f"w3_{1 - e}_bank0", f"w3_{1 - e}_bank1", f"w3_{e}_bank0"]
+            if n == 0:
+                for u in range(2):
+                    y_sbuf = keep.tile([P, HALF_C], F32, name=f"y{e}_0_{u}")
+                    down(e, 0, u * HALF_C, (u + 1) * HALF_C, tags[u], y_sbuf[:])
+            elif host is None:
+                y_sbuf = keep.tile([P, C], F32, name=f"y{e}_{n}")
+                down(e, n, 0, C, tags[n + 1], y_sbuf[:])
             else:
-                y_sbuf = keep.tile([P, c1 - c0], F32, name=f"y{e}_{n}_{c0}")[:]
-            nc.scalar.copy(y_sbuf, y[:, 0 : c1 - c0])
-            scatter(e, n, c0, c1, y_sbuf)
-
-        def w2_block(e, c0, c1):
-            entry = ("w2", e, 0)
-            words, scales = codes[entry]
-            cols = slice(c0, c1)
-            if c0 == 0 and EARLY[e]:
-                part = keep.tile([P, BANK], BF16, name=f"w2_first{e}", tag=f"first{e}", align_bytes=64)[:]
-            else:
-                part = rounded[entry][:, c0 * PACK : c1 * PACK]
-            start = max(c for c in W2_CUTS[e] if c <= c0)
-            interleave(nc.scalar.copy, part, w2_parts[e, start][:, :, c0 - start : c1 - start], 0, c1 - c0)
-            nc.vector.quantize_mx(words[:, cols].bitcast(FP8X4), scales[:, cols], part)
-
-        def way_back(e, n):
-            o = 1 - e
-            banks = [f"w1_{e}_bank0", f"w1_{e}_bank1", f"w3_{o}_bank0", f"w3_{o}_bank1", f"w3_{e}_bank0"]
-            if n == 0 and SPLIT0[e]:
-                down(e, 0, 0, HALF_C, banks[0])
-                down(e, 0, HALF_C, C, banks[1])
-            else:
-                down(e, n, 0, C, banks[n + 1])
+                down(e, n, 0, C, tags[n + 1], raws[host][:, n, C:])
             if e == E - 1:
                 nc.sync.dma_start(out[n * P : (n + 1) * P, :], windows[n][:])
 
-        if not OFFS_LATE:
-            nc.sync.dma_start(offsets[:], offs)
-        load(stream[0])
-        if OFFS_LATE:
-            nc.sync.dma_start(offsets[:], offs)
-        round_to_bf16(stream[0])
-        for i, entry in enumerate(stream):
+        load(STREAM[0])
+        nc.sync.dma_start(offsets[:], offs)
+        round_to_bf16(STREAM[0])
+        for entry, following in zip(STREAM, STREAM[1:] + [None]):
             kind, e, s = entry
-            if i + 1 < len(stream):
-                load(stream[i + 1])
+            if following is not None:
+                load(following)
                 if kind != "w2":
-                    round_to_bf16(stream[i + 1])
+                    round_to_bf16(following)
             quantize(entry)
-            if kind == "w2" and EARLY[e]:
-                w2_block(e, 0, P)
-            if entry == HIDDEN_AT[0] or entry == HIDDEN_AT[1]:
-                hidden(HIDDEN_AT.index(entry))
-            if kind == "x" and s > 0:
-                gather_words(s - 1)
-            if entry == ("x", 0, last):
-                gather_scales()
-                gather_words(last)
-            if (kind, e, s - 1) in QPAIR:
-                multiply_up((kind, e, s - 1))
-            if kind in up_weights and entry not in QPAIR:
-                multiply_up(entry)
-            if entry in GELU_HOST:
-                gelu(GELU_HOST.index(entry), entry)
-            if kind == "w2":
-                for c0, c1 in zip(W2_ROUND[e][:-1], W2_ROUND[e][1:]):
-                    if c0 > 0 or not EARLY[e]:
-                        w2_block(e, c0, c1)
-            if entry in WAY_AT:
-                e2 = WAY_AT.index(entry)
+            if kind == "x":
+                if s > 0:
+                    gather_words(s - 1)
+                if s == LAST:
+                    gather_scales()
+                    gather_words(LAST)
+            elif kind == "w2":
+                hidden(e)
                 for n in range(BLOCKS):
-                    if (e2, n) not in Y_HOST or Y_HOST[e2, n][0] == "w2":
-                        way_back(e2, n)
-            if kind == "w2":
-                if i + 1 < len(stream):
-                    round_to_bf16(stream[i + 1])
-            for (e2, n), host in Y_HOST.items():
-                if host == entry and kind != "w2":
-                    way_back(e2, n)
-            if entry in WINDOW_HOST:
-                n = WINDOW_HOST[entry]
-                windows[n] = keep.tile([P, T], F32, name=f"window{n}", tag=f"window{n}", align_bytes=64)
-                scatter_now(0, n, 0, C, held[n])
+                    w2_block(e, n)
+                for n in range(BLOCKS if e == E - 1 else 2):
+                    way_back(e, n)
+                if following is not None:
+                    round_to_bf16(following)
+            else:
+                multiply_up(entry)
+                if (kind, s) == ("w3", GELU_BEHIND[e]):
+                    gelu(e)
+                if (kind, e) == ("w1", 1) and s < 2:
+                    way_back(0, 2 + s, host=entry)

@@ -35,7 +35,6 @@ STREAM = [("x", 0, s) for s in range(PASSES)] + [
 
 LOADED_WITH_NEXT = [("x", 0, 2), ("w1", 0, 0), ("w1", 0, 2)]
 GELU_BEHIND = (1, 2)
-SHARED = 3 * WIDTH // 8
 
 
 def columns_on_vector(kind, e, s):
@@ -49,9 +48,15 @@ def columns_on_vector(kind, e, s):
         return 0
     if s == GELU_BEHIND[e] + 1:
         return WIDTH
-    if s == LAST - 1:
-        return WIDTH // 2
-    return SHARED
+    if (e, s) == (0, GELU_BEHIND[0]):
+        return 3 * WIDTH // 8
+    return WIDTH // 2
+
+
+def in_halves(kind, e, s):
+    if kind not in ("w1", "w3") or (kind, s) in (("w3", LAST), ("w3", GELU_BEHIND[e])):
+        return False
+    return columns_on_vector(kind, e, s) > 0
 
 
 def tile_routed_moe_kernel(tc, xT, w1, w3, w2, gate, offs, out):
@@ -64,6 +69,7 @@ def tile_routed_moe_kernel(tc, xT, w1, w3, w2, gate, offs, out):
         pair_pool = ctx.enter_context(tc.tile_pool(name="pair", bufs=len(LOADED_WITH_NEXT)))
         code_pool = ctx.enter_context(tc.tile_pool(name="codes", bufs=2 * PASSES))
         rounded_pool = ctx.enter_context(tc.tile_pool(name="rounded", bufs=7))
+        halves_pool = ctx.enter_context(tc.tile_pool(name="halves", bufs=E))
         psum = ctx.enter_context(tc.psum_pool(name="psum", bufs=1))
 
         offsets = keep.tile([P, SLOTS // LIST_ROWS], U16, name="offsets")
@@ -144,6 +150,11 @@ def tile_routed_moe_kernel(tc, xT, w1, w3, w2, gate, offs, out):
                 interleave_permuted(nc.scalar.copy, dst, raw, slice(2, 3), 0, WIDTH)
                 return
             cut = columns_on_vector(kind, e, s)
+            if in_halves(kind, e, s):
+                interleave_permuted(nc.vector.tensor_copy, dst, raw, slice(0, 2), 0, WIDTH)
+                second = nc.vector.tensor_copy if cut == WIDTH else nc.scalar.copy
+                interleave_permuted(second, dst, raw, slice(2, 4), 0, WIDTH)
+                return
             for copy, c0, c1 in ((nc.vector.tensor_copy, 0, cut), (nc.scalar.copy, cut, WIDTH)):
                 if c1 > c0 and kind == "x":
                     interleave(copy, dst, raw, c0, c1)
@@ -165,8 +176,15 @@ def tile_routed_moe_kernel(tc, xT, w1, w3, w2, gate, offs, out):
             codes[entry] = (words, scales)
             if kind == "w2":
                 return
-            cuts = (0, 2 * P, 3 * P, WIDTH) if (kind, s) == ("w3", LAST) else (0, WIDTH)
-            for c0, c1 in zip(cuts[:-1], cuts[1:]):
+            if (kind, s) == ("w3", LAST):
+                spans = [(0, 2 * P), (2 * P, 3 * P), (3 * P, WIDTH)]
+            elif not in_halves(kind, e, s):
+                spans = [(0, WIDTH)]
+            elif columns_on_vector(kind, e, s) == WIDTH:
+                spans = [(0, 2 * P), (2 * P, WIDTH)]
+            else:
+                spans = [(2 * P, WIDTH), (0, 2 * P)]
+            for c0, c1 in spans:
                 quantize_columns(words, scales, rounded[entry], c0, c1)
 
         def w2_block(e, n):
@@ -215,8 +233,8 @@ def tile_routed_moe_kernel(tc, xT, w1, w3, w2, gate, offs, out):
                 nc.scalar.activation(of_gelus(e, b), of_bank(sums["w1", e][b]), GELU)
 
         def hidden(e):
-            h = [keep.tile([P, PACK * HALF_C], BF16, name=f"h{e}_{u}", align_bytes=64) for u in range(2)]
-            halves = keep.tile([P, 2, 2 * C], BF16, name=f"halves{e}", align_bytes=64)
+            h = [keep.tile([P, PACK * HALF_C], BF16, name=f"{half}{e}", align_bytes=64) for half in ("first", "second")]
+            halves = halves_pool.tile([P, 2, 2 * C], BF16, name="halves", align_bytes=64)
             for b, a0, a1 in ((0, 0, QUARTERS), (1, 0, QUARTERS // 2), (1, QUARTERS // 2, QUARTERS)):
                 nc.vector.tensor_tensor(
                     halves[:, b, :].rearrange("p (a c i t) -> p a c t i", a=QUARTERS, t=2, i=PAIR)[:, a0:a1],
@@ -258,10 +276,10 @@ def tile_routed_moe_kernel(tc, xT, w1, w3, w2, gate, offs, out):
             tags = [f"w1_{e}_bank0", f"w1_{e}_bank1", f"w3_{1 - e}_bank0", f"w3_{1 - e}_bank1", f"w3_{e}_bank0"]
             if n == 0:
                 for u in range(2):
-                    y_sbuf = keep.tile([P, HALF_C], F32, name=f"y{e}_0_{u}")
+                    y_sbuf = keep.tile([P, HALF_C], F32, name=f"y{e}_0_{u * HALF_C}")
                     down(e, 0, u * HALF_C, (u + 1) * HALF_C, tags[u], y_sbuf[:])
             elif host is None:
-                y_sbuf = keep.tile([P, C], F32, name=f"y{e}_{n}")
+                y_sbuf = keep.tile([P, C], F32, name=f"y{e}_{n}_0")
                 down(e, n, 0, C, tags[n + 1], y_sbuf[:])
             else:
                 down(e, n, 0, C, tags[n + 1], raws[host][:, n, C:])

@@ -40,7 +40,7 @@ GELU_BEHIND = (1, 2)
 def columns_on_vector(kind, e, s):
     if kind == "x":
         return WIDTH // 4
-    if kind == "w1" and s == LAST:
+    if kind == "w1" and s == LAST - e:
         return WIDTH
     if kind == "w1" and e == 0:
         return WIDTH // 2 if s == 1 else 0
@@ -145,9 +145,8 @@ def tile_routed_moe_kernel(tc, xT, w1, w3, w2, gate, offs, out):
             if kind == "w2":
                 return
             if (kind, s) == ("w3", LAST):
-                interleave_permuted(nc.vector.tensor_copy, dst, raw, slice(0, 2), 0, WIDTH)
-                interleave_permuted(nc.vector.tensor_copy, dst, raw, slice(3, 4), 0, WIDTH)
-                interleave_permuted(nc.scalar.copy, dst, raw, slice(2, 3), 0, WIDTH)
+                for t, copy in enumerate((nc.vector.tensor_copy, nc.vector.tensor_copy, nc.scalar.copy)):
+                    interleave_permuted(copy, dst, raw, slice(t, t + 1), 0, WIDTH)
                 return
             cut = columns_on_vector(kind, e, s)
             if in_halves(kind, e, s):
@@ -177,7 +176,10 @@ def tile_routed_moe_kernel(tc, xT, w1, w3, w2, gate, offs, out):
             if kind == "w2":
                 return
             if (kind, s) == ("w3", LAST):
-                spans = [(0, 2 * P), (2 * P, 3 * P), (3 * P, WIDTH)]
+                for t in range(2):
+                    quantize_columns(words, scales, rounded[entry], t * P, (t + 1) * P)
+                interleave_permuted(nc.vector.tensor_copy, rounded[entry], raws[entry], slice(3, 4), 0, WIDTH)
+                spans = [(2 * P, 3 * P), (3 * P, WIDTH)]
             elif not in_halves(kind, e, s):
                 spans = [(0, WIDTH)]
             elif columns_on_vector(kind, e, s) == WIDTH:
@@ -242,14 +244,14 @@ def tile_routed_moe_kernel(tc, xT, w1, w3, w2, gate, offs, out):
                     of_gelus(e, b)[:, a0:a1],
                     MULT,
                 )
+            h_words = keep.tile([P, C], U32, name=f"h_words{e}", align_bytes=64)
+            h_scales = keep.tile([P, C], U8, name=f"h_scales{e}", align_bytes=64)
             for u in range(2):
                 nc.vector.tensor_copy(
                     h[u][:].bitcast(U32).rearrange("p (c b) -> p c b", b=2),
                     halves[:].bitcast(U32).rearrange("p b c -> p c b")[:, u * HALF_C : (u + 1) * HALF_C],
                 )
-            h_words = keep.tile([P, C], U32, name=f"h_words{e}", align_bytes=64)
-            h_scales = keep.tile([P, C], U8, name=f"h_scales{e}", align_bytes=64)
-            for u in range(2):
+                w2_block(e, u)
                 cols = slice(u * HALF_C, (u + 1) * HALF_C)
                 nc.vector.quantize_mx(h_words[:, cols].bitcast(FP8X4), h_scales[:, cols], h[u][:])
             hidden_codes[e] = (h_words, h_scales)
@@ -304,7 +306,7 @@ def tile_routed_moe_kernel(tc, xT, w1, w3, w2, gate, offs, out):
                     gather_words(LAST)
             elif kind == "w2":
                 hidden(e)
-                for n in range(BLOCKS):
+                for n in range(2, BLOCKS):
                     w2_block(e, n)
                 for n in range(BLOCKS if e == E - 1 else 2):
                     way_back(e, n)

@@ -90,15 +90,14 @@ def tile_routed_moe_kernel(tc, xT, w1, w3, w2, gate, offs, out):
             gates[e] = tile
 
         def load_w2(e, raw, pieces):
-            rows = w2[e].rearrange("(m t r) n -> r m t n", t=PACK, r=PAIR)
+            rows = w2[e].rearrange("(p t) n -> p t n", t=PACK)
             flat = raw[:].rearrange("p t c -> p (t c)")
             width = WIDTH // pieces
             for c0 in range(0, WIDTH, width):
                 part = flat[:, PACK * c0 : PACK * (c0 + width)].rearrange("p (t c) -> p t c", t=PACK)
                 for n in range(c0 // P, (c0 + width) // P):
                     w2_raw[e, n] = part[:, :, n * P - c0 : (n + 1) * P - c0]
-                for r in range(PAIR):
-                    nc.sync.dma_start(part[r::PAIR], rows[r][:, :, c0 : c0 + width])
+                nc.sync.dma_start(part, rows[:, :, c0 : c0 + width])
 
         def load(entry):
             kind, e, s = entry
@@ -130,11 +129,11 @@ def tile_routed_moe_kernel(tc, xT, w1, w3, w2, gate, offs, out):
                 src[:].rearrange("p j (c i) -> p c j i", i=PAIR)[:, c0 // PAIR : c1 // PAIR],
             )
 
-        def interleave_permuted(copy, dst, src, blocks, c0, c1):
-            ms = slice(c0 // (PACK * PAIR), c1 // (PACK * PAIR))
+        def interleave_permuted(copy, dst, src, banks, c0, c1):
+            ms = slice(c0 // BLOCKS, c1 // BLOCKS)
             copy(
-                dst[:].rearrange("p (t m r j) -> p t m j r", t=BLOCKS, r=PAIR, j=PACK)[:, blocks, ms],
-                src[:].rearrange("p j (m t r) -> p t m j r", t=BLOCKS, r=PAIR)[:, blocks, ms],
+                dst[:].rearrange("p (b i m j) -> p b m j i", b=2, i=PAIR, j=PACK)[:, banks, ms],
+                src[:].rearrange("p j (m b i) -> p b m j i", b=2, i=PAIR)[:, banks, ms],
             )
 
         def round_to_bf16(entry):
@@ -145,20 +144,21 @@ def tile_routed_moe_kernel(tc, xT, w1, w3, w2, gate, offs, out):
             if kind == "w2":
                 return
             if (kind, s) == ("w3", LAST):
-                for t, copy in enumerate((nc.vector.tensor_copy, nc.vector.tensor_copy, nc.scalar.copy)):
-                    interleave_permuted(copy, dst, raw, slice(t, t + 1), 0, WIDTH)
+                interleave_permuted(nc.vector.tensor_copy, dst, raw, slice(0, 1), 0, WIDTH)
+                interleave_permuted(nc.vector.tensor_copy, dst, raw, slice(1, 2), 0, WIDTH // 2)
+                interleave_permuted(nc.scalar.copy, dst, raw, slice(1, 2), WIDTH // 2, WIDTH)
                 return
             cut = columns_on_vector(kind, e, s)
             if in_halves(kind, e, s):
-                interleave_permuted(nc.vector.tensor_copy, dst, raw, slice(0, 2), 0, WIDTH)
+                interleave_permuted(nc.vector.tensor_copy, dst, raw, slice(0, 1), 0, WIDTH)
                 second = nc.vector.tensor_copy if cut == WIDTH else nc.scalar.copy
-                interleave_permuted(second, dst, raw, slice(2, 4), 0, WIDTH)
+                interleave_permuted(second, dst, raw, slice(1, 2), 0, WIDTH)
                 return
             for copy, c0, c1 in ((nc.vector.tensor_copy, 0, cut), (nc.scalar.copy, cut, WIDTH)):
                 if c1 > c0 and kind == "x":
                     interleave(copy, dst, raw, c0, c1)
                 elif c1 > c0:
-                    interleave_permuted(copy, dst, raw, slice(0, BLOCKS), c0, c1)
+                    interleave_permuted(copy, dst, raw, slice(0, 2), c0, c1)
 
         def quantize_columns(words, scales, src, c0, c1):
             nc.vector.quantize_mx(words[:, c0:c1].bitcast(FP8X4), scales[:, c0:c1], src[:, PACK * c0 : PACK * c1])
@@ -176,10 +176,7 @@ def tile_routed_moe_kernel(tc, xT, w1, w3, w2, gate, offs, out):
             if kind == "w2":
                 return
             if (kind, s) == ("w3", LAST):
-                for t in range(2):
-                    quantize_columns(words, scales, rounded[entry], t * P, (t + 1) * P)
-                interleave_permuted(nc.vector.tensor_copy, rounded[entry], raws[entry], slice(3, 4), 0, WIDTH)
-                spans = [(2 * P, 3 * P), (3 * P, WIDTH)]
+                spans = [(0, 2 * P), (2 * P, 3 * P), (3 * P, WIDTH)]
             elif not in_halves(kind, e, s):
                 spans = [(0, WIDTH)]
             elif columns_on_vector(kind, e, s) == WIDTH:

@@ -13,6 +13,7 @@ U8 = mybir.dt.uint8
 FP8X4 = mybir.dt.float8_e4m3fn_x4
 MULT = mybir.AluOpType.mult
 GELU = mybir.ActivationFunctionType.Gelu_apprx_tanh
+COPY = mybir.ActivationFunctionType.Copy
 
 P = 128
 PACK = 4
@@ -23,105 +24,57 @@ WIDTH = 512
 BLOCKS = WIDTH // P
 BANK = 512
 SLOTS = E * C
-HALF_C = C // 2
-QUARTERS = 4
 LIST_ROWS = 16
 PAIR = 2
 WINDOW = T + T // 2
-
-STREAM = [("x", 0, s) for s in range(PASSES)] + [
-    (kind, e, s) for e in range(E) for kind, passes in (("w1", PASSES), ("w3", PASSES), ("w2", 1)) for s in range(passes)
-]
-
-LOADED_WITH_NEXT = [("x", 0, 2), ("w1", 0, 0), ("w1", 0, 2)]
-GELU_BEHIND = (1, 2)
-
-
-def columns_on_vector(kind, e, s):
-    if kind == "x":
-        return WIDTH // 4
-    if kind == "w1" and s == LAST - e:
-        return WIDTH
-    if kind == "w1" and e == 0:
-        return WIDTH // 2 if s == 1 else 0
-    if kind == "w1" or (e, s) == (1, 0):
-        return 0
-    if s == GELU_BEHIND[e] + 1:
-        return WIDTH
-    if (e, s) == (0, GELU_BEHIND[0]):
-        return 3 * WIDTH // 8
-    return WIDTH // 2
-
-
-def in_halves(kind, e, s):
-    if kind not in ("w1", "w3") or (kind, s) in (("w3", LAST), ("w3", GELU_BEHIND[e])):
-        return False
-    return columns_on_vector(kind, e, s) > 0
+TOKENS_ON_VECTOR = T // 4
 
 
 def tile_routed_moe_kernel(tc, xT, w1, w3, w2, gate, offs, out):
     nc = tc.nc
-    along_k = {("x", 0): xT, ("w1", 0): w1[0], ("w1", 1): w1[1], ("w3", 0): w3[0], ("w3", 1): w3[1]}
+    vector, scalar = nc.vector.tensor_copy, nc.scalar.copy
+
+    def rounders(kind, e, s):
+        if (kind, e, s) == ("w1", 0, 0):
+            return scalar, scalar
+        if (kind, e) == ("w1", 1) and s < LAST:
+            return vector, vector
+        if (kind, s) == ("w3", 0):
+            return vector, vector
+        return vector, scalar
 
     with ExitStack() as ctx:
         keep = ctx.enter_context(tc.tile_pool(name="keep", bufs=1))
-        raw_pool = ctx.enter_context(tc.tile_pool(name="raw", bufs=9))
-        pair_pool = ctx.enter_context(tc.tile_pool(name="pair", bufs=len(LOADED_WITH_NEXT)))
+        raw_pool = ctx.enter_context(tc.tile_pool(name="raw", bufs=12))
+        rounded_pool = ctx.enter_context(tc.tile_pool(name="rounded", bufs=5))
         code_pool = ctx.enter_context(tc.tile_pool(name="codes", bufs=2 * PASSES))
-        rounded_pool = ctx.enter_context(tc.tile_pool(name="rounded", bufs=7))
-        halves_pool = ctx.enter_context(tc.tile_pool(name="halves", bufs=E))
         psum = ctx.enter_context(tc.psum_pool(name="psum", bufs=1))
 
         offsets = keep.tile([P, SLOTS // LIST_ROWS], U16, name="offsets")
-
         x_scales = keep.tile([P, WINDOW], U8, name="x_scales", align_bytes=64)
         nc.gpsimd.memset(x_scales[:, 0:T], 0)
-
         windows = [keep.tile([P, T], F32, name=f"window{n}") for n in range(BLOCKS)]
 
-        raws, rounded, codes = {}, {}, {}
-        w2_raw, gates, sums, hidden_codes, slot_words, slot_scales = {}, {}, {}, {}, {}, []
+        def load(rows):
+            raw = raw_pool.tile([P, PACK, WIDTH], F32, name="raw")
+            nc.sync.dma_start(raw[:], rows.rearrange("(p j) c -> p j c", j=PACK))
+            return raw
 
         def load_gate(e, pieces):
-            tile = keep.tile([P, BLOCKS, C], F32, name=f"gate{e}")
+            raw = raw_pool.tile([P, PACK, WIDTH], F32, name="raw")
+            tile = raw[:].rearrange("p j c -> p (j c)")[:, 0 : BLOCKS * C].rearrange("p (n c) -> p n c", n=BLOCKS)
             rows = gate[:, e * C : (e + 1) * C].rearrange("(n p) c -> p n c", p=P)
             for n0 in range(0, BLOCKS, BLOCKS // pieces):
                 nc.sync.dma_start(tile[:, n0 : n0 + BLOCKS // pieces], rows[:, n0 : n0 + BLOCKS // pieces])
-            gates[e] = tile
+            return tile
 
-        def load_w2(e, raw, pieces):
-            rows = w2[e].rearrange("(p t) n -> p t n", t=PACK)
-            flat = raw[:].rearrange("p t c -> p (t c)")
-            width = WIDTH // pieces
-            for c0 in range(0, WIDTH, width):
-                part = flat[:, PACK * c0 : PACK * (c0 + width)].rearrange("p (t c) -> p t c", t=PACK)
-                for n in range(c0 // P, (c0 + width) // P):
-                    w2_raw[e, n] = part[:, :, n * P - c0 : (n + 1) * P - c0]
-                nc.sync.dma_start(part, rows[:, :, c0 : c0 + width])
+        def rounded_tile():
+            return rounded_pool.tile([P, PACK * WIDTH], BF16, name="rounded", align_bytes=64)
 
-        def load(entry):
-            kind, e, s = entry
-            if entry == ("w1", 1, 0):
-                load_gate(0, 1)
-            if entry in raws:
-                return
-            if entry in LOADED_WITH_NEXT:
-                pair = pair_pool.tile([P, 2, PACK, WIDTH], F32, name="pair")
-                rows = along_k[kind, e][s * K_PASS : (s + 2) * K_PASS, :]
-                nc.sync.dma_start(
-                    pair[:].rearrange("p g j c -> p g (j c)"), rows.rearrange("(g p j) c -> p g (j c)", g=2, j=PACK)
-                )
-                raws[entry], raws[kind, e, s + 1] = pair[:, 0], pair[:, 1]
-                return
-            raw = raw_pool.tile([P, PACK, WIDTH], F32, name="raw")
-            raws[entry] = raw
-            if kind == "w2":
-                load_w2(e, raw, 2 if e == E - 1 else 1)
-                if e == E - 1:
-                    load_gate(e, 2)
-            else:
-                rows = along_k[kind, e][s * K_PASS : (s + 1) * K_PASS, :]
-                nc.sync.dma_start(raw[:], rows.rearrange("(p j) c -> p j c", j=PACK))
+        def code_tiles():
+            words = code_pool.tile([P, WIDTH], U32, name="words", align_bytes=64)
+            scales = code_pool.tile([P, WIDTH], U8, name="scales", align_bytes=64)
+            return words, scales
 
         def interleave(copy, dst, src, c0, c1):
             copy(
@@ -129,189 +82,134 @@ def tile_routed_moe_kernel(tc, xT, w1, w3, w2, gate, offs, out):
                 src[:].rearrange("p j (c i) -> p c j i", i=PAIR)[:, c0 // PAIR : c1 // PAIR],
             )
 
-        def interleave_permuted(copy, dst, src, banks, c0, c1):
-            ms = slice(c0 // BLOCKS, c1 // BLOCKS)
+        def interleave_permuted(copy, dst, src, b):
             copy(
-                dst[:].rearrange("p (b i m j) -> p b m j i", b=2, i=PAIR, j=PACK)[:, banks, ms],
-                src[:].rearrange("p j (m b i) -> p b m j i", b=2, i=PAIR)[:, banks, ms],
+                dst[:].rearrange("p (b i m j) -> p b m j i", b=2, i=PAIR, j=PACK)[:, b],
+                src[:].rearrange("p j (m b i) -> p b m j i", b=2, i=PAIR)[:, b],
             )
 
-        def round_to_bf16(entry):
-            kind, e, s = entry
-            raw = raws[entry]
-            dst = rounded_pool.tile([P, PACK * WIDTH], BF16, name="dst", align_bytes=64)
-            rounded[entry] = dst
-            if kind == "w2":
-                return
-            if (kind, s) == ("w3", LAST):
-                interleave_permuted(nc.vector.tensor_copy, dst, raw, slice(0, 1), 0, WIDTH)
-                interleave_permuted(nc.vector.tensor_copy, dst, raw, slice(1, 2), 0, WIDTH // 2)
-                interleave_permuted(nc.scalar.copy, dst, raw, slice(1, 2), WIDTH // 2, WIDTH)
-                return
-            cut = columns_on_vector(kind, e, s)
-            if in_halves(kind, e, s):
-                interleave_permuted(nc.vector.tensor_copy, dst, raw, slice(0, 1), 0, WIDTH)
-                second = nc.vector.tensor_copy if cut == WIDTH else nc.scalar.copy
-                interleave_permuted(second, dst, raw, slice(1, 2), 0, WIDTH)
-                return
-            for copy, c0, c1 in ((nc.vector.tensor_copy, 0, cut), (nc.scalar.copy, cut, WIDTH)):
-                if c1 > c0 and kind == "x":
-                    interleave(copy, dst, raw, c0, c1)
-                elif c1 > c0:
-                    interleave_permuted(copy, dst, raw, slice(0, 2), c0, c1)
-
-        def quantize_columns(words, scales, src, c0, c1):
+        def quantize(words, scales, src, c0, c1):
             nc.vector.quantize_mx(words[:, c0:c1].bitcast(FP8X4), scales[:, c0:c1], src[:, PACK * c0 : PACK * c1])
-
-        def quantize(entry):
-            kind, e, s = entry
-            if kind == "x":
-                words = keep.tile([P, WINDOW], U32, name=f"x_words{s}", align_bytes=64)
-                quantize_columns(words, x_scales[4 * s : P], rounded[entry], 0, T)
-                codes[entry] = (words, x_scales)
-                return
-            words = code_pool.tile([P, WIDTH], U32, name="words", align_bytes=64)
-            scales = code_pool.tile([P, WIDTH], U8, name="scales", align_bytes=64)
-            codes[entry] = (words, scales)
-            if kind == "w2":
-                return
-            if (kind, s) == ("w3", LAST):
-                spans = [(0, 2 * P), (2 * P, 3 * P), (3 * P, WIDTH)]
-            elif not in_halves(kind, e, s):
-                spans = [(0, WIDTH)]
-            elif columns_on_vector(kind, e, s) == WIDTH:
-                spans = [(0, 2 * P), (2 * P, WIDTH)]
-            else:
-                spans = [(2 * P, WIDTH), (0, 2 * P)]
-            for c0, c1 in spans:
-                quantize_columns(words, scales, rounded[entry], c0, c1)
-
-        def w2_block(e, n):
-            entry = ("w2", e, 0)
-            interleave(nc.scalar.copy, rounded[entry][:, n * PACK * P : (n + 1) * PACK * P], w2_raw[e, n], 0, P)
-            quantize_columns(*codes[entry], rounded[entry], n * P, (n + 1) * P)
-
-        def gather_words(s):
-            slot_words[s] = keep.tile([P, SLOTS], U32, name=f"slot_words{s}", align_bytes=64)
-            nc.vector.tensor_copy(slot_words[s][:], codes["x", 0, s][0][:].indirect(offsets[:]))
-
-        def gather_scales():
-            slot_scales.append(keep.tile([P, SLOTS], U8, name="slot_scales", align_bytes=64))
-            nc.vector.tensor_copy(slot_scales[0][:], x_scales[:].indirect(offsets[:]))
 
         def bank(tag):
             return psum.tile([P, BANK], F32, name=tag, tag=tag)
 
-        def multiply_up(entry):
-            kind, e, s = entry
+        slot_words = []
+
+        def gather_words(s, words):
+            slot_words.append(keep.tile([P, SLOTS], U32, name=f"slot_words{s}", align_bytes=64))
+            nc.vector.tensor_copy(slot_words[s][:], words[:].indirect(offsets[:]))
+
+        x_words = []
+        for s in range(PASSES):
+            raw = load(xT[s * K_PASS : (s + 1) * K_PASS, :])
             if s == 0:
-                sums[kind, e] = [bank(f"{kind}_{e}_bank{b}") for b in range(2)]
-            words, scales = codes[entry]
+                nc.sync.dma_start(offsets[:], offs)
+            dst = rounded_tile()
+            interleave(vector, dst, raw, 0, TOKENS_ON_VECTOR)
+            interleave(scalar, dst, raw, TOKENS_ON_VECTOR, T)
+            if s > 0:
+                gather_words(s - 1, x_words[s - 1])
+            x_words.append(keep.tile([P, WINDOW], U32, name=f"x_words{s}", align_bytes=64))
+            quantize(x_words[s], x_scales[4 * s : P], dst, 0, T)
+        slot_scales = keep.tile([P, SLOTS], U8, name="slot_scales", align_bytes=64)
+        nc.vector.tensor_copy(slot_scales[:], x_scales[:].indirect(offsets[:]))
+        gather_words(LAST, x_words[LAST])
+
+        def first_layer(kind, e, weights):
+            sums = [bank(f"{kind}_{e}_bank{b}") for b in range(2)]
             slots = slice(e * C, (e + 1) * C)
-            for t in range(BLOCKS):
-                cols = slice(t * P, (t + 1) * P)
-                nc.tensor.matmul_mx(
-                    sums[kind, e][t // 2][:, (t % 2) * C : (t % 2 + 1) * C],
-                    lhsT=words[:, cols].bitcast(FP8X4),
-                    lhsT_scale=scales[:, cols],
-                    rhs=slot_words[s][:, slots].bitcast(FP8X4),
-                    rhs_scale=slot_scales[0][4 * s : P, slots],
-                    start=(s == 0 and t % 2 == 0),
-                    stop=(s == LAST and t % 2 == 1),
-                )
+            for s in range(PASSES):
+                raw = load(weights[s * K_PASS : (s + 1) * K_PASS, :])
+                dst = rounded_tile()
+                words, scales = code_tiles()
+                for b, copy in enumerate(rounders(kind, e, s)):
+                    interleave_permuted(copy, dst, raw, b)
+                for b in range(2):
+                    quantize(words, scales, dst, 2 * b * P, 2 * (b + 1) * P)
+                    for t in (2 * b, 2 * b + 1):
+                        cols = slice(t * P, (t + 1) * P)
+                        nc.tensor.matmul_mx(
+                            sums[b][:, (t % 2) * C : (t % 2 + 1) * C],
+                            lhsT=words[:, cols].bitcast(FP8X4),
+                            lhsT_scale=scales[:, cols],
+                            rhs=slot_words[s][:, slots].bitcast(FP8X4),
+                            rhs_scale=slot_scales[4 * s : P, slots],
+                            start=(s == 0 and t % 2 == 0),
+                            stop=(s == LAST and t % 2 == 1),
+                        )
+            return sums
 
-        def of_bank(sums_of_bank):
-            return sums_of_bank[:].rearrange("p (t a c i) -> p a c t i", t=2, a=QUARTERS, i=PAIR)
+        def in_pairs(sums_of_bank):
+            return sums_of_bank[:].rearrange("p (t c i) -> p c t i", t=2, i=PAIR)
 
-        def of_gelus(e, b):
-            rows = raws["w3", e, GELU_BEHIND[e]][:, :, C:]
-            return rows.rearrange("p a (c t i) -> p a c t i", t=BLOCKS, i=PAIR)[:, :, :, 2 * b : 2 * b + 2, :]
-
-        def gelu(e):
+        for e in range(E):
+            a = first_layer("w1", e, w1[e])
+            gelus = keep.tile([P, 2, BANK], F32, name=f"gelus{e}")
             for b in range(2):
-                nc.scalar.activation(of_gelus(e, b), of_bank(sums["w1", e][b]), GELU)
+                nc.scalar.activation(gelus[:, b, :].rearrange("p (c t i) -> p c t i", t=2, i=PAIR), in_pairs(a[b]), GELU)
+            sums = first_layer("w3", e, w3[e])
+            w2_raw = load(w2[e])
+            gates = load_gate(e, 2 if e == E - 1 else 1)
 
-        def hidden(e):
-            h = [keep.tile([P, PACK * HALF_C], BF16, name=f"{half}{e}", align_bytes=64) for half in ("first", "second")]
-            halves = halves_pool.tile([P, 2, 2 * C], BF16, name="halves", align_bytes=64)
-            for b, a0, a1 in ((0, 0, QUARTERS), (1, 0, QUARTERS // 2), (1, QUARTERS // 2, QUARTERS)):
+            halves = keep.tile([P, 2, 2 * C], BF16, name=f"halves{e}", align_bytes=64)
+            for b in range(2):
                 nc.vector.tensor_tensor(
-                    halves[:, b, :].rearrange("p (a c i t) -> p a c t i", a=QUARTERS, t=2, i=PAIR)[:, a0:a1],
-                    of_bank(sums["w3", e][b])[:, a0:a1],
-                    of_gelus(e, b)[:, a0:a1],
+                    halves[:, b, :].rearrange("p (c i t) -> p c t i", t=2, i=PAIR),
+                    in_pairs(sums[b]),
+                    gelus[:, b, :].rearrange("p (c t i) -> p c t i", t=2, i=PAIR),
                     MULT,
                 )
+            h = keep.tile([P, PACK * C], BF16, name=f"h{e}", align_bytes=64)
+            nc.vector.tensor_copy(
+                h[:].bitcast(U32).rearrange("p (c b) -> p c b", b=2),
+                halves[:].bitcast(U32).rearrange("p b c -> p c b"),
+            )
+            w2_rounded = rounded_tile()
+            w2_words, w2_scales = code_tiles()
+            for n in range(BLOCKS):
+                interleave(vector if (e, n) == (E - 1, BLOCKS - 1) else scalar, w2_rounded, w2_raw, n * P, (n + 1) * P)
+            quantize(w2_words, w2_scales, w2_rounded, 0, 2 * P)
             h_words = keep.tile([P, C], U32, name=f"h_words{e}", align_bytes=64)
             h_scales = keep.tile([P, C], U8, name=f"h_scales{e}", align_bytes=64)
-            for u in range(2):
-                nc.vector.tensor_copy(
-                    h[u][:].bitcast(U32).rearrange("p (c b) -> p c b", b=2),
-                    halves[:].bitcast(U32).rearrange("p b c -> p c b")[:, u * HALF_C : (u + 1) * HALF_C],
+            quantize(h_words, h_scales, h, 0, C)
+            quantize(w2_words, w2_scales, w2_rounded, 2 * P, WIDTH)
+
+            tags = [f"w1_{e}_bank0", f"w1_{e}_bank1", f"w3_{e}_bank0", f"w3_{e}_bank1"]
+            entries = offsets[:, e * C // LIST_ROWS : (e + 1) * C // LIST_ROWS]
+            ys, results = [], []
+            for n in range(BLOCKS):
+                cols = slice(n * P, (n + 1) * P)
+                ys.append(bank(tags[n]))
+                nc.tensor.matmul_mx(
+                    ys[n][:, 0:C],
+                    lhsT=w2_words[:, cols].bitcast(FP8X4),
+                    lhsT_scale=w2_scales[:, cols],
+                    rhs=h_words[:].bitcast(FP8X4),
+                    rhs_scale=h_scales[:],
+                    start=True,
+                    stop=True,
                 )
-                w2_block(e, u)
-                cols = slice(u * HALF_C, (u + 1) * HALF_C)
-                nc.vector.quantize_mx(h_words[:, cols].bitcast(FP8X4), h_scales[:, cols], h[u][:])
-            hidden_codes[e] = (h_words, h_scales)
+                results.append(keep.tile([P, C], F32, name=f"result{e}_{n}"))
 
-        def down(e, n, c0, c1, tag, y_sbuf):
-            y = bank(tag)
-            words, scales = codes["w2", e, 0]
-            h_words, h_scales = hidden_codes[e]
-            cols = slice(n * P, (n + 1) * P)
-            nc.tensor.matmul_mx(
-                y[:, 0 : c1 - c0],
-                lhsT=words[:, cols].bitcast(FP8X4),
-                lhsT_scale=scales[:, cols],
-                rhs=h_words[:, c0:c1].bitcast(FP8X4),
-                rhs_scale=h_scales[:, c0:c1],
-                start=True,
-                stop=True,
-            )
-            nc.scalar.copy(y_sbuf, y[:, 0 : c1 - c0])
-            entries = offsets[:, (e * C + c0) // LIST_ROWS : (e * C + c1) // LIST_ROWS]
-            nc.vector.tensor_tensor(windows[n][:].indirect(entries), y_sbuf, gates[e][:, n, c0:c1], MULT)
+            def times_gate(n):
+                nc.vector.tensor_tensor(results[n][:], ys[n][:, 0:C], gates[:, n], MULT)
 
-        def way_back(e, n, host=None):
-            tags = [f"w1_{e}_bank0", f"w1_{e}_bank1", f"w3_{1 - e}_bank0", f"w3_{1 - e}_bank1", f"w3_{e}_bank0"]
-            if n == 0:
-                for u in range(2):
-                    y_sbuf = keep.tile([P, HALF_C], F32, name=f"y{e}_0_{u * HALF_C}")
-                    down(e, 0, u * HALF_C, (u + 1) * HALF_C, tags[u], y_sbuf[:])
-            elif host is None:
-                y_sbuf = keep.tile([P, C], F32, name=f"y{e}_{n}_0")
-                down(e, n, 0, C, tags[n + 1], y_sbuf[:])
-            else:
-                down(e, n, 0, C, tags[n + 1], raws[host][:, n, C:])
-            if e == E - 1:
+            def scatter_on_scalar(n):
+                nc.scalar.activation(windows[n][:].indirect(entries), results[n][:], COPY)
+
+            def store(n):
                 nc.sync.dma_start(out[n * P : (n + 1) * P, :], windows[n][:])
 
-        load(STREAM[0])
-        nc.sync.dma_start(offsets[:], offs)
-        round_to_bf16(STREAM[0])
-        for entry, following in zip(STREAM, STREAM[1:] + [None]):
-            kind, e, s = entry
-            if following is not None:
-                load(following)
-                if kind != "w2":
-                    round_to_bf16(following)
-            quantize(entry)
-            if kind == "x":
-                if s > 0:
-                    gather_words(s - 1)
-                if s == LAST:
-                    gather_scales()
-                    gather_words(LAST)
-            elif kind == "w2":
-                hidden(e)
-                for n in range(2, BLOCKS):
-                    w2_block(e, n)
-                for n in range(BLOCKS if e == E - 1 else 2):
-                    way_back(e, n)
-                if following is not None:
-                    round_to_bf16(following)
+            if e < E - 1:
+                for n in range(BLOCKS):
+                    times_gate(n)
+                    scatter_on_scalar(n)
             else:
-                multiply_up(entry)
-                if (kind, s) == ("w3", GELU_BEHIND[e]):
-                    gelu(e)
-                if (kind, e) == ("w1", 1) and s < 2:
-                    way_back(0, 2 + s, host=entry)
+                for n in range(0, BLOCKS, 2):
+                    nc.scalar.copy(results[n][:], ys[n][:, 0:C])
+                    times_gate(n + 1)
+                    nc.vector.tensor_tensor(windows[n][:].indirect(entries), results[n][:], gates[:, n], MULT)
+                    scatter_on_scalar(n + 1)
+                    store(n)
+                    store(n + 1)

@@ -60,6 +60,17 @@ def tile_routed_moe_kernel(tc, xT, w1, w3, w2, gate, offs, out):
             nc.sync.dma_start(raw[:], rows.rearrange("(p j) c -> p j c", j=PACK))
             return raw
 
+        def load_w2(e, pieces):
+            raw = raw_pool.tile([P, PACK, WIDTH], F32, name="raw")
+            parts = raw[:].rearrange("p j c -> p (j c)").rearrange("p (u j c) -> p u j c", u=2, j=PACK)
+            rows = w2[e].rearrange("(p j) (u c) -> p u j c", j=PACK, u=2)
+            if pieces == 1:
+                nc.sync.dma_start(raw[:], w2[e].rearrange("(p j) c -> p j c", j=PACK))
+                return [raw[:, :, u * 2 * P : (u + 1) * 2 * P] for u in range(2)]
+            for u in range(2):
+                nc.sync.dma_start(parts[:, u], rows[:, u])
+            return [parts[:, u] for u in range(2)]
+
         def load_gate(e, pieces):
             raw = raw_pool.tile([P, PACK, WIDTH], F32, name="raw")
             tile = raw[:].rearrange("p j c -> p (j c)")[:, 0 : BLOCKS * C].rearrange("p (n c) -> p n c", n=BLOCKS)
@@ -82,10 +93,10 @@ def tile_routed_moe_kernel(tc, xT, w1, w3, w2, gate, offs, out):
                 src[:].rearrange("p j (c i) -> p c j i", i=PAIR)[:, c0 // PAIR : c1 // PAIR],
             )
 
-        def interleave_permuted(copy, dst, src, b):
+        def interleave_permuted(copy, dst, src, b, m0=0, m1=P):
             copy(
-                dst[:].rearrange("p (b i m j) -> p b m j i", b=2, i=PAIR, j=PACK)[:, b],
-                src[:].rearrange("p j (m b i) -> p b m j i", b=2, i=PAIR)[:, b],
+                dst[:].rearrange("p (b i m j) -> p b m j i", b=2, i=PAIR, j=PACK)[:, b, m0:m1],
+                src[:].rearrange("p j (m b i) -> p b m j i", b=2, i=PAIR)[:, b, m0:m1],
             )
 
         def quantize(words, scales, src, c0, c1):
@@ -123,8 +134,13 @@ def tile_routed_moe_kernel(tc, xT, w1, w3, w2, gate, offs, out):
                 raw = load(weights[s * K_PASS : (s + 1) * K_PASS, :])
                 dst = rounded_tile()
                 words, scales = code_tiles()
-                for b, copy in enumerate(rounders(kind, e, s)):
-                    interleave_permuted(copy, dst, raw, b)
+                if (kind, s) == ("w3", LAST):
+                    interleave_permuted(vector, dst, raw, 0)
+                    interleave_permuted(vector, dst, raw, 1, 0, P // 2)
+                    interleave_permuted(scalar, dst, raw, 1, P // 2, P)
+                else:
+                    for b, copy in enumerate(rounders(kind, e, s)):
+                        interleave_permuted(copy, dst, raw, b)
                 for b in range(2):
                     quantize(words, scales, dst, 2 * b * P, 2 * (b + 1) * P)
                     for t in (2 * b, 2 * b + 1):
@@ -149,7 +165,7 @@ def tile_routed_moe_kernel(tc, xT, w1, w3, w2, gate, offs, out):
             for b in range(2):
                 nc.scalar.activation(gelus[:, b, :].rearrange("p (c t i) -> p c t i", t=2, i=PAIR), in_pairs(a[b]), GELU)
             sums = first_layer("w3", e, w3[e])
-            w2_raw = load(w2[e])
+            w2_raw = load_w2(e, 2 if e == E - 1 else 1)
             gates = load_gate(e, 2 if e == E - 1 else 1)
 
             halves = keep.tile([P, 2, 2 * C], BF16, name=f"halves{e}", align_bytes=64)
@@ -160,16 +176,17 @@ def tile_routed_moe_kernel(tc, xT, w1, w3, w2, gate, offs, out):
                     gelus[:, b, :].rearrange("p (c t i) -> p c t i", t=2, i=PAIR),
                     MULT,
                 )
+            w2_rounded = rounded_tile()
+            w2_words, w2_scales = code_tiles()
+            for u in range(2):
+                interleave(scalar, w2_rounded[:, u * 2 * P * PACK :], w2_raw[u], 0, 2 * P)
+            quantize(w2_words, w2_scales, w2_rounded, 0, P)
             h = keep.tile([P, PACK * C], BF16, name=f"h{e}", align_bytes=64)
             nc.vector.tensor_copy(
                 h[:].bitcast(U32).rearrange("p (c b) -> p c b", b=2),
                 halves[:].bitcast(U32).rearrange("p b c -> p c b"),
             )
-            w2_rounded = rounded_tile()
-            w2_words, w2_scales = code_tiles()
-            for n in range(BLOCKS):
-                interleave(vector if (e, n) == (E - 1, BLOCKS - 1) else scalar, w2_rounded, w2_raw, n * P, (n + 1) * P)
-            quantize(w2_words, w2_scales, w2_rounded, 0, 2 * P)
+            quantize(w2_words, w2_scales, w2_rounded, P, 2 * P)
             h_words = keep.tile([P, C], U32, name=f"h_words{e}", align_bytes=64)
             h_scales = keep.tile([P, C], U8, name=f"h_scales{e}", align_bytes=64)
             quantize(h_words, h_scales, h, 0, C)
@@ -190,7 +207,10 @@ def tile_routed_moe_kernel(tc, xT, w1, w3, w2, gate, offs, out):
                     start=True,
                     stop=True,
                 )
-                results.append(keep.tile([P, C], F32, name=f"result{e}_{n}"))
+                if (e, n) == (E - 1, 1):
+                    results.append(w2_raw[1][:, 0])
+                else:
+                    results.append(keep.tile([P, C], F32, name=f"result{e}_{n}"))
 
             def times_gate(n):
                 nc.vector.tensor_tensor(results[n][:], ys[n][:, 0:C], gates[:, n], MULT)
@@ -207,9 +227,14 @@ def tile_routed_moe_kernel(tc, xT, w1, w3, w2, gate, offs, out):
                     scatter_on_scalar(n)
             else:
                 for n in range(0, BLOCKS, 2):
-                    nc.scalar.copy(results[n][:], ys[n][:, 0:C])
-                    times_gate(n + 1)
-                    nc.vector.tensor_tensor(windows[n][:].indirect(entries), results[n][:], gates[:, n], MULT)
-                    scatter_on_scalar(n + 1)
+                    times_gate(n)
+                    if n == 0:
+                        nc.scalar.copy(results[1][:], ys[1][:, 0:C])
+                        scatter_on_scalar(0)
+                        nc.vector.tensor_tensor(windows[1][:].indirect(entries), results[1][:], gates[:, 1], MULT)
+                    else:
+                        times_gate(3)
+                        scatter_on_scalar(2)
+                        nc.vector.tensor_copy(windows[3][:].indirect(entries), results[3][:])
                     store(n)
                     store(n + 1)

@@ -27,7 +27,6 @@ SLOTS = E * C
 LIST_ROWS = 16
 PAIR = 2
 WINDOW = T + T // 2
-TOKENS_ON_VECTOR = T // 4
 
 
 def tile_routed_moe_kernel(tc, xT, w1, w3, w2, gate, offs, out):
@@ -36,12 +35,10 @@ def tile_routed_moe_kernel(tc, xT, w1, w3, w2, gate, offs, out):
 
     def rounders(kind, e, s):
         if (kind, e, s) == ("w1", 0, 0):
-            return scalar, scalar
-        if (kind, e) == ("w1", 1) and s < LAST:
-            return vector, vector
-        if (kind, s) == ("w3", 0):
-            return vector, vector
-        return vector, scalar
+            return [(scalar, slice(0, 2))]
+        if ((kind, e) == ("w1", 1) and s < LAST) or (kind, s) == ("w3", 0):
+            return [(vector, slice(0, 2))]
+        return [(vector, slice(0, 1)), (scalar, slice(1, 2))]
 
     with ExitStack() as ctx:
         keep = ctx.enter_context(tc.tile_pool(name="keep", bufs=1))
@@ -95,8 +92,8 @@ def tile_routed_moe_kernel(tc, xT, w1, w3, w2, gate, offs, out):
 
         def interleave_permuted(copy, dst, src, b, m0=0, m1=P):
             copy(
-                dst[:].rearrange("p (b i m j) -> p b m j i", b=2, i=PAIR, j=PACK)[:, b, m0:m1],
-                src[:].rearrange("p j (m b i) -> p b m j i", b=2, i=PAIR)[:, b, m0:m1],
+                dst[:].rearrange("p (b i m j) -> p b m j i", b=2, i=PAIR, j=PACK)[:, b, m0:m1] if isinstance(b, int) else dst[:].rearrange("p (b i m j) -> p b m j i", b=2, i=PAIR, j=PACK)[:, b],
+                src[:].rearrange("p j (m b i) -> p b m j i", b=2, i=PAIR)[:, b, m0:m1] if isinstance(b, int) else src[:].rearrange("p j (m b i) -> p b m j i", b=2, i=PAIR)[:, b],
             )
 
         def quantize(words, scales, src, c0, c1):
@@ -117,8 +114,7 @@ def tile_routed_moe_kernel(tc, xT, w1, w3, w2, gate, offs, out):
             if s == 0:
                 nc.sync.dma_start(offsets[:], offs)
             dst = rounded_tile()
-            interleave(vector, dst, raw, 0, TOKENS_ON_VECTOR)
-            interleave(scalar, dst, raw, TOKENS_ON_VECTOR, T)
+            interleave(scalar, dst, raw, 0, T)
             if s > 0:
                 gather_words(s - 1, x_words[s - 1])
             x_words.append(keep.tile([P, WINDOW], U32, name=f"x_words{s}", align_bytes=64))
@@ -134,15 +130,20 @@ def tile_routed_moe_kernel(tc, xT, w1, w3, w2, gate, offs, out):
                 raw = load(weights[s * K_PASS : (s + 1) * K_PASS, :])
                 dst = rounded_tile()
                 words, scales = code_tiles()
-                if (kind, s) == ("w3", LAST):
+                last = (kind, e, s) == ("w3", E - 1, LAST)
+                if last:
                     interleave_permuted(vector, dst, raw, 0)
                     interleave_permuted(vector, dst, raw, 1, 0, P // 2)
                     interleave_permuted(scalar, dst, raw, 1, P // 2, P)
                 else:
-                    for b, copy in enumerate(rounders(kind, e, s)):
+                    for copy, b in rounders(kind, e, s):
                         interleave_permuted(copy, dst, raw, b)
+                whole = len(rounders(kind, e, s)) == 1
+                if whole:
+                    quantize(words, scales, dst, 0, WIDTH)
                 for b in range(2):
-                    quantize(words, scales, dst, 2 * b * P, 2 * (b + 1) * P)
+                    if not whole:
+                        quantize(words, scales, dst, 2 * b * P, 2 * (b + 1) * P)
                     for t in (2 * b, 2 * b + 1):
                         cols = slice(t * P, (t + 1) * P)
                         nc.tensor.matmul_mx(
@@ -180,26 +181,32 @@ def tile_routed_moe_kernel(tc, xT, w1, w3, w2, gate, offs, out):
             w2_words, w2_scales = code_tiles()
             for u in range(2):
                 interleave(scalar, w2_rounded[:, u * 2 * P * PACK :], w2_raw[u], 0, 2 * P)
-            quantize(w2_words, w2_scales, w2_rounded, 0, P)
+            if e == E - 1:
+                quantize(w2_words, w2_scales, w2_rounded, 0, P)
             h = keep.tile([P, PACK * C], BF16, name=f"h{e}", align_bytes=64)
             nc.vector.tensor_copy(
                 h[:].bitcast(U32).rearrange("p (c b) -> p c b", b=2),
                 halves[:].bitcast(U32).rearrange("p b c -> p c b"),
             )
-            quantize(w2_words, w2_scales, w2_rounded, P, 2 * P)
+            if e == E - 1:
+                quantize(w2_words, w2_scales, w2_rounded, P, 2 * P)
             h_words = keep.tile([P, C], U32, name=f"h_words{e}", align_bytes=64)
             h_scales = keep.tile([P, C], U8, name=f"h_scales{e}", align_bytes=64)
             quantize(h_words, h_scales, h, 0, C)
-            quantize(w2_words, w2_scales, w2_rounded, 2 * P, WIDTH)
+            quantize(w2_words, w2_scales, w2_rounded, 2 * P if e == E - 1 else 0, WIDTH)
 
             tags = [f"w1_{e}_bank0", f"w1_{e}_bank1", f"w3_{e}_bank0", f"w3_{e}_bank1"]
             entries = offsets[:, e * C // LIST_ROWS : (e + 1) * C // LIST_ROWS]
             ys, results = [], []
             for n in range(BLOCKS):
                 cols = slice(n * P, (n + 1) * P)
-                ys.append(bank(tags[n]))
+                if e == E - 1:
+                    ys.append(bank(tags[n])[:, 0:C])
+                elif n % 2 == 0:
+                    both = bank(tags[n])
+                    ys.extend([both[:, 0:C], both[:, C:], both])
                 nc.tensor.matmul_mx(
-                    ys[n][:, 0:C],
+                    ys[n] if e == E - 1 else ys[n // 2 * 3 + n % 2],
                     lhsT=w2_words[:, cols].bitcast(FP8X4),
                     lhsT_scale=w2_scales[:, cols],
                     rhs=h_words[:].bitcast(FP8X4),
@@ -209,11 +216,11 @@ def tile_routed_moe_kernel(tc, xT, w1, w3, w2, gate, offs, out):
                 )
                 if (e, n) == (E - 1, 1):
                     results.append(w2_raw[1][:, 0])
-                else:
+                elif e == E - 1:
                     results.append(keep.tile([P, C], F32, name=f"result{e}_{n}"))
 
             def times_gate(n):
-                nc.vector.tensor_tensor(results[n][:], ys[n][:, 0:C], gates[:, n], MULT)
+                nc.vector.tensor_tensor(results[n][:], ys[n], gates[:, n], MULT)
 
             def scatter_on_scalar(n):
                 nc.scalar.activation(windows[n][:].indirect(entries), results[n][:], COPY)
@@ -222,14 +229,19 @@ def tile_routed_moe_kernel(tc, xT, w1, w3, w2, gate, offs, out):
                 nc.sync.dma_start(out[n * P : (n + 1) * P, :], windows[n][:])
 
             if e < E - 1:
-                for n in range(BLOCKS):
-                    times_gate(n)
+                for n in range(0, BLOCKS, 2):
+                    pair = keep.tile([P, 2 * C], F32, name=f"results{n}")
+                    nc.vector.tensor_tensor(
+                        pair[:], ys[n // 2 * 3 + 2][:], gates[:, n : n + 2].rearrange("p n c -> p (n c)"), MULT
+                    )
+                    results.extend([pair[:, 0:C], pair[:, C:]])
                     scatter_on_scalar(n)
+                    scatter_on_scalar(n + 1)
             else:
                 for n in range(0, BLOCKS, 2):
                     times_gate(n)
                     if n == 0:
-                        nc.scalar.copy(results[1][:], ys[1][:, 0:C])
+                        nc.scalar.copy(results[1][:], ys[1])
                         scatter_on_scalar(0)
                         nc.vector.tensor_tensor(windows[1][:].indirect(entries), results[1][:], gates[:, 1], MULT)
                     else:

@@ -102,6 +102,11 @@ def tile_routed_moe_kernel(tc, xT, w1, w3, w2, gate, offs, out):
         def bank(tag):
             return psum.tile([P, BANK], F32, name=tag, tag=tag)
 
+        def warm_up(src, times):
+            unread = bank("w3_0_bank1")
+            for i in range(times):
+                nc.tensor.matmul(unread[:], src[:, 0:P], src[:, 0:BANK], start=(i == 0), stop=(i == times - 1))
+
         slot_words = []
 
         def gather_words(s, words):
@@ -138,6 +143,8 @@ def tile_routed_moe_kernel(tc, xT, w1, w3, w2, gate, offs, out):
                 else:
                     for copy, b in rounders(kind, e, s):
                         interleave_permuted(copy, dst, raw, b)
+                if (kind, e) == ("w3", E - 1) and s >= LAST - 1:
+                    warm_up(dst, 2 if last else 1)
                 whole = len(rounders(kind, e, s)) == 1
                 if whole:
                     quantize(words, scales, dst, 0, WIDTH)
@@ -177,6 +184,8 @@ def tile_routed_moe_kernel(tc, xT, w1, w3, w2, gate, offs, out):
                     gelus[:, b, :].rearrange("p (c t i) -> p c t i", t=2, i=PAIR),
                     MULT,
                 )
+            if e == E - 1:
+                warm_up(halves[:, 1, :], 2)
             w2_rounded = rounded_tile()
             w2_words, w2_scales = code_tiles()
             for u in range(2):

@@ -27,6 +27,7 @@ SLOTS = E * C
 LIST_ROWS = 16
 PAIR = 2
 WINDOW = T + T // 2
+PAGE = 4096
 
 
 def tile_routed_moe_kernel(tc, xT, w1, w3, w2, gate, offs, out):
@@ -42,6 +43,7 @@ def tile_routed_moe_kernel(tc, xT, w1, w3, w2, gate, offs, out):
 
     with ExitStack() as ctx:
         keep = ctx.enter_context(tc.tile_pool(name="keep", bufs=1))
+        placed = ctx.enter_context(tc.tile_pool(name="placed", bufs=1))
         raw_pool = ctx.enter_context(tc.tile_pool(name="raw", bufs=12))
         rounded_pool = ctx.enter_context(tc.tile_pool(name="rounded", bufs=5))
         code_pool = ctx.enter_context(tc.tile_pool(name="codes", bufs=2 * PASSES))
@@ -50,15 +52,15 @@ def tile_routed_moe_kernel(tc, xT, w1, w3, w2, gate, offs, out):
         offsets = keep.tile([P, SLOTS // LIST_ROWS], U16, name="offsets")
         x_scales = keep.tile([P, WINDOW], U8, name="x_scales", align_bytes=64)
         nc.gpsimd.memset(x_scales[:, 0:T], 0)
-        windows = [keep.tile([P, T], F32, name=f"window{n}") for n in range(BLOCKS)]
+        windows = [placed.tile([P, T], F32, name=f"window{n}", offset=E * PAGE + n * PAGE // 2) for n in range(BLOCKS)]
 
         def load(rows):
-            raw = raw_pool.tile([P, PACK, WIDTH], F32, name="raw")
+            raw = raw_pool.tile([P, PACK, WIDTH], F32, name="raw", align_bytes=PAGE)
             nc.sync.dma_start(raw[:], rows.rearrange("(p j) c -> p j c", j=PACK))
             return raw
 
         def load_w2(e, pieces):
-            raw = raw_pool.tile([P, PACK, WIDTH], F32, name="raw")
+            raw = raw_pool.tile([P, PACK, WIDTH], F32, name="raw", align_bytes=PAGE)
             parts = raw[:].rearrange("p j c -> p (j c)").rearrange("p (u j c) -> p u j c", u=2, j=PACK)
             rows = w2[e].rearrange("(p j) (u c) -> p u j c", j=PACK, u=2)
             if pieces == 1:
@@ -69,7 +71,7 @@ def tile_routed_moe_kernel(tc, xT, w1, w3, w2, gate, offs, out):
             return [parts[:, u] for u in range(2)]
 
         def load_gate(e, pieces):
-            raw = raw_pool.tile([P, PACK, WIDTH], F32, name="raw")
+            raw = raw_pool.tile([P, PACK, WIDTH], F32, name="raw", align_bytes=PAGE)
             tile = raw[:].rearrange("p j c -> p (j c)")[:, 0 : BLOCKS * C].rearrange("p (n c) -> p n c", n=BLOCKS)
             rows = gate[:, e * C : (e + 1) * C].rearrange("(n p) c -> p n c", p=P)
             for n0 in range(0, BLOCKS, BLOCKS // pieces):
@@ -206,16 +208,19 @@ def tile_routed_moe_kernel(tc, xT, w1, w3, w2, gate, offs, out):
 
             tags = [f"w1_{e}_bank0", f"w1_{e}_bank1", f"w3_{e}_bank0", f"w3_{e}_bank1"]
             entries = offsets[:, e * C // LIST_ROWS : (e + 1) * C // LIST_ROWS]
-            ys, results = [], []
-            for n in range(BLOCKS):
+            sources = placed.tile([P, BLOCKS, C], F32, name=f"sources{e}", offset=e * PAGE, align_bytes=PAGE)
+            place = {1: 0, 3: 1, 0: 2, 2: 3}
+            results = [sources[:, place[n]] for n in range(BLOCKS)]
+            if e == E - 1:
+                ys = [bank(tags[n])[:, 0:C] for n in range(BLOCKS)]
+                results[1] = w2_raw[1][:, 0]
+            else:
+                both = [bank(tags[0]), bank(tags[2])]
+                ys = [both[n % 2][:, n // 2 * C : (n // 2 + 1) * C] for n in range(BLOCKS)]
+            for n in (range(BLOCKS) if e == E - 1 else (0, 2, 1, 3)):
                 cols = slice(n * P, (n + 1) * P)
-                if e == E - 1:
-                    ys.append(bank(tags[n])[:, 0:C])
-                elif n % 2 == 0:
-                    both = bank(tags[n])
-                    ys.extend([both[:, 0:C], both[:, C:], both])
                 nc.tensor.matmul_mx(
-                    ys[n] if e == E - 1 else ys[n // 2 * 3 + n % 2],
+                    ys[n],
                     lhsT=w2_words[:, cols].bitcast(FP8X4),
                     lhsT_scale=w2_scales[:, cols],
                     rhs=h_words[:].bitcast(FP8X4),
@@ -223,10 +228,6 @@ def tile_routed_moe_kernel(tc, xT, w1, w3, w2, gate, offs, out):
                     start=True,
                     stop=True,
                 )
-                if (e, n) == (E - 1, 1):
-                    results.append(w2_raw[1][:, 0])
-                elif e == E - 1:
-                    results.append(keep.tile([P, C], F32, name=f"result{e}_{n}"))
 
             def times_gate(n):
                 nc.vector.tensor_tensor(results[n][:], ys[n], gates[:, n], MULT)
@@ -238,14 +239,15 @@ def tile_routed_moe_kernel(tc, xT, w1, w3, w2, gate, offs, out):
                 nc.sync.dma_start(out[n * P : (n + 1) * P, :], windows[n][:])
 
             if e < E - 1:
-                for n in range(0, BLOCKS, 2):
-                    pair = keep.tile([P, 2 * C], F32, name=f"results{n}")
+                for n in range(2):
                     nc.vector.tensor_tensor(
-                        pair[:], ys[n // 2 * 3 + 2][:], gates[:, n : n + 2].rearrange("p n c -> p (n c)"), MULT
+                        sources[:, place[n] : place[n] + 2],
+                        both[n][:].rearrange("p (n c) -> p n c", n=2),
+                        gates[:, n::2],
+                        MULT,
                     )
-                    results.extend([pair[:, 0:C], pair[:, C:]])
                     scatter_on_scalar(n)
-                    scatter_on_scalar(n + 1)
+                    scatter_on_scalar(n + 2)
             else:
                 for n in range(0, BLOCKS, 2):
                     times_gate(n)

@@ -130,23 +130,63 @@ def tile_routed_moe_kernel(tc, xT, w1, w3, w2, gate, offs, out):
         nc.vector.tensor_copy(slot_scales[:], x_scales[:].indirect(offsets[:]))
         gather_words(LAST, x_words[LAST])
 
+        def last_pass(sums, rows, slots):
+            raw = raw_pool.tile([P, PACK, WIDTH], F32, name="raw", align_bytes=PAGE)
+            dst = rounded_tile()
+            words, scales = code_tiles()
+            parts = raw[:].rearrange("p j c -> p (j c)").rearrange("p (u j c) -> p u j c", u=2, j=PACK)
+            for u in range(2):
+                nc.sync.dma_start(parts[:, u], rows.rearrange("(p j) (u c) -> p u j c", j=PACK, u=2)[:, u])
+
+            def part(copy, u, b, m0, m1):
+                copy(
+                    dst[:].rearrange("p (b i m j) -> p b m j i", b=2, i=PAIR, j=PACK)[:, b, m0:m1],
+                    parts[:, u].rearrange("p j (m b i) -> p b m j i", b=2, i=PAIR)[:, b, m0 - u * P // 2 : m1 - u * P // 2],
+                )
+
+            for u in range(2):
+                m0, m1 = u * P // 2, (u + 1) * P // 2
+                split = m0 + (0 if u == 0 else P // 8)
+                part(vector, u, 0, m0, m1)
+                if split > m0:
+                    part(vector, u, 1, m0, split)
+                part(scalar, u, 1, split, m1)
+                if u == 0:
+                    unread = bank("w3_0_bank1")
+                    early = dst[:].rearrange("p (t x) -> p t x", t=BLOCKS)[:, 0:2, 0:C]
+                    for i in range(2):
+                        nc.tensor.matmul(
+                            unread[:].rearrange("p (t x) -> p t x", t=2), dst[:, 0:P], early, start=(i == 0), stop=(i == 1)
+                        )
+                for t in range(BLOCKS):
+                    quantize(words, scales, dst, t * P + m0, t * P + m1)
+                    if u == 1:
+                        cols = slice(t * P, (t + 1) * P)
+                        nc.tensor.matmul_mx(
+                            sums[t // 2][:, (t % 2) * C : (t % 2 + 1) * C],
+                            lhsT=words[:, cols].bitcast(FP8X4),
+                            lhsT_scale=scales[:, cols],
+                            rhs=slot_words[LAST][:, slots].bitcast(FP8X4),
+                            rhs_scale=slot_scales[4 * LAST : P, slots],
+                            start=False,
+                            stop=(t % 2 == 1),
+                        )
+
         def first_layer(kind, e, weights):
             sums = [bank(f"{kind}_{e}_bank{b}") for b in range(2)]
             slots = slice(e * C, (e + 1) * C)
             for s in range(PASSES):
-                raw = load(weights[s * K_PASS : (s + 1) * K_PASS, :])
+                rows = weights[s * K_PASS : (s + 1) * K_PASS, :]
+                if (kind, e, s) == ("w3", E - 1, LAST):
+                    last_pass(sums, rows, slots)
+                    continue
+                raw = load(rows)
                 dst = rounded_tile()
                 words, scales = code_tiles()
-                last = (kind, e, s) == ("w3", E - 1, LAST)
-                if last:
-                    interleave_permuted(vector, dst, raw, 0)
-                    interleave_permuted(vector, dst, raw, 1, 0, P // 2)
-                    interleave_permuted(scalar, dst, raw, 1, P // 2, P)
-                else:
-                    for copy, b in rounders(kind, e, s):
-                        interleave_permuted(copy, dst, raw, b)
-                if (kind, e) == ("w3", E - 1) and s >= LAST - 1:
-                    warm_up(dst, 2 if last else 1)
+                for copy, b in rounders(kind, e, s):
+                    interleave_permuted(copy, dst, raw, b)
+                if (kind, e, s) == ("w3", E - 1, LAST - 1):
+                    warm_up(dst, 1)
                 whole = len(rounders(kind, e, s)) == 1
                 if whole:
                     quantize(words, scales, dst, 0, WIDTH)
@@ -190,8 +230,9 @@ def tile_routed_moe_kernel(tc, xT, w1, w3, w2, gate, offs, out):
                 warm_up(halves[:, 1, :], 2)
             w2_rounded = rounded_tile()
             w2_words, w2_scales = code_tiles()
-            for u in range(2):
-                interleave(scalar, w2_rounded[:, u * 2 * P * PACK :], w2_raw[u], 0, 2 * P)
+            right = placed.tile([P, PACK * 2 * P], BF16, name=f"right{e}", tag="right", offset=4 * PAGE + PAGE // 4, align_bytes=64)
+            interleave(scalar, w2_rounded[:, 0 : 2 * P * PACK], w2_raw[0], 0, 2 * P)
+            interleave(scalar, right, w2_raw[1], 0, 2 * P)
             if e == E - 1:
                 quantize(w2_words, w2_scales, w2_rounded, 0, P)
             h = keep.tile([P, PACK * C], BF16, name=f"h{e}", align_bytes=64)
@@ -204,7 +245,9 @@ def tile_routed_moe_kernel(tc, xT, w1, w3, w2, gate, offs, out):
             h_words = keep.tile([P, C], U32, name=f"h_words{e}", align_bytes=64)
             h_scales = keep.tile([P, C], U8, name=f"h_scales{e}", align_bytes=64)
             quantize(h_words, h_scales, h, 0, C)
-            quantize(w2_words, w2_scales, w2_rounded, 2 * P if e == E - 1 else 0, WIDTH)
+            if e < E - 1:
+                quantize(w2_words, w2_scales, w2_rounded, 0, 2 * P)
+            quantize(w2_words[:, 2 * P :], w2_scales[:, 2 * P :], right, 0, 2 * P)
 
             tags = [f"w1_{e}_bank0", f"w1_{e}_bank1", f"w3_{e}_bank0", f"w3_{e}_bank1"]
             entries = offsets[:, e * C // LIST_ROWS : (e + 1) * C // LIST_ROWS]
@@ -213,7 +256,7 @@ def tile_routed_moe_kernel(tc, xT, w1, w3, w2, gate, offs, out):
             results = [sources[:, place[n]] for n in range(BLOCKS)]
             if e == E - 1:
                 ys = [bank(tags[n])[:, 0:C] for n in range(BLOCKS)]
-                results[1] = w2_raw[1][:, 0]
+                results[0:2] = [right[:].bitcast(F32)[:, C:], right[:].bitcast(F32)[:, 0:C]]
             else:
                 both = [bank(tags[0]), bank(tags[2])]
                 ys = [both[n % 2][:, n // 2 * C : (n // 2 + 1) * C] for n in range(BLOCKS)]
@@ -249,15 +292,10 @@ def tile_routed_moe_kernel(tc, xT, w1, w3, w2, gate, offs, out):
                     scatter_on_scalar(n)
                     scatter_on_scalar(n + 2)
             else:
-                for n in range(0, BLOCKS, 2):
+                for n in range(BLOCKS):
                     times_gate(n)
-                    if n == 0:
-                        nc.scalar.copy(results[1][:], ys[1])
-                        scatter_on_scalar(0)
-                        nc.vector.tensor_tensor(windows[1][:].indirect(entries), results[1][:], gates[:, 1], MULT)
-                    else:
-                        times_gate(3)
-                        scatter_on_scalar(2)
-                        nc.vector.tensor_copy(windows[3][:].indirect(entries), results[3][:])
+                for n in range(0, BLOCKS, 2):
+                    scatter_on_scalar(n)
+                    nc.vector.tensor_copy(windows[n + 1][:].indirect(entries), results[n + 1][:])
                     store(n)
                     store(n + 1)

@@ -59,16 +59,14 @@ def tile_routed_moe_kernel(tc, xT, w1, w3, w2, gate, offs, out):
             nc.sync.dma_start(raw[:], rows.rearrange("(p j) c -> p j c", j=PACK))
             return raw
 
-        def load_w2(e, pieces):
-            raw = raw_pool.tile([P, PACK, WIDTH], F32, name="raw", align_bytes=PAGE)
-            parts = raw[:].rearrange("p j c -> p (j c)").rearrange("p (u j c) -> p u j c", u=2, j=PACK)
-            rows = w2[e].rearrange("(p j) (u c) -> p u j c", j=PACK, u=2)
-            if pieces == 1:
-                nc.sync.dma_start(raw[:], w2[e].rearrange("(p j) c -> p j c", j=PACK))
-                return [raw[:, :, u * 2 * P : (u + 1) * 2 * P] for u in range(2)]
-            for u in range(2):
-                nc.sync.dma_start(parts[:, u], rows[:, u])
-            return [parts[:, u] for u in range(2)]
+        def load_w2(e, cuts):
+            raw = raw_pool.tile([P, PACK * WIDTH], F32, name="raw", align_bytes=PAGE)
+            rows = w2[e].rearrange("(p j) c -> p j c", j=PACK)
+            pieces = []
+            for c0, c1 in zip(cuts, cuts[1:]):
+                pieces.append(raw[:, PACK * c0 : PACK * c1].rearrange("p (j c) -> p j c", j=PACK))
+                nc.sync.dma_start(pieces[-1], rows[:, :, c0:c1])
+            return pieces
 
         def load_gate(e, pieces):
             raw = raw_pool.tile([P, PACK, WIDTH], F32, name="raw", align_bytes=PAGE)
@@ -215,8 +213,9 @@ def tile_routed_moe_kernel(tc, xT, w1, w3, w2, gate, offs, out):
             for b in range(2):
                 nc.scalar.activation(gelus[:, b, :].rearrange("p (c t i) -> p c t i", t=2, i=PAIR), in_pairs(a[b]), GELU)
             sums = first_layer("w3", e, w3[e])
-            w2_raw = load_w2(e, 2 if e == E - 1 else 1)
-            gates = load_gate(e, 2 if e == E - 1 else 1)
+            cuts = (0, P, P + 3 * P // 2, WIDTH) if e == E - 1 else (0, WIDTH)
+            w2_raw = load_w2(e, cuts)
+            gates = load_gate(e, 1)
 
             halves = keep.tile([P, 2, 2 * C], BF16, name=f"halves{e}", align_bytes=64)
             for b in range(2):
@@ -230,24 +229,26 @@ def tile_routed_moe_kernel(tc, xT, w1, w3, w2, gate, offs, out):
                 warm_up(halves[:, 1, :], 2)
             w2_rounded = rounded_tile()
             w2_words, w2_scales = code_tiles()
-            right = placed.tile([P, PACK * 2 * P], BF16, name=f"right{e}", tag="right", offset=4 * PAGE + PAGE // 4, align_bytes=64)
-            interleave(scalar, w2_rounded[:, 0 : 2 * P * PACK], w2_raw[0], 0, 2 * P)
-            interleave(scalar, right, w2_raw[1], 0, 2 * P)
+            for c0, c1, piece in zip(cuts, cuts[1:], w2_raw):
+                ends = sorted({c0, c1} | {c for c in range(0, WIDTH, P if e == E - 1 else 2 * P) if c0 < c < c1})
+                for a0, a1 in zip(ends, ends[1:]):
+                    interleave(scalar, w2_rounded[:, PACK * c0 : PACK * c1], piece, a0 - c0, a1 - c0)
             if e == E - 1:
                 quantize(w2_words, w2_scales, w2_rounded, 0, P)
+                quantize(w2_words, w2_scales, w2_rounded, P, 2 * P)
             h = keep.tile([P, PACK * C], BF16, name=f"h{e}", align_bytes=64)
             nc.vector.tensor_copy(
                 h[:].bitcast(U32).rearrange("p (c b) -> p c b", b=2),
                 halves[:].bitcast(U32).rearrange("p b c -> p c b"),
             )
             if e == E - 1:
-                quantize(w2_words, w2_scales, w2_rounded, P, 2 * P)
+                quantize(w2_words, w2_scales, w2_rounded, 2 * P, 3 * P)
             h_words = keep.tile([P, C], U32, name=f"h_words{e}", align_bytes=64)
             h_scales = keep.tile([P, C], U8, name=f"h_scales{e}", align_bytes=64)
             quantize(h_words, h_scales, h, 0, C)
             if e < E - 1:
                 quantize(w2_words, w2_scales, w2_rounded, 0, 2 * P)
-            quantize(w2_words[:, 2 * P :], w2_scales[:, 2 * P :], right, 0, 2 * P)
+            quantize(w2_words, w2_scales, w2_rounded, (3 if e == E - 1 else 2) * P, WIDTH)
 
             tags = [f"w1_{e}_bank0", f"w1_{e}_bank1", f"w3_{e}_bank0", f"w3_{e}_bank1"]
             entries = offsets[:, e * C // LIST_ROWS : (e + 1) * C // LIST_ROWS]
@@ -256,7 +257,6 @@ def tile_routed_moe_kernel(tc, xT, w1, w3, w2, gate, offs, out):
             results = [sources[:, place[n]] for n in range(BLOCKS)]
             if e == E - 1:
                 ys = [bank(tags[n])[:, 0:C] for n in range(BLOCKS)]
-                results[0:2] = [right[:].bitcast(F32)[:, C:], right[:].bitcast(F32)[:, 0:C]]
             else:
                 both = [bank(tags[0]), bank(tags[2])]
                 ys = [both[n % 2][:, n // 2 * C : (n // 2 + 1) * C] for n in range(BLOCKS)]

@@ -128,7 +128,7 @@ def tile_routed_moe_kernel(tc, xT, w1, w3, w2, gate, offs, out):
         nc.vector.tensor_copy(slot_scales[:], x_scales[:].indirect(offsets[:]))
         gather_words(LAST, x_words[LAST])
 
-        def last_pass(sums, rows, slots):
+        def last_pass(sums, rows, slots, rest_of_pass_before):
             raw = raw_pool.tile([P, PACK, WIDTH], F32, name="raw", align_bytes=PAGE)
             dst = rounded_tile()
             words, scales = code_tiles()
@@ -146,6 +146,8 @@ def tile_routed_moe_kernel(tc, xT, w1, w3, w2, gate, offs, out):
                 m0, m1 = u * P // 2, (u + 1) * P // 2
                 split = m0 + (0 if u == 0 else P // 8)
                 part(vector, u, 0, m0, m1)
+                if u == 0:
+                    rest_of_pass_before()
                 if split > m0:
                     part(vector, u, 1, m0, split)
                 part(scalar, u, 1, split, m1)
@@ -173,11 +175,9 @@ def tile_routed_moe_kernel(tc, xT, w1, w3, w2, gate, offs, out):
         def first_layer(kind, e, weights):
             sums = [bank(f"{kind}_{e}_bank{b}") for b in range(2)]
             slots = slice(e * C, (e + 1) * C)
-            for s in range(PASSES):
+            ending = (kind, e) == ("w3", E - 1)
+            for s in range(LAST if ending else PASSES):
                 rows = weights[s * K_PASS : (s + 1) * K_PASS, :]
-                if (kind, e, s) == ("w3", E - 1, LAST):
-                    last_pass(sums, rows, slots)
-                    continue
                 raw = load(rows)
                 dst = rounded_tile()
                 words, scales = code_tiles()
@@ -188,7 +188,8 @@ def tile_routed_moe_kernel(tc, xT, w1, w3, w2, gate, offs, out):
                 whole = len(rounders(kind, e, s)) == 1
                 if whole:
                     quantize(words, scales, dst, 0, WIDTH)
-                for b in range(2):
+
+                def finish(b):
                     if not whole:
                         quantize(words, scales, dst, 2 * b * P, 2 * (b + 1) * P)
                     for t in (2 * b, 2 * b + 1):
@@ -202,6 +203,12 @@ def tile_routed_moe_kernel(tc, xT, w1, w3, w2, gate, offs, out):
                             start=(s == 0 and t % 2 == 0),
                             stop=(s == LAST and t % 2 == 1),
                         )
+
+                finish(0)
+                if ending and s == LAST - 1:
+                    last_pass(sums, weights[LAST * K_PASS :, :], slots, lambda: finish(1))
+                else:
+                    finish(1)
             return sums
 
         def in_pairs(sums_of_bank):
@@ -213,9 +220,9 @@ def tile_routed_moe_kernel(tc, xT, w1, w3, w2, gate, offs, out):
             for b in range(2):
                 nc.scalar.activation(gelus[:, b, :].rearrange("p (c t i) -> p c t i", t=2, i=PAIR), in_pairs(a[b]), GELU)
             sums = first_layer("w3", e, w3[e])
-            cuts = (0, P, P + 3 * P // 2, WIDTH) if e == E - 1 else (0, WIDTH)
+            cuts = (0, 2 * P, WIDTH) if e == E - 1 else (0, WIDTH)
             w2_raw = load_w2(e, cuts)
-            gates = load_gate(e, 1)
+            gates = load_gate(e, 2 if e == E - 1 else 1)
 
             halves = keep.tile([P, 2, 2 * C], BF16, name=f"halves{e}", align_bytes=64)
             for b in range(2):
@@ -231,24 +238,24 @@ def tile_routed_moe_kernel(tc, xT, w1, w3, w2, gate, offs, out):
             w2_words, w2_scales = code_tiles()
             for c0, c1, piece in zip(cuts, cuts[1:], w2_raw):
                 ends = sorted({c0, c1} | {c for c in range(0, WIDTH, P if e == E - 1 else 2 * P) if c0 < c < c1})
+                if (e, c1) == (E - 1, WIDTH):
+                    ends = [c0, WIDTH - P // 2]
                 for a0, a1 in zip(ends, ends[1:]):
                     interleave(scalar, w2_rounded[:, PACK * c0 : PACK * c1], piece, a0 - c0, a1 - c0)
             if e == E - 1:
                 quantize(w2_words, w2_scales, w2_rounded, 0, P)
-                quantize(w2_words, w2_scales, w2_rounded, P, 2 * P)
             h = keep.tile([P, PACK * C], BF16, name=f"h{e}", align_bytes=64)
             nc.vector.tensor_copy(
                 h[:].bitcast(U32).rearrange("p (c b) -> p c b", b=2),
                 halves[:].bitcast(U32).rearrange("p b c -> p c b"),
             )
             if e == E - 1:
-                quantize(w2_words, w2_scales, w2_rounded, 2 * P, 3 * P)
+                interleave(vector, w2_rounded[:, PACK * 2 * P :], w2_raw[1], 2 * P - P // 2, 2 * P)
             h_words = keep.tile([P, C], U32, name=f"h_words{e}", align_bytes=64)
             h_scales = keep.tile([P, C], U8, name=f"h_scales{e}", align_bytes=64)
             quantize(h_words, h_scales, h, 0, C)
-            if e < E - 1:
-                quantize(w2_words, w2_scales, w2_rounded, 0, 2 * P)
-            quantize(w2_words, w2_scales, w2_rounded, (3 if e == E - 1 else 2) * P, WIDTH)
+            quantize(w2_words, w2_scales, w2_rounded, P if e == E - 1 else 0, 2 * P)
+            quantize(w2_words, w2_scales, w2_rounded, 2 * P, WIDTH)
 
             tags = [f"w1_{e}_bank0", f"w1_{e}_bank1", f"w3_{e}_bank0", f"w3_{e}_bank1"]
             entries = offsets[:, e * C // LIST_ROWS : (e + 1) * C // LIST_ROWS]

@@ -102,11 +102,6 @@ def tile_routed_moe_kernel(tc, xT, w1, w3, w2, gate, offs, out):
         def bank(tag):
             return psum.tile([P, BANK], F32, name=tag, tag=tag)
 
-        def warm_up(src, times):
-            unread = bank("w3_0_bank1")
-            for i in range(times):
-                nc.tensor.matmul(unread[:], src[:, 0:P], src[:, 0:BANK], start=(i == 0), stop=(i == times - 1))
-
         slot_words = []
 
         def gather_words(s, words):
@@ -151,13 +146,6 @@ def tile_routed_moe_kernel(tc, xT, w1, w3, w2, gate, offs, out):
                 if split > m0:
                     part(vector, u, 1, m0, split)
                 part(scalar, u, 1, split, m1)
-                if u == 0:
-                    unread = bank("w3_0_bank1")
-                    early = dst[:].rearrange("p (t x) -> p t x", t=BLOCKS)[:, 0:2, 0:C]
-                    for i in range(2):
-                        nc.tensor.matmul(
-                            unread[:].rearrange("p (t x) -> p t x", t=2), dst[:, 0:P], early, start=(i == 0), stop=(i == 1)
-                        )
                 for t in range(BLOCKS):
                     quantize(words, scales, dst, t * P + m0, t * P + m1)
                     if u == 1:
@@ -183,8 +171,6 @@ def tile_routed_moe_kernel(tc, xT, w1, w3, w2, gate, offs, out):
                 words, scales = code_tiles()
                 for copy, b in rounders(kind, e, s):
                     interleave_permuted(copy, dst, raw, b)
-                if (kind, e, s) == ("w3", E - 1, LAST - 1):
-                    warm_up(dst, 1)
                 whole = len(rounders(kind, e, s)) == 1
                 if whole:
                     quantize(words, scales, dst, 0, WIDTH)
@@ -232,8 +218,6 @@ def tile_routed_moe_kernel(tc, xT, w1, w3, w2, gate, offs, out):
                     gelus[:, b, :].rearrange("p (c t i) -> p c t i", t=2, i=PAIR),
                     MULT,
                 )
-            if e == E - 1:
-                warm_up(halves[:, 1, :], 2)
             w2_rounded = rounded_tile()
             w2_words, w2_scales = code_tiles()
             for c0, c1, piece in zip(cuts, cuts[1:], w2_raw):

@@ -244,7 +244,7 @@ def tile_routed_moe_kernel(tc, xT, w1, w3, w2, gate, offs, out):
             tags = [f"w1_{e}_bank0", f"w1_{e}_bank1", f"w3_{e}_bank0", f"w3_{e}_bank1"]
             entries = offsets[:, e * C // LIST_ROWS : (e + 1) * C // LIST_ROWS]
             sources = placed.tile([P, BLOCKS, C], F32, name=f"sources{e}", offset=e * PAGE, align_bytes=PAGE)
-            place = {1: 0, 3: 1, 0: 2, 2: 3}
+            place = {1: 0, 3: 1, 0: 2, 2: 3} if e < E - 1 else {1: 0, 0: 1, 3: 2, 2: 3}
             results = [sources[:, place[n]] for n in range(BLOCKS)]
             if e == E - 1:
                 ys = [bank(tags[n])[:, 0:C] for n in range(BLOCKS)]

from contextlib import ExitStack

import concourse.mybir as mybir

K, T, E, C, H, N = 2048, 512, 2, 256, 512, 512
FLOPS = 2 * E * C * (2 * K * H + H * N)

F32 = mybir.dt.float32
BF16 = mybir.dt.bfloat16
U32 = mybir.dt.uint32
U16 = mybir.dt.uint16
U8 = mybir.dt.uint8
FP8X4 = mybir.dt.float8_e4m3fn_x4
MULT = mybir.AluOpType.mult
GELU = mybir.ActivationFunctionType.Gelu_apprx_tanh
COPY = mybir.ActivationFunctionType.Copy

P = 128
PACK = 4
K_PASS = P * PACK
PASSES = K // K_PASS
LAST = PASSES - 1
WIDTH = 512
BLOCKS = WIDTH // P
BANK = 512
SLOTS = E * C
LIST_ROWS = 16
PAIR = 2
WINDOW = T + T // 2
PAGE = 4096


def tile_routed_moe_kernel(tc, xT, w1, w3, w2, gate, offs, out):
    nc = tc.nc
    vector, scalar = nc.vector.tensor_copy, nc.scalar.copy

    def rounders(kind, e, s):
        if (kind, e, s) == ("w1", 0, 0):
            return [(scalar, slice(0, 2))]
        if ((kind, e) == ("w1", 1) and s < LAST) or (kind, s) == ("w3", 0):
            return [(vector, slice(0, 2))]
        return [(vector, slice(0, 1)), (scalar, slice(1, 2))]

    with ExitStack() as ctx:
        keep = ctx.enter_context(tc.tile_pool(name="keep", bufs=1))
        placed = ctx.enter_context(tc.tile_pool(name="placed", bufs=1))
        raw_pool = ctx.enter_context(tc.tile_pool(name="raw", bufs=12))
        rounded_pool = ctx.enter_context(tc.tile_pool(name="rounded", bufs=5))
        code_pool = ctx.enter_context(tc.tile_pool(name="codes", bufs=2 * PASSES))
        psum = ctx.enter_context(tc.psum_pool(name="psum", bufs=1))

        offsets = keep.tile([P, SLOTS // LIST_ROWS], U16, name="offsets")
        x_scales = keep.tile([P, WINDOW], U8, name="x_scales", align_bytes=64)
        nc.gpsimd.memset(x_scales[:, 0:T], 0)
        windows = [placed.tile([P, T], F32, name=f"window{n}", offset=E * PAGE + n * PAGE // 2) for n in range(BLOCKS)]

        def load(rows):
            raw = raw_pool.tile([P, PACK, WIDTH], F32, name="raw", align_bytes=PAGE)
            nc.sync.dma_start(raw[:], rows.rearrange("(p j) c -> p j c", j=PACK))
            return raw

        def load_w2(e, cuts):
            raw = raw_pool.tile([P, PACK * WIDTH], F32, name="raw", align_bytes=PAGE)
            rows = w2[e].rearrange("(p j) c -> p j c", j=PACK)
            pieces = []
            for c0, c1 in zip(cuts, cuts[1:]):
                pieces.append(raw[:, PACK * c0 : PACK * c1].rearrange("p (j c) -> p j c", j=PACK))
                nc.sync.dma_start(pieces[-1], rows[:, :, c0:c1])
            return pieces

        def load_gate(e, pieces):
            raw = raw_pool.tile([P, PACK, WIDTH], F32, name="raw", align_bytes=PAGE)
            tile = raw[:].rearrange("p j c -> p (j c)")[:, 0 : BLOCKS * C].rearrange("p (n c) -> p n c", n=BLOCKS)
            rows = gate[:, e * C : (e + 1) * C].rearrange("(n p) c -> p n c", p=P)
            for n0 in range(0, BLOCKS, BLOCKS // pieces):
                nc.sync.dma_start(tile[:, n0 : n0 + BLOCKS // pieces], rows[:, n0 : n0 + BLOCKS // pieces])
            return tile

        def rounded_tile():
            return rounded_pool.tile([P, PACK * WIDTH], BF16, name="rounded", align_bytes=64)

        def code_tiles():
            words = code_pool.tile([P, WIDTH], U32, name="words", align_bytes=64)
            scales = code_pool.tile([P, WIDTH], U8, name="scales", align_bytes=64)
            return words, scales

        def interleave(copy, dst, src, c0, c1):
            copy(
                dst[:].rearrange("p (c i j) -> p c j i", i=PAIR, j=PACK)[:, c0 // PAIR : c1 // PAIR],
                src[:].rearrange("p j (c i) -> p c j i", i=PAIR)[:, c0 // PAIR : c1 // PAIR],
            )

        def interleave_permuted(copy, dst, src, b, m0=0, m1=P):
            copy(
                dst[:].rearrange("p (b i m j) -> p b m j i", b=2, i=PAIR, j=PACK)[:, b, m0:m1] if isinstance(b, int) else dst[:].rearrange("p (b i m j) -> p b m j i", b=2, i=PAIR, j=PACK)[:, b],
                src[:].rearrange("p j (m b i) -> p b m j i", b=2, i=PAIR)[:, b, m0:m1] if isinstance(b, int) else src[:].rearrange("p j (m b i) -> p b m j i", b=2, i=PAIR)[:, b],
            )

        def quantize(words, scales, src, c0, c1):
            nc.vector.quantize_mx(words[:, c0:c1].bitcast(FP8X4), scales[:, c0:c1], src[:, PACK * c0 : PACK * c1])

        def bank(tag):
            return psum.tile([P, BANK], F32, name=tag, tag=tag)

        slot_words = []

        def gather_words(s, words):
            slot_words.append(keep.tile([P, SLOTS], U32, name=f"slot_words{s}", align_bytes=64))
            nc.vector.tensor_copy(slot_words[s][:], words[:].indirect(offsets[:]))

        x_words = []
        for s in range(PASSES):
            raw = load(xT[s * K_PASS : (s + 1) * K_PASS, :])
            if s == 0:
                nc.sync.dma_start(offsets[:], offs)
            dst = rounded_tile()
            interleave(scalar, dst, raw, 0, T)
            if s > 0:
                gather_words(s - 1, x_words[s - 1])
            x_words.append(keep.tile([P, WINDOW], U32, name=f"x_words{s}", align_bytes=64))
            quantize(x_words[s], x_scales[4 * s : P], dst, 0, T)
        slot_scales = keep.tile([P, SLOTS], U8, name="slot_scales", align_bytes=64)
        nc.vector.tensor_copy(slot_scales[:], x_scales[:].indirect(offsets[:]))
        gather_words(LAST, x_words[LAST])

        def last_pass(sums, rows, slots, rest_of_pass_before):
            raw = raw_pool.tile([P, PACK, WIDTH], F32, name="raw", align_bytes=PAGE)
            dst = rounded_tile()
            words, scales = code_tiles()
            parts = raw[:].rearrange("p j c -> p (j c)").rearrange("p (u j c) -> p u j c", u=2, j=PACK)
            for u in range(2):
                nc.sync.dma_start(parts[:, u], rows.rearrange("(p j) (u c) -> p u j c", j=PACK, u=2)[:, u])

            def part(copy, u, b, m0, m1):
                copy(
                    dst[:].rearrange("p (b i m j) -> p b m j i", b=2, i=PAIR, j=PACK)[:, b, m0:m1],
                    parts[:, u].rearrange("p j (m b i) -> p b m j i", b=2, i=PAIR)[:, b, m0 - u * P // 2 : m1 - u * P // 2],
                )

            for u in range(2):
                m0, m1 = u * P // 2, (u + 1) * P // 2
                split = m0 + (0 if u == 0 else P // 8)
                part(vector, u, 0, m0, m1)
                if u == 0:
                    rest_of_pass_before()
                if split > m0:
                    part(vector, u, 1, m0, split)
                part(scalar, u, 1, split, m1)
                for t in range(BLOCKS):
                    quantize(words, scales, dst, t * P + m0, t * P + m1)
                    if u == 1:
                        cols = slice(t * P, (t + 1) * P)
                        nc.tensor.matmul_mx(
                            sums[t // 2][:, (t % 2) * C : (t % 2 + 1) * C],
                            lhsT=words[:, cols].bitcast(FP8X4),
                            lhsT_scale=scales[:, cols],
                            rhs=slot_words[LAST][:, slots].bitcast(FP8X4),
                            rhs_scale=slot_scales[4 * LAST : P, slots],
                            start=False,
                            stop=(t % 2 == 1),
                        )

        def first_layer(kind, e, weights):
            sums = [bank(f"{kind}_{e}_bank{b}") for b in range(2)]
            slots = slice(e * C, (e + 1) * C)
            ending = (kind, e) == ("w3", E - 1)
            for s in range(LAST if ending else PASSES):
                rows = weights[s * K_PASS : (s + 1) * K_PASS, :]
                raw = load(rows)
                dst = rounded_tile()
                words, scales = code_tiles()
                for copy, b in rounders(kind, e, s):
                    interleave_permuted(copy, dst, raw, b)
                whole = len(rounders(kind, e, s)) == 1
                if whole:
                    quantize(words, scales, dst, 0, WIDTH)

                def finish(b):
                    if not whole:
                        quantize(words, scales, dst, 2 * b * P, 2 * (b + 1) * P)
                    for t in (2 * b, 2 * b + 1):
                        cols = slice(t * P, (t + 1) * P)
                        nc.tensor.matmul_mx(
                            sums[b][:, (t % 2) * C : (t % 2 + 1) * C],
                            lhsT=words[:, cols].bitcast(FP8X4),
                            lhsT_scale=scales[:, cols],
                            rhs=slot_words[s][:, slots].bitcast(FP8X4),
                            rhs_scale=slot_scales[4 * s : P, slots],
                            start=(s == 0 and t % 2 == 0),
                            stop=(s == LAST and t % 2 == 1),
                        )

                finish(0)
                if ending and s == LAST - 1:
                    last_pass(sums, weights[LAST * K_PASS :, :], slots, lambda: finish(1))
                else:
                    finish(1)
            return sums

        def in_pairs(sums_of_bank):
            return sums_of_bank[:].rearrange("p (t c i) -> p c t i", t=2, i=PAIR)

        for e in range(E):
            a = first_layer("w1", e, w1[e])
            gelus = keep.tile([P, 2, BANK], F32, name=f"gelus{e}")
            for b in range(2):
                nc.scalar.activation(gelus[:, b, :].rearrange("p (c t i) -> p c t i", t=2, i=PAIR), in_pairs(a[b]), GELU)
            sums = first_layer("w3", e, w3[e])
            cuts = (0, 2 * P, WIDTH) if e == E - 1 else (0, WIDTH)
            w2_raw = load_w2(e, cuts)
            gates = load_gate(e, 2 if e == E - 1 else 1)

            halves = keep.tile([P, 2, 2 * C], BF16, name=f"halves{e}", align_bytes=64)
            for b in range(2):
                nc.vector.tensor_tensor(
                    halves[:, b, :].rearrange("p (c i t) -> p c t i", t=2, i=PAIR),
                    in_pairs(sums[b]),
                    gelus[:, b, :].rearrange("p (c t i) -> p c t i", t=2, i=PAIR),
                    MULT,
                )
            w2_rounded = rounded_tile()
            w2_words, w2_scales = code_tiles()
            for c0, c1, piece in zip(cuts, cuts[1:], w2_raw):
                ends = sorted({c0, c1} | {c for c in range(0, WIDTH, P if e == E - 1 else 2 * P) if c0 < c < c1})
                if (e, c1) == (E - 1, WIDTH):
                    ends = [c0, WIDTH - P // 2]
                for a0, a1 in zip(ends, ends[1:]):
                    interleave(scalar, w2_rounded[:, PACK * c0 : PACK * c1], piece, a0 - c0, a1 - c0)
            if e == E - 1:
                quantize(w2_words, w2_scales, w2_rounded, 0, P)
            h = keep.tile([P, PACK * C], BF16, name=f"h{e}", align_bytes=64)
            nc.vector.tensor_copy(
                h[:].bitcast(U32).rearrange("p (c b) -> p c b", b=2),
                halves[:].bitcast(U32).rearrange("p b c -> p c b"),
            )
            if e == E - 1:
                interleave(vector, w2_rounded[:, PACK * 2 * P :], w2_raw[1], 2 * P - P // 2, 2 * P)
            h_words = keep.tile([P, C], U32, name=f"h_words{e}", align_bytes=64)
            h_scales = keep.tile([P, C], U8, name=f"h_scales{e}", align_bytes=64)
            quantize(h_words, h_scales, h, 0, C)
            quantize(w2_words, w2_scales, w2_rounded, P if e == E - 1 else 0, 2 * P)
            quantize(w2_words, w2_scales, w2_rounded, 2 * P, WIDTH)

            tags = [f"w1_{e}_bank0", f"w1_{e}_bank1", f"w3_{e}_bank0", f"w3_{e}_bank1"]
            entries = offsets[:, e * C // LIST_ROWS : (e + 1) * C // LIST_ROWS]
            sources = placed.tile([P, BLOCKS, C], F32, name=f"sources{e}", offset=e * PAGE, align_bytes=PAGE)
            place = {1: 0, 3: 1, 0: 2, 2: 3} if e < E - 1 else {1: 0, 0: 1, 3: 2, 2: 3}
            results = [sources[:, place[n]] for n in range(BLOCKS)]
            if e == E - 1:
                ys = [bank(tags[n])[:, 0:C] for n in range(BLOCKS)]
            else:
                both = [bank(tags[0]), bank(tags[2])]
                ys = [both[n % 2][:, n // 2 * C : (n // 2 + 1) * C] for n in range(BLOCKS)]
            for n in (range(BLOCKS) if e == E - 1 else (0, 2, 1, 3)):
                cols = slice(n * P, (n + 1) * P)
                nc.tensor.matmul_mx(
                    ys[n],
                    lhsT=w2_words[:, cols].bitcast(FP8X4),
                    lhsT_scale=w2_scales[:, cols],
                    rhs=h_words[:].bitcast(FP8X4),
                    rhs_scale=h_scales[:],
                    start=True,
                    stop=True,
                )

            def times_gate(n):
                nc.vector.tensor_tensor(results[n][:], ys[n], gates[:, n], MULT)

            def scatter_on_scalar(n):
                nc.scalar.activation(windows[n][:].indirect(entries), results[n][:], COPY)

            def store(n):
                nc.sync.dma_start(out[n * P : (n + 1) * P, :], windows[n][:])

            if e < E - 1:
                for n in range(2):
                    nc.vector.tensor_tensor(
                        sources[:, place[n] : place[n] + 2],
                        both[n][:].rearrange("p (n c) -> p n c", n=2),
                        gates[:, n::2],
                        MULT,
                    )
                    scatter_on_scalar(n)
                    scatter_on_scalar(n + 2)
            else:
                for n in range(BLOCKS):
                    times_gate(n)
                for n in range(0, BLOCKS, 2):
                    scatter_on_scalar(n)
                    nc.vector.tensor_copy(windows[n + 1][:].indirect(entries), results[n + 1][:])
                    store(n)
                    store(n + 1)
